import numpy as np
import ml_dtypes


def mxq(x, axis, fmt="e4m3"):
    dtype, down = {"e4m3": (ml_dtypes.float8_e4m3fn, 7), "e5m2": (ml_dtypes.float8_e5m2, 14)}[fmt]
    v = np.moveaxis(np.asarray(x, np.float32).astype(ml_dtypes.bfloat16).astype(np.float64), axis, -1)
    blocks = v.reshape(v.shape[:-1] + (-1, 32))
    amax = np.abs(blocks).max(-1, keepdims=True)
    byte = np.maximum(np.where(amax > 0, np.frexp(amax)[1] - 1 + 127, 0) - down, 1)
    scale = np.exp2(byte - 127.0)
    codes = (blocks / scale).astype(np.float32).astype(dtype).astype(np.float64)
    return np.moveaxis((codes * scale).reshape(v.shape), -1, axis)


WIDE = False


def mx_kscale(k):
    if not WIDE:
        return np.ones(k)
    levels = np.array([10, -10, 5, -5, 0])
    if k % 512:
        return np.exp2(np.random.permutation(np.resize(levels, k // 32))).repeat(32)
    a = np.empty((k // 512, 16))
    for p in range(k // 512):
        a[p, :8] = np.random.permutation(np.resize(levels, 8))
        for g in range(8):
            far = levels[np.abs(levels - a[p, g]) >= 10]
            a[p, g + 8] = far[np.random.randint(len(far))]
    return np.exp2(a.ravel()).repeat(32)


def f64(x):
    return np.asarray(x).astype(np.float64)


def striped(idx):
    return np.tile(idx.reshape(-1, 16).T, (8, 1)).astype(np.uint16)


def unstriped(offs):
    return offs[:16].T.reshape(-1).astype(np.int64)


def pack_weight(w):
    k, n = w.shape
    w = f64(np.asarray(w, np.float32).astype(ml_dtypes.bfloat16)).reshape(k // 32, 32, n)
    amax = np.abs(w).max(1)
    byte = np.clip(np.where(amax > 0, np.frexp(amax)[1] - 1 + 127 - 7, 1), 1, 254)
    scaled = (w * np.exp2(127.0 - byte)[:, None, :]).reshape(k, n).astype(np.float32)
    words = np.ascontiguousarray(scaled.reshape(k // 512, 128, 4, n).transpose(0, 1, 3, 2)).astype(ml_dtypes.float8_e4m3fn).view(np.uint8)
    return words, np.ascontiguousarray(byte.astype(np.uint8).reshape(k // 512, 16, n))


def unpack_weight(words, scales):
    g, p, n, _ = words.shape
    vals = np.ascontiguousarray(words).view(ml_dtypes.float8_e4m3fn).astype(np.float64) * np.repeat(np.exp2(scales.astype(np.float64) - 127.0), 8, axis=1)[..., None]
    return vals.transpose(0, 1, 3, 2).reshape(g * 512, n)


E2M1 = np.array([0.0, 0.5, 1.0, 1.5, 2.0, 3.0, 4.0, 6.0, -0.0, -0.5, -1.0, -1.5, -2.0, -3.0, -4.0, -6.0])


def pack_fp4(w):
    k, n = w.shape
    w = f64(np.asarray(w, np.float32).astype(ml_dtypes.bfloat16)).reshape(k // 32, 32, n)
    amax = np.abs(w).max(1)
    mant, ex = np.frexp(amax / 6.0)
    byte = np.clip(np.where(amax > 0, np.where(mant > 0.5, ex, ex - 1) + 127, 1), 1, 254)
    scaled = (w * np.exp2(127.0 - byte)[:, None, :]).reshape(k, n).astype(np.float32)
    c = np.ascontiguousarray(scaled.reshape(k // 512, 128, 4, n).transpose(0, 1, 3, 2)).astype(ml_dtypes.float4_e2m1fn).view(np.uint8) & 0xF
    words = (c[..., 0::2] | (c[..., 1::2] << 4)).reshape(k // 512, 128, 2 * n)
    return np.ascontiguousarray(words), np.ascontiguousarray(byte.astype(np.uint8).reshape(k // 512, 16, n))


def unpack_fp4(words, scales):
    g, _, n = scales.shape
    words = np.ascontiguousarray(words).reshape(g, 128, n, 2)
    nib = np.empty((g, 128, n, 4), np.uint8)
    nib[..., 0::2] = words & 0xF
    nib[..., 1::2] = words >> 4
    vals = E2M1[nib] * np.repeat(np.exp2(scales.astype(np.float64) - 127.0), 8, axis=1)[..., None]
    return vals.transpose(0, 1, 3, 2).reshape(g * 512, n)


K, T, S, V, H, N = 512, 2048, 1536, 512, 512, 256


def setup_inputs():
    n = np.random.standard_normal
    s = mx_kscale(K)[:, None]
    u = mx_kscale(H)
    packed_xT = pack_weight(n((K, T)) * s)
    packed_w4 = pack_fp4(n((H, N)) / np.sqrt(H) / u[:, None])
    return {
        "x_words": packed_xT[0],
        "x_scales": packed_xT[1],
        "w1": (n((K, H)) / np.sqrt(K) / s * u).astype(np.float32),
        "w2": (n((K, H)) / np.sqrt(K) / s).astype(np.float32),
        "w3": (n((K, H)) / np.sqrt(K) / s).astype(np.float32),
        "w4_words": packed_w4[0],
        "w4_scales": packed_w4[1],
        "offs": striped(np.random.permutation(T)[:S]),
    }


def reference(x_words, x_scales, w1, w2, w3, w4_words, w4_scales, offs):
    xq = unpack_weight(x_words, x_scales)[:, unstriped(offs)]
    z = (((mxq(f64(w1), 0, "e4m3").T @ xq[:, :V])) * ((mxq(f64(w2), 0, "e4m3").T @ xq[:, V:2 * V]))) * ((mxq(f64(w3), 0, "e4m3").T @ xq[:, 2 * V:3 * V]))
    return unpack_fp4(w4_words, w4_scales).T @ mxq(z, 0, "e4m3")

@@ -1,0 +1,192 @@
+from contextlib import ExitStack
+
+import concourse.mybir as mybir
+
+K, T, S, V, H, N = 512, 2048, 1536, 512, 512, 256
+FLOPS = 2 * K * H * S + 2 * H * N * V
+
+F32 = mybir.dt.float32
+BF16 = mybir.dt.bfloat16
+I32 = mybir.dt.int32
+U32 = mybir.dt.uint32
+U16 = mybir.dt.uint16
+U8 = mybir.dt.uint8
+FP8X4 = mybir.dt.float8_e4m3fn_x4
+FP4X4 = mybir.dt.float4_e2m1fn_x4
+MULT = mybir.AluOpType.mult
+ADD = mybir.AluOpType.add
+
+P = 128
+PACK = 4
+PIECES = 3
+CHUNK = 128
+CHUNKS = V // CHUNK
+HALVES = N // P
+
+
+def tile_picked_trilin_none_p_kernel(
+    tc, x_words, x_scales, w1, w2, w3, w4_words, w4_scales, offs, out
+):
+    nc = tc.nc
+    weights = (w1, w2, w3)
+
+    with ExitStack() as ctx:
+        keep = ctx.enter_context(tc.tile_pool(name="keep", bufs=1))
+        ring = ctx.enter_context(tc.tile_pool(name="ring", bufs=2))
+        acc_pool = ctx.enter_context(tc.psum_pool(name="acc", bufs=6))
+        res_pool = ctx.enter_context(tc.psum_pool(name="res", bufs=2))
+
+        offsets = keep.tile([P, S // 16], U16, name="offsets")
+        table_words = keep.tile([P, T], U32, name="table_words", align_bytes=64)
+        table_scales = keep.tile([P, T], U8, name="table_scales", align_bytes=64)
+        last_words = keep.tile([P, 2 * N], U8, name="last_words", align_bytes=64)
+        last_scales = keep.tile([P, N], U8, name="last_scales", align_bytes=64)
+        rounded = [keep.tile([P, PACK, P, PACK], BF16, name=f"rounded{d}", align_bytes=64) for d in range(PIECES)]
+        w_codes = [keep.tile([P, H], U32, name=f"w_codes{d}", align_bytes=64) for d in range(PIECES)]
+        w_scales = [keep.tile([P, H], U8, name=f"w_scales{d}", align_bytes=64) for d in range(PIECES)]
+        x_codes = [keep.tile([P, V], U32, name=f"x_codes{d}", align_bytes=64) for d in range(PIECES)]
+        x_bytes = [keep.tile([P, V], U8, name=f"x_bytes{d}", align_bytes=64) for d in range(PIECES)]
+        raw = {}
+
+        def load_scale_rows(queue, plane, rows):
+            for q in range(4):
+                queue.dma_start(
+                    out=plane[32 * q : 32 * q + 32, :].bitcast(I32),
+                    in_=rows[0, 4 * q : 4 * q + 4, :].bitcast(I32).partition_broadcast(8),
+                )
+
+        def load_weight(d, m0, m1):
+            t = keep.tile([P, PACK, PACK * (m1 - m0)], F32, name=f"raw{d}_{m0}", align_bytes=64)
+            nc.sync.dma_start(
+                out=t[:], in_=weights[d].rearrange("(p j) c -> p j c", j=PACK)[:, :, PACK * m0 : PACK * m1]
+            )
+            for m in range(m0, m1):
+                raw[d, m] = (t, m0)
+
+        def views(d, m0, m1):
+            t, base = raw[d, m0]
+            src = t[:, :, PACK * (m0 - base) : PACK * (m1 - base)].rearrange("p j (m t) -> p m j t", t=PACK)
+            dst = rounded[d][:, :, m0:m1, :].rearrange("p t m j -> p m j t")
+            return dst, src
+
+        def round_scalar(d, m0, m1):
+            dst, src = views(d, m0, m1)
+            nc.scalar.copy(out=dst, in_=src)
+
+        def round_vector(d, m0, m1):
+            dst, src = views(d, m0, m1)
+            nc.vector.tensor_copy(out=dst, in_=src)
+
+        def round_gpsimd(d, m0, m1):
+            dst, src = views(d, m0, m1)
+            nc.gpsimd.tensor_scalar(out=dst, in0=src, scalar1=1.0, scalar2=0.0, op0=MULT, op1=ADD)
+
+        def quantize_weight(d):
+            nc.vector.quantize_mx(
+                out=w_codes[d][:].bitcast(FP8X4),
+                scales=w_scales[d][:],
+                in_=rounded[d][:].rearrange("p t m j -> p (t m j)"),
+            )
+
+        def piece(d):
+            return offsets[:, d * (V // 16) : (d + 1) * (V // 16)]
+
+        def gather_scales(d):
+            nc.vector.tensor_copy(out=x_bytes[d][:], in_=table_scales[:].indirect(piece(d)))
+
+        def gather_words(d):
+            nc.vector.tensor_copy(out=x_codes[d][:], in_=table_words[:].indirect(piece(d)))
+
+        def product(d, c):
+            bank = acc_pool.tile([P, PACK, CHUNK], F32, name="bank")
+            cols = slice(c * CHUNK, (c + 1) * CHUNK)
+            for t in range(PACK):
+                chans = slice(t * P, (t + 1) * P)
+                nc.tensor.matmul_mx(
+                    out=bank[:, t, :],
+                    lhsT=w_codes[d][:, chans].bitcast(FP8X4),
+                    lhsT_scale=w_scales[d][:, chans],
+                    rhs=x_codes[d][:, cols].bitcast(FP8X4),
+                    rhs_scale=x_bytes[d][:, cols],
+                    start=True,
+                    stop=True,
+                )
+            return bank[:].rearrange("p t v -> p v t")
+
+        first = [keep.tile([P, CHUNK, PACK], F32, name=f"first{c}", align_bytes=64) for c in range(CHUNKS)]
+        pair = [keep.tile([P, CHUNK, PACK], F32, name=f"pair{c}", align_bytes=64) for c in range(CHUNKS)]
+        z = {}
+        z_codes = [keep.tile([P, CHUNK], U32, name=f"z_codes{c}", align_bytes=64) for c in range(CHUNKS)]
+        z_scales = [keep.tile([P, CHUNK], U8, name=f"z_scales{c}", align_bytes=64) for c in range(CHUNKS)]
+        staged = [keep.tile([P, HALVES, CHUNK], F32, name=f"staged{c}", align_bytes=64) for c in range(CHUNKS)]
+        out_view = out.rearrange("(h m) v -> m h v", h=HALVES)
+
+        def first_factor(c):
+            nc.scalar.copy(out=first[c][:], in_=product(0, c))
+
+        def second_factor(c):
+            nc.vector.tensor_tensor(out=pair[c][:], in0=product(1, c), in1=first[c][:], op=MULT)
+
+        def third_factor(c):
+            z[c] = ring.tile([P, CHUNK, PACK], BF16, name="z", align_bytes=64)
+            nc.vector.tensor_tensor(out=z[c][:], in0=product(2, c), in1=pair[c][:], op=MULT)
+
+        def finish(c):
+            nc.vector.quantize_mx(
+                out=z_codes[c][:].bitcast(FP8X4),
+                scales=z_scales[c][:],
+                in_=z[c][:].rearrange("p v t -> p (v t)"),
+            )
+            res = res_pool.tile([P, HALVES, CHUNK], F32, name="res")
+            for h in range(HALVES):
+                nc.tensor.matmul_mx(
+                    out=res[:, h, :],
+                    lhsT=last_words[:, 2 * P * h : 2 * P * (h + 1)].bitcast(FP4X4),
+                    lhsT_scale=last_scales[:, P * h : P * (h + 1)],
+                    rhs=z_codes[c][:].bitcast(FP8X4),
+                    rhs_scale=z_scales[c][:],
+                    start=True,
+                    stop=True,
+                )
+            nc.scalar.copy(out=staged[c][:], in_=res[:])
+            nc.sync.dma_start(out=out_view[:, :, c * CHUNK : (c + 1) * CHUNK], in_=staged[c][:])
+
+        def load_table_words():
+            nc.sync.dma_start(
+                out=table_words[:].bitcast(I32), in_=x_words[0].rearrange("p c r -> p (c r)").bitcast(I32)
+            )
+
+        def load_last():
+            nc.sync.dma_start(out=last_words[:].bitcast(I32), in_=w4_words[0].bitcast(I32))
+            load_scale_rows(nc.sync, last_scales, w4_scales)
+
+        nc.sync.dma_start(offsets[:], offs)
+        load_scale_rows(nc.sync, table_scales, x_scales)
+        load_table_words()
+        load_weight(0, 0, P)
+        load_weight(1, 0, P)
+        load_weight(2, 0, P)
+        load_last()
+
+        for d in range(PIECES):
+            gather_scales(d)
+        for d in range(PIECES):
+            gather_words(d)
+        round_scalar(0, 0, P)
+        quantize_weight(0)
+        round_scalar(1, 0, 64)
+        round_vector(1, 64, P)
+        quantize_weight(1)
+        for c in range(CHUNKS):
+            first_factor(c)
+        round_scalar(2, 0, 56)
+        round_vector(2, 56, P)
+        for c in range(CHUNKS - 1):
+            second_factor(c)
+        quantize_weight(2)
+        second_factor(CHUNKS - 1)
+        third_factor(0)
+        for c in range(1, CHUNKS):
+            third_factor(c)
+            finish(c - 1)
+        finish(CHUNKS - 1)

@@ -33,7 +33,7 @@ def tile_picked_trilin_none_p_kernel(
     with ExitStack() as ctx:
         keep = ctx.enter_context(tc.tile_pool(name="keep", bufs=1))
         ring = ctx.enter_context(tc.tile_pool(name="ring", bufs=2))
-        acc_pool = ctx.enter_context(tc.psum_pool(name="acc", bufs=6))
+        acc_pool = ctx.enter_context(tc.psum_pool(name="acc", bufs=4))
         res_pool = ctx.enter_context(tc.psum_pool(name="res", bufs=2))
 
         offsets = keep.tile([P, S // 16], U16, name="offsets")
@@ -41,11 +41,14 @@ def tile_picked_trilin_none_p_kernel(
         table_scales = keep.tile([P, T], U8, name="table_scales", align_bytes=64)
         last_words = keep.tile([P, 2 * N], U8, name="last_words", align_bytes=64)
         last_scales = keep.tile([P, N], U8, name="last_scales", align_bytes=64)
-        rounded = [keep.tile([P, PACK, P, PACK], BF16, name=f"rounded{d}", align_bytes=64) for d in range(PIECES)]
+        rounded = [keep.tile([P, PACK, P, PACK], BF16, name=f"rounded{d}", tag=f"rounded{d}", align_bytes=64) for d in range(1)]
         w_codes = [keep.tile([P, H], U32, name=f"w_codes{d}", align_bytes=64) for d in range(PIECES)]
         w_scales = [keep.tile([P, H], U8, name=f"w_scales{d}", align_bytes=64) for d in range(PIECES)]
-        x_codes = [keep.tile([P, V], U32, name=f"x_codes{d}", align_bytes=64) for d in range(PIECES)]
-        x_bytes = [keep.tile([P, V], U8, name=f"x_bytes{d}", align_bytes=64) for d in range(PIECES)]
+        early_codes = keep.tile([P, S], U32, name="early_codes", align_bytes=64)
+        x_bytes_all = keep.tile([P, S], U8, name="x_bytes_all", align_bytes=64)
+        x_bytes = [x_bytes_all[:, d * V : (d + 1) * V] for d in range(PIECES)]
+        x_codes = [early_codes[:, d * V : (d + 1) * V] for d in range(PIECES)]
+        row_pairs = {}
         raw = {}
 
         def load_scale_rows(queue, plane, rows):
@@ -88,17 +91,69 @@ def tile_picked_trilin_none_p_kernel(
                 in_=rounded[d][:].rearrange("p t m j -> p (t m j)"),
             )
 
+        halves = {}
+
+        def round_half(d, u, engine, tag=None):
+            t = keep.tile([P, 2, P, PACK], BF16, name=f"half{d}_{u}", tag=tag or f"half{d}_{u}", align_bytes=64)
+            halves[d, u] = t
+            src = raw[d, 0][0][:].rearrange("p j (m t) -> p m j t", t=PACK)[:, :, :, 2 * u : 2 * u + 2]
+            dst = t[:].rearrange("p t m j -> p m j t")
+            if engine == "scalar":
+                nc.scalar.copy(out=dst, in_=src)
+            elif engine == "vector":
+                nc.vector.tensor_copy(out=dst, in_=src)
+            else:
+                nc.gpsimd.tensor_scalar(
+                    out=dst.rearrange("p m j t -> p m t j"),
+                    in0=src.rearrange("p m j t -> p m t j"),
+                    scalar1=1.0,
+                    scalar2=0.0,
+                    op0=MULT,
+                    op1=ADD,
+                )
+
+        def quantize_half(d, u):
+            cols = slice(2 * P * u, 2 * P * (u + 1))
+            nc.vector.quantize_mx(
+                out=w_codes[d][:, cols].bitcast(FP8X4),
+                scales=w_scales[d][:, cols],
+                in_=halves[d, u][:].rearrange("p t m j -> p (t m j)"),
+            )
+
+        def clock(ap, name):
+            t = keep.tile([P, 1], ap.dtype, name=name)
+            nc.gpsimd.tensor_copy(out=t[:], in_=ap)
+
         def piece(d):
             return offsets[:, d * (V // 16) : (d + 1) * (V // 16)]
 
-        def gather_scales(d):
-            nc.vector.tensor_copy(out=x_bytes[d][:], in_=table_scales[:].indirect(piece(d)))
+        def gather_scales():
+            nc.vector.tensor_copy(out=x_bytes_all[:], in_=table_scales[:].indirect(offsets[:]))
 
-        def gather_words(d):
-            nc.vector.tensor_copy(out=x_codes[d][:], in_=table_words[:].indirect(piece(d)))
+        def gather_early():
+            nc.vector.tensor_copy(out=early_codes[:], in_=table_words[:].indirect(offsets[:]))
+
+        def gather_late():
+            late_codes = keep.tile([P, V], U32, name="late_codes", tag="rounded0", align_bytes=64)
+            x_codes[2] = late_codes[:]
+            nc.vector.tensor_copy(out=late_codes[:], in_=table_words[:].indirect(piece(2)))
+
+        def load_row_pair(d, u):
+            t = keep.tile([P, 2, H], F32, name=f"rows{d}_{u}", align_bytes=64)
+            nc.sync.dma_start(out=t[:], in_=weights[d].rearrange("(p j) c -> p j c", j=PACK)[:, 2 * u : 2 * u + 2, :])
+            row_pairs[d, u] = t
+
+        def round_row_pair(d, u):
+            nc.scalar.copy(
+                out=rounded[d][:, :, :, 2 * u : 2 * u + 2].rearrange("p t m j -> p m j t"),
+                in_=row_pairs[d, u][:].rearrange("p j (m t) -> p m j t", t=PACK),
+            )
 
         def product(d, c):
-            bank = acc_pool.tile([P, PACK, CHUNK], F32, name="bank")
+            if d == 0:
+                bank = acc_pool.tile([P, PACK, CHUNK], F32, name="first_bank", bufs=2)
+            else:
+                bank = acc_pool.tile([P, PACK, CHUNK], F32, name="bank", bufs=3)
             cols = slice(c * CHUNK, (c + 1) * CHUNK)
             for t in range(PACK):
                 chans = slice(t * P, (t + 1) * P)
@@ -114,7 +169,7 @@ def tile_picked_trilin_none_p_kernel(
             return bank[:].rearrange("p t v -> p v t")
 
         first = [keep.tile([P, CHUNK, PACK], F32, name=f"first{c}", align_bytes=64) for c in range(CHUNKS)]
-        pair = [keep.tile([P, CHUNK, PACK], F32, name=f"pair{c}", align_bytes=64) for c in range(CHUNKS)]
+        pair = {}
         z = {}
         z_codes = [keep.tile([P, CHUNK], U32, name=f"z_codes{c}", align_bytes=64) for c in range(CHUNKS)]
         z_scales = [keep.tile([P, CHUNK], U8, name=f"z_scales{c}", align_bytes=64) for c in range(CHUNKS)]
@@ -125,7 +180,14 @@ def tile_picked_trilin_none_p_kernel(
             nc.scalar.copy(out=first[c][:], in_=product(0, c))
 
         def second_factor(c):
+            pair[c] = keep.tile([P, CHUNK, PACK], F32, name=f"pair{c}", tag="half2_1" if c == 0 else f"pair{c}", align_bytes=64)
             nc.vector.tensor_tensor(out=pair[c][:], in0=product(1, c), in1=first[c][:], op=MULT)
+
+        def second_factor_gpsimd(c):
+            second = keep.tile([P, CHUNK, PACK], F32, name="second", align_bytes=64)
+            pair[c] = keep.tile([P, CHUNK, PACK], F32, name=f"pair{c}", align_bytes=64)
+            nc.scalar.copy(out=second[:], in_=product(1, c))
+            nc.gpsimd.tensor_tensor(out=pair[c][:], in0=second[:], in1=first[c][:], op=MULT)
 
         def third_factor(c):
             z[c] = ring.tile([P, CHUNK, PACK], BF16, name="z", align_bytes=64)
@@ -137,10 +199,11 @@ def tile_picked_trilin_none_p_kernel(
                 scales=z_scales[c][:],
                 in_=z[c][:].rearrange("p v t -> p (v t)"),
             )
-            res = res_pool.tile([P, HALVES, CHUNK], F32, name="res")
-            for h in range(HALVES):
+            cols = slice(c * CHUNK, (c + 1) * CHUNK)
+
+            def last_product(target, h):
                 nc.tensor.matmul_mx(
-                    out=res[:, h, :],
+                    out=target,
                     lhsT=last_words[:, 2 * P * h : 2 * P * (h + 1)].bitcast(FP4X4),
                     lhsT_scale=last_scales[:, P * h : P * (h + 1)],
                     rhs=z_codes[c][:].bitcast(FP8X4),
@@ -148,8 +211,21 @@ def tile_picked_trilin_none_p_kernel(
                     start=True,
                     stop=True,
                 )
-            nc.scalar.copy(out=staged[c][:], in_=res[:])
-            nc.sync.dma_start(out=out_view[:, :, c * CHUNK : (c + 1) * CHUNK], in_=staged[c][:])
+
+            res = res_pool.tile([P, HALVES, CHUNK], F32, name="res")
+            if c < CHUNKS - 1:
+                for h in range(HALVES):
+                    last_product(res[:, h, :], h)
+                nc.scalar.copy(out=staged[c][:], in_=res[:])
+                nc.sync.dma_start(out=out_view[:, :, cols], in_=staged[c][:])
+            else:
+                other = res_pool.tile([P, CHUNK], F32, name="other", bufs=1)
+                last_product(res[:, 0, :], 0)
+                last_product(other[:], 1)
+                nc.scalar.copy(out=staged[c][:, 0, :], in_=res[:, 0, :])
+                nc.vector.tensor_copy(out=staged[c][:, 1, :], in_=other[:])
+                nc.scalar.dma_start(out=out_view[:, 0, cols], in_=staged[c][:, 0, :])
+                nc.sync.dma_start(out=out_view[:, 1, cols], in_=staged[c][:, 1, :])
 
         def load_table_words():
             nc.sync.dma_start(
@@ -168,24 +244,27 @@ def tile_picked_trilin_none_p_kernel(
         load_weight(2, 0, P)
         load_last()
 
-        for d in range(PIECES):
-            gather_scales(d)
-        for d in range(PIECES):
-            gather_words(d)
+        gather_scales()
+        gather_early()
         round_scalar(0, 0, P)
         quantize_weight(0)
-        round_scalar(1, 0, 64)
-        round_vector(1, 64, P)
-        quantize_weight(1)
-        for c in range(CHUNKS):
-            first_factor(c)
-        round_scalar(2, 0, 56)
-        round_vector(2, 56, P)
-        for c in range(CHUNKS - 1):
-            second_factor(c)
-        quantize_weight(2)
-        second_factor(CHUNKS - 1)
+        round_half(1, 0, "scalar")
+        round_half(1, 1, "vector", tag="rounded0")
+        quantize_half(1, 0)
+        quantize_half(1, 1)
+        round_half(2, 1, "vector")
+        quantize_half(2, 1)
+        first_factor(0)
+        second_factor(0)
+        round_half(2, 0, "scalar")
+        quantize_half(2, 0)
+        first_factor(1)
+        second_factor(1)
+        first_factor(3)
+        second_factor_gpsimd(3)
         third_factor(0)
+        first_factor(2)
+        second_factor(2)
         for c in range(1, CHUNKS):
             third_factor(c)
             finish(c - 1)

@@ -22,6 +22,7 @@ PIECES = 3
 CHUNK = 128
 CHUNKS = V // CHUNK
 HALVES = N // P
+KIB = 1024
 
 
 def tile_picked_trilin_none_p_kernel(
@@ -32,162 +33,115 @@ def tile_picked_trilin_none_p_kernel(
 
     with ExitStack() as ctx:
         keep = ctx.enter_context(tc.tile_pool(name="keep", bufs=1))
+        shared = ctx.enter_context(tc.tile_pool(name="shared", bufs=1))
         ring = ctx.enter_context(tc.tile_pool(name="ring", bufs=2))
-        acc_pool = ctx.enter_context(tc.psum_pool(name="acc", bufs=4))
-        res_pool = ctx.enter_context(tc.psum_pool(name="res", bufs=2))
+        psum = ctx.enter_context(tc.psum_pool(name="psum", bufs=1))
 
         offsets = keep.tile([P, S // 16], U16, name="offsets")
         table_words = keep.tile([P, T], U32, name="table_words", align_bytes=64)
         table_scales = keep.tile([P, T], U8, name="table_scales", align_bytes=64)
         last_words = keep.tile([P, 2 * N], U8, name="last_words", align_bytes=64)
         last_scales = keep.tile([P, N], U8, name="last_scales", align_bytes=64)
-        rounded = [keep.tile([P, PACK, P, PACK], BF16, name=f"rounded{d}", tag=f"rounded{d}", align_bytes=64) for d in range(1)]
         w_codes = [keep.tile([P, H], U32, name=f"w_codes{d}", align_bytes=64) for d in range(PIECES)]
         w_scales = [keep.tile([P, H], U8, name=f"w_scales{d}", align_bytes=64) for d in range(PIECES)]
-        early_codes = keep.tile([P, S], U32, name="early_codes", align_bytes=64)
-        x_bytes_all = keep.tile([P, S], U8, name="x_bytes_all", align_bytes=64)
-        x_bytes = [x_bytes_all[:, d * V : (d + 1) * V] for d in range(PIECES)]
-        x_codes = [early_codes[:, d * V : (d + 1) * V] for d in range(PIECES)]
-        row_pairs = {}
-        raw = {}
+        x_bytes = keep.tile([P, S], U8, name="x_bytes", align_bytes=64)
 
-        def load_scale_rows(queue, plane, rows):
+        RAW_AT = [0, 8 * KIB, 16 * KIB]
+        AT = 24 * KIB
+        raw = {}
+        rounded = {}
+        x_codes = {}
+        first = {}
+        pair = {}
+        z = {}
+
+        def load_scale_rows(plane, rows):
             for q in range(4):
-                queue.dma_start(
+                nc.sync.dma_start(
                     out=plane[32 * q : 32 * q + 32, :].bitcast(I32),
                     in_=rows[0, 4 * q : 4 * q + 4, :].bitcast(I32).partition_broadcast(8),
                 )
 
-        def load_weight(d, m0, m1):
-            t = keep.tile([P, PACK, PACK * (m1 - m0)], F32, name=f"raw{d}_{m0}", align_bytes=64)
-            nc.sync.dma_start(
-                out=t[:], in_=weights[d].rearrange("(p j) c -> p j c", j=PACK)[:, :, PACK * m0 : PACK * m1]
-            )
-            for m in range(m0, m1):
-                raw[d, m] = (t, m0)
+        def load_weight(d):
+            raw[d] = shared.tile([P, PACK, H], F32, name=f"raw{d}", align_bytes=64, offset=RAW_AT[d])
+            nc.sync.dma_start(out=raw[d][:], in_=weights[d].rearrange("(p j) c -> p j c", j=PACK))
 
-        def views(d, m0, m1):
-            t, base = raw[d, m0]
-            src = t[:, :, PACK * (m0 - base) : PACK * (m1 - base)].rearrange("p j (m t) -> p m j t", t=PACK)
-            dst = rounded[d][:, :, m0:m1, :].rearrange("p t m j -> p m j t")
+        def place_rounded(d, at):
+            rounded[d] = shared.tile([P, PACK * H], BF16, name=f"rounded{d}", align_bytes=64, offset=at)
+
+        def round_views(d, u):
+            src = raw[d][:].rearrange("p j (m t) -> p m j t", t=PACK)[:, :, :, 2 * u : 2 * u + 2]
+            dst = rounded[d][:, 2 * H * u : 2 * H * (u + 1)].rearrange("p (t m j) -> p m j t", t=2, j=PACK)
             return dst, src
 
-        def round_scalar(d, m0, m1):
-            dst, src = views(d, m0, m1)
+        def round_scalar(d, u):
+            dst, src = round_views(d, u)
             nc.scalar.copy(out=dst, in_=src)
 
-        def round_vector(d, m0, m1):
-            dst, src = views(d, m0, m1)
+        def round_vector(d, u):
+            dst, src = round_views(d, u)
             nc.vector.tensor_copy(out=dst, in_=src)
 
-        def round_gpsimd(d, m0, m1):
-            dst, src = views(d, m0, m1)
-            nc.gpsimd.tensor_scalar(out=dst, in0=src, scalar1=1.0, scalar2=0.0, op0=MULT, op1=ADD)
-
-        def quantize_weight(d):
-            nc.vector.quantize_mx(
-                out=w_codes[d][:].bitcast(FP8X4),
-                scales=w_scales[d][:],
-                in_=rounded[d][:].rearrange("p t m j -> p (t m j)"),
+        def round_gpsimd(d, u):
+            dst, src = round_views(d, u)
+            nc.gpsimd.tensor_scalar(
+                out=dst.rearrange("p m j t -> p m t j"),
+                in0=src.rearrange("p m j t -> p m t j"),
+                scalar1=1.0,
+                scalar2=0.0,
+                op0=MULT,
+                op1=ADD,
             )
 
-        halves = {}
-
-        def round_half(d, u, engine, tag=None):
-            t = keep.tile([P, 2, P, PACK], BF16, name=f"half{d}_{u}", tag=tag or f"half{d}_{u}", align_bytes=64)
-            halves[d, u] = t
-            src = raw[d, 0][0][:].rearrange("p j (m t) -> p m j t", t=PACK)[:, :, :, 2 * u : 2 * u + 2]
-            dst = t[:].rearrange("p t m j -> p m j t")
-            if engine == "scalar":
-                nc.scalar.copy(out=dst, in_=src)
-            elif engine == "vector":
-                nc.vector.tensor_copy(out=dst, in_=src)
-            else:
-                nc.gpsimd.tensor_scalar(
-                    out=dst.rearrange("p m j t -> p m t j"),
-                    in0=src.rearrange("p m j t -> p m t j"),
-                    scalar1=1.0,
-                    scalar2=0.0,
-                    op0=MULT,
-                    op1=ADD,
-                )
-
-        def quantize_half(d, u):
-            cols = slice(2 * P * u, 2 * P * (u + 1))
+        def quantize_weight(d, t0, t1):
+            cols = slice(P * t0, P * t1)
             nc.vector.quantize_mx(
                 out=w_codes[d][:, cols].bitcast(FP8X4),
                 scales=w_scales[d][:, cols],
-                in_=halves[d, u][:].rearrange("p t m j -> p (t m j)"),
+                in_=rounded[d][:, H * t0 : H * t1],
             )
 
-        def clock(ap, name):
-            t = keep.tile([P, 1], ap.dtype, name=name)
-            nc.gpsimd.tensor_copy(out=t[:], in_=ap)
-
-        def piece(d):
-            return offsets[:, d * (V // 16) : (d + 1) * (V // 16)]
-
-        def gather_scales():
-            nc.vector.tensor_copy(out=x_bytes_all[:], in_=table_scales[:].indirect(offsets[:]))
-
-        def gather_early():
-            nc.vector.tensor_copy(out=early_codes[:], in_=table_words[:].indirect(offsets[:]))
-
-        def gather_late():
-            late_codes = keep.tile([P, V], U32, name="late_codes", tag="rounded0", align_bytes=64)
-            x_codes[2] = late_codes[:]
-            nc.vector.tensor_copy(out=late_codes[:], in_=table_words[:].indirect(piece(2)))
-
-        def load_row_pair(d, u):
-            t = keep.tile([P, 2, H], F32, name=f"rows{d}_{u}", align_bytes=64)
-            nc.sync.dma_start(out=t[:], in_=weights[d].rearrange("(p j) c -> p j c", j=PACK)[:, 2 * u : 2 * u + 2, :])
-            row_pairs[d, u] = t
-
-        def round_row_pair(d, u):
-            nc.scalar.copy(
-                out=rounded[d][:, :, :, 2 * u : 2 * u + 2].rearrange("p t m j -> p m j t"),
-                in_=row_pairs[d, u][:].rearrange("p j (m t) -> p m j t", t=PACK),
-            )
+        def gather_words(c0, c1, at):
+            codes = shared.tile([P, (c1 - c0) * CHUNK], U32, name=f"x_codes{c0}", align_bytes=64, offset=at)
+            picked = offsets[:, c0 * CHUNK // 16 : c1 * CHUNK // 16]
+            nc.vector.tensor_copy(out=codes[:], in_=table_words[:].indirect(picked))
+            for c in range(c0, c1):
+                x_codes[divmod(c, CHUNKS)] = codes[:, (c - c0) * CHUNK : (c - c0 + 1) * CHUNK]
 
         def product(d, c):
-            if d == 0:
-                bank = acc_pool.tile([P, PACK, CHUNK], F32, name="first_bank", bufs=2)
-            else:
-                bank = acc_pool.tile([P, PACK, CHUNK], F32, name="bank", bufs=3)
-            cols = slice(c * CHUNK, (c + 1) * CHUNK)
+            bank = psum.tile([P, PACK, CHUNK], F32, name="bank", bufs=6)
+            cols = slice(d * V + c * CHUNK, d * V + (c + 1) * CHUNK)
             for t in range(PACK):
                 chans = slice(t * P, (t + 1) * P)
                 nc.tensor.matmul_mx(
                     out=bank[:, t, :],
                     lhsT=w_codes[d][:, chans].bitcast(FP8X4),
                     lhsT_scale=w_scales[d][:, chans],
-                    rhs=x_codes[d][:, cols].bitcast(FP8X4),
-                    rhs_scale=x_bytes[d][:, cols],
+                    rhs=x_codes[d, c].bitcast(FP8X4),
+                    rhs_scale=x_bytes[:, cols],
                     start=True,
                     stop=True,
                 )
             return bank[:].rearrange("p t v -> p v t")
 
-        first = [keep.tile([P, CHUNK, PACK], F32, name=f"first{c}", align_bytes=64) for c in range(CHUNKS)]
-        pair = {}
-        z = {}
         z_codes = [keep.tile([P, CHUNK], U32, name=f"z_codes{c}", align_bytes=64) for c in range(CHUNKS)]
         z_scales = [keep.tile([P, CHUNK], U8, name=f"z_scales{c}", align_bytes=64) for c in range(CHUNKS)]
         staged = [keep.tile([P, HALVES, CHUNK], F32, name=f"staged{c}", align_bytes=64) for c in range(CHUNKS)]
         out_view = out.rearrange("(h m) v -> m h v", h=HALVES)
 
-        def first_factor(c):
-            nc.scalar.copy(out=first[c][:], in_=product(0, c))
+        def first_factor(c, at, bank=None):
+            first[c] = shared.tile([P, CHUNK, PACK], F32, name=f"first{c}", align_bytes=64, offset=at)
+            nc.scalar.copy(out=first[c][:], in_=product(0, c) if bank is None else bank)
 
-        def second_factor(c):
-            pair[c] = keep.tile([P, CHUNK, PACK], F32, name=f"pair{c}", tag="half2_1" if c == 0 else f"pair{c}", align_bytes=64)
-            nc.vector.tensor_tensor(out=pair[c][:], in0=product(1, c), in1=first[c][:], op=MULT)
-
-        def second_factor_gpsimd(c):
-            second = keep.tile([P, CHUNK, PACK], F32, name="second", align_bytes=64)
-            pair[c] = keep.tile([P, CHUNK, PACK], F32, name=f"pair{c}", align_bytes=64)
+        def second_factor_gpsimd(c, at):
+            second = shared.tile([P, CHUNK, PACK], F32, name="second", align_bytes=64, offset=RAW_AT[2] + 4 * KIB)
+            pair[c] = shared.tile([P, CHUNK, PACK], F32, name=f"pair{c}", align_bytes=64, offset=at)
             nc.scalar.copy(out=second[:], in_=product(1, c))
             nc.gpsimd.tensor_tensor(out=pair[c][:], in0=second[:], in1=first[c][:], op=MULT)
+
+        def second_factor(c, at):
+            pair[c] = shared.tile([P, CHUNK, PACK], F32, name=f"pair{c}", align_bytes=64, offset=at)
+            nc.vector.tensor_tensor(out=pair[c][:], in0=product(1, c), in1=first[c][:], op=MULT)
 
         def third_factor(c):
             z[c] = ring.tile([P, CHUNK, PACK], BF16, name="z", align_bytes=64)
@@ -212,14 +166,14 @@ def tile_picked_trilin_none_p_kernel(
                     stop=True,
                 )
 
-            res = res_pool.tile([P, HALVES, CHUNK], F32, name="res")
+            res = psum.tile([P, HALVES, CHUNK], F32, name="res", bufs=2)
             if c < CHUNKS - 1:
                 for h in range(HALVES):
                     last_product(res[:, h, :], h)
                 nc.scalar.copy(out=staged[c][:], in_=res[:])
                 nc.sync.dma_start(out=out_view[:, :, cols], in_=staged[c][:])
             else:
-                other = res_pool.tile([P, CHUNK], F32, name="other", bufs=1)
+                other = psum.tile([P, CHUNK], F32, name="other", tag="bank", bufs=6)
                 last_product(res[:, 0, :], 0)
                 last_product(other[:], 1)
                 nc.scalar.copy(out=staged[c][:, 0, :], in_=res[:, 0, :])
@@ -227,44 +181,42 @@ def tile_picked_trilin_none_p_kernel(
                 nc.scalar.dma_start(out=out_view[:, 0, cols], in_=staged[c][:, 0, :])
                 nc.sync.dma_start(out=out_view[:, 1, cols], in_=staged[c][:, 1, :])
 
-        def load_table_words():
-            nc.sync.dma_start(
-                out=table_words[:].bitcast(I32), in_=x_words[0].rearrange("p c r -> p (c r)").bitcast(I32)
-            )
-
-        def load_last():
-            nc.sync.dma_start(out=last_words[:].bitcast(I32), in_=w4_words[0].bitcast(I32))
-            load_scale_rows(nc.sync, last_scales, w4_scales)
-
         nc.sync.dma_start(offsets[:], offs)
-        load_scale_rows(nc.sync, table_scales, x_scales)
-        load_table_words()
-        load_weight(0, 0, P)
-        load_weight(1, 0, P)
-        load_weight(2, 0, P)
-        load_last()
+        load_scale_rows(table_scales, x_scales)
+        load_weight(0)
+        nc.sync.dma_start(out=table_words[:].bitcast(I32), in_=x_words[0].rearrange("p c r -> p (c r)").bitcast(I32))
+        load_weight(1)
+        load_weight(2)
+        nc.sync.dma_start(out=last_words[:].bitcast(I32), in_=w4_words[0].bitcast(I32))
+        load_scale_rows(last_scales, w4_scales)
 
-        gather_scales()
-        gather_early()
-        round_scalar(0, 0, P)
-        quantize_weight(0)
-        round_half(1, 0, "scalar")
-        round_half(1, 1, "vector", tag="rounded0")
-        quantize_half(1, 0)
-        quantize_half(1, 1)
-        round_half(2, 1, "vector")
-        quantize_half(2, 1)
-        first_factor(0)
-        second_factor(0)
-        round_half(2, 0, "scalar")
-        quantize_half(2, 0)
-        first_factor(1)
-        second_factor(1)
-        first_factor(3)
-        second_factor_gpsimd(3)
+        nc.vector.tensor_copy(out=x_bytes[:], in_=table_scales[:].indirect(offsets[:]))
+        place_rounded(0, AT + KIB)
+        round_scalar(0, 0)
+        round_gpsimd(0, 1)
+        quantize_weight(0, 0, 4)
+        gather_words(0, 2, AT + KIB // 2)
+        gather_words(2, 8, AT + 3 * KIB // 2)
+        gather_words(8, 10, AT + 9 * KIB // 2)
+        first_factor(0, AT + 10 * KIB)
+        place_rounded(1, AT + 6 * KIB)
+        round_scalar(1, 0)
+        round_gpsimd(1, 1)
+        quantize_weight(1, 2, 4)
+        quantize_weight(1, 0, 2)
+        gather_words(10, 12, AT + 6 * KIB)
+        first_factor(1, RAW_AT[1])
+        place_rounded(2, AT + 14 * KIB)
+        round_scalar(2, 0)
+        round_gpsimd(2, 1)
+        second_factor(0, AT + 18 * KIB)
+        quantize_weight(2, 0, 4)
+        first_factor(2, RAW_AT[2])
+        first_factor(3, RAW_AT[2] + 2 * KIB)
+        second_factor(1, AT + 14 * KIB)
+        second_factor_gpsimd(3, AT + 24 * KIB)
+        second_factor(2, AT + 26 * KIB)
         third_factor(0)
-        first_factor(2)
-        second_factor(2)
         for c in range(1, CHUNKS):
             third_factor(c)
             finish(c - 1)

@@ -34,7 +34,6 @@ def tile_picked_trilin_none_p_kernel(
     with ExitStack() as ctx:
         keep = ctx.enter_context(tc.tile_pool(name="keep", bufs=1))
         shared = ctx.enter_context(tc.tile_pool(name="shared", bufs=1))
-        ring = ctx.enter_context(tc.tile_pool(name="ring", bufs=2))
         psum = ctx.enter_context(tc.psum_pool(name="psum", bufs=1))
 
         offsets = keep.tile([P, S // 16], U16, name="offsets")
@@ -42,7 +41,7 @@ def tile_picked_trilin_none_p_kernel(
         table_scales = keep.tile([P, T], U8, name="table_scales", align_bytes=64)
         last_words = keep.tile([P, 2 * N], U8, name="last_words", align_bytes=64)
         last_scales = keep.tile([P, N], U8, name="last_scales", align_bytes=64)
-        w_codes = [keep.tile([P, H], U32, name=f"w_codes{d}", align_bytes=64) for d in range(PIECES)]
+        w_codes = {}
         w_scales = [keep.tile([P, H], U8, name=f"w_scales{d}", align_bytes=64) for d in range(PIECES)]
         x_bytes = keep.tile([P, S], U8, name="x_bytes", align_bytes=64)
 
@@ -53,7 +52,8 @@ def tile_picked_trilin_none_p_kernel(
         x_codes = {}
         first = {}
         pair = {}
-        z = {}
+        banks = {}
+        z_codes = {}
 
         def load_scale_rows(plane, rows):
             for q in range(4):
@@ -66,39 +66,35 @@ def tile_picked_trilin_none_p_kernel(
             raw[d] = shared.tile([P, PACK, H], F32, name=f"raw{d}", align_bytes=64, offset=RAW_AT[d])
             nc.sync.dma_start(out=raw[d][:], in_=weights[d].rearrange("(p j) c -> p j c", j=PACK))
 
-        def place_rounded(d, at):
-            rounded[d] = shared.tile([P, PACK * H], BF16, name=f"rounded{d}", align_bytes=64, offset=at)
+        def place_rounded(d, t0, t1, at):
+            tile = shared.tile([P, (t1 - t0) * H], BF16, name=f"rounded{d}_{t0}", align_bytes=64, offset=at)
+            for t in range(t0, t1):
+                rounded[d, t] = (tile, t0)
 
-        def round_views(d, u):
-            src = raw[d][:].rearrange("p j (m t) -> p m j t", t=PACK)[:, :, :, 2 * u : 2 * u + 2]
-            dst = rounded[d][:, 2 * H * u : 2 * H * (u + 1)].rearrange("p (t m j) -> p m j t", t=2, j=PACK)
+        def rounded_part(d, t0, t1):
+            tile, base = rounded[d, t0]
+            return tile[:, (t0 - base) * H : (t1 - base) * H]
+
+        def round_views(d, t0, t1):
+            src = raw[d][:].rearrange("p j (m t) -> p m j t", t=PACK)[:, :, :, t0:t1]
+            dst = rounded_part(d, t0, t1).rearrange("p (t m j) -> p m j t", m=P, j=PACK)
             return dst, src
 
-        def round_scalar(d, u):
-            dst, src = round_views(d, u)
+        def round_scalar(d, t0, t1):
+            dst, src = round_views(d, t0, t1)
             nc.scalar.copy(out=dst, in_=src)
 
-        def round_vector(d, u):
-            dst, src = round_views(d, u)
+        def round_vector(d, t0, t1):
+            dst, src = round_views(d, t0, t1)
             nc.vector.tensor_copy(out=dst, in_=src)
 
-        def round_gpsimd(d, u):
-            dst, src = round_views(d, u)
-            nc.gpsimd.tensor_scalar(
-                out=dst.rearrange("p m j t -> p m t j"),
-                in0=src.rearrange("p m j t -> p m t j"),
-                scalar1=1.0,
-                scalar2=0.0,
-                op0=MULT,
-                op1=ADD,
-            )
+        def place_codes(d, at):
+            w_codes[d] = shared.tile([P, H], U32, name=f"w_codes{d}", align_bytes=64, offset=at)
 
         def quantize_weight(d, t0, t1):
             cols = slice(P * t0, P * t1)
             nc.vector.quantize_mx(
-                out=w_codes[d][:, cols].bitcast(FP8X4),
-                scales=w_scales[d][:, cols],
-                in_=rounded[d][:, H * t0 : H * t1],
+                out=w_codes[d][:, cols].bitcast(FP8X4), scales=w_scales[d][:, cols], in_=rounded_part(d, t0, t1)
             )
 
         def gather_words(c0, c1, at):
@@ -109,7 +105,7 @@ def tile_picked_trilin_none_p_kernel(
                 x_codes[divmod(c, CHUNKS)] = codes[:, (c - c0) * CHUNK : (c - c0 + 1) * CHUNK]
 
         def product(d, c):
-            bank = psum.tile([P, PACK, CHUNK], F32, name="bank", bufs=6)
+            bank = psum.tile([P, PACK, CHUNK], F32, name="bank", bufs=8)
             cols = slice(d * V + c * CHUNK, d * V + (c + 1) * CHUNK)
             for t in range(PACK):
                 chans = slice(t * P, (t + 1) * P)
@@ -122,37 +118,42 @@ def tile_picked_trilin_none_p_kernel(
                     start=True,
                     stop=True,
                 )
-            return bank[:].rearrange("p t v -> p v t")
+            banks[d, c] = bank[:].rearrange("p t v -> p v t")
 
-        z_codes = [keep.tile([P, CHUNK], U32, name=f"z_codes{c}", align_bytes=64) for c in range(CHUNKS)]
-        z_scales = [keep.tile([P, CHUNK], U8, name=f"z_scales{c}", align_bytes=64) for c in range(CHUNKS)]
         staged = [keep.tile([P, HALVES, CHUNK], F32, name=f"staged{c}", align_bytes=64) for c in range(CHUNKS)]
         out_view = out.rearrange("(h m) v -> m h v", h=HALVES)
+        z = keep.tile([P, V * PACK], BF16, name="z", align_bytes=64)
+        z_scales = keep.tile([P, V], U8, name="z_scales", align_bytes=64)
 
-        def first_factor(c, at, bank=None):
+        def first_factor(c, at):
             first[c] = shared.tile([P, CHUNK, PACK], F32, name=f"first{c}", align_bytes=64, offset=at)
-            nc.scalar.copy(out=first[c][:], in_=product(0, c) if bank is None else bank)
+            nc.scalar.copy(out=first[c][:], in_=banks[0, c])
 
         def second_factor_gpsimd(c, at):
-            second = shared.tile([P, CHUNK, PACK], F32, name="second", align_bytes=64, offset=RAW_AT[2] + 4 * KIB)
-            pair[c] = shared.tile([P, CHUNK, PACK], F32, name=f"pair{c}", align_bytes=64, offset=at)
-            nc.scalar.copy(out=second[:], in_=product(1, c))
+            second = shared.tile([P, CHUNK, PACK], F32, name="second", align_bytes=64, offset=at)
+            pair[c] = keep.tile([P, CHUNK, PACK], F32, name=f"pair{c}", align_bytes=64)
+            nc.scalar.copy(out=second[:], in_=banks[1, c])
             nc.gpsimd.tensor_tensor(out=pair[c][:], in0=second[:], in1=first[c][:], op=MULT)
 
-        def second_factor(c, at):
-            pair[c] = shared.tile([P, CHUNK, PACK], F32, name=f"pair{c}", align_bytes=64, offset=at)
-            nc.vector.tensor_tensor(out=pair[c][:], in0=product(1, c), in1=first[c][:], op=MULT)
+        def second_factor(c):
+            pair[c] = keep.tile([P, CHUNK, PACK], F32, name=f"pair{c}", align_bytes=64)
+            nc.vector.tensor_tensor(out=pair[c][:], in0=banks[1, c], in1=first[c][:], op=MULT)
 
         def third_factor(c):
-            z[c] = ring.tile([P, CHUNK, PACK], BF16, name="z", align_bytes=64)
-            nc.vector.tensor_tensor(out=z[c][:], in0=product(2, c), in1=pair[c][:], op=MULT)
+            part = z[:, c * CHUNK * PACK : (c + 1) * CHUNK * PACK].rearrange("p (v t) -> p v t", t=PACK)
+            nc.vector.tensor_tensor(out=part, in0=banks[2, c], in1=pair[c][:], op=MULT)
+
+        def quantize_z(c0, c1, at):
+            codes = shared.tile([P, (c1 - c0) * CHUNK], U32, name=f"z_codes{c0}", align_bytes=64, offset=at)
+            nc.vector.quantize_mx(
+                out=codes[:].bitcast(FP8X4),
+                scales=z_scales[:, c0 * CHUNK : c1 * CHUNK],
+                in_=z[:, c0 * CHUNK * PACK : c1 * CHUNK * PACK],
+            )
+            for c in range(c0, c1):
+                z_codes[c] = codes[:, (c - c0) * CHUNK : (c - c0 + 1) * CHUNK]
 
         def finish(c):
-            nc.vector.quantize_mx(
-                out=z_codes[c][:].bitcast(FP8X4),
-                scales=z_scales[c][:],
-                in_=z[c][:].rearrange("p v t -> p (v t)"),
-            )
             cols = slice(c * CHUNK, (c + 1) * CHUNK)
 
             def last_product(target, h):
@@ -160,20 +161,20 @@ def tile_picked_trilin_none_p_kernel(
                     out=target,
                     lhsT=last_words[:, 2 * P * h : 2 * P * (h + 1)].bitcast(FP4X4),
                     lhsT_scale=last_scales[:, P * h : P * (h + 1)],
-                    rhs=z_codes[c][:].bitcast(FP8X4),
-                    rhs_scale=z_scales[c][:],
+                    rhs=z_codes[c].bitcast(FP8X4),
+                    rhs_scale=z_scales[:, cols],
                     start=True,
                     stop=True,
                 )
 
-            res = psum.tile([P, HALVES, CHUNK], F32, name="res", bufs=2)
+            res = psum.tile([P, HALVES, CHUNK], F32, name="res", tag="bank", bufs=8)
             if c < CHUNKS - 1:
                 for h in range(HALVES):
                     last_product(res[:, h, :], h)
                 nc.scalar.copy(out=staged[c][:], in_=res[:])
                 nc.sync.dma_start(out=out_view[:, :, cols], in_=staged[c][:])
             else:
-                other = psum.tile([P, CHUNK], F32, name="other", tag="bank", bufs=6)
+                other = psum.tile([P, CHUNK], F32, name="other", tag="bank", bufs=8)
                 last_product(res[:, 0, :], 0)
                 last_product(other[:], 1)
                 nc.scalar.copy(out=staged[c][:, 0, :], in_=res[:, 0, :])
@@ -181,43 +182,59 @@ def tile_picked_trilin_none_p_kernel(
                 nc.scalar.dma_start(out=out_view[:, 0, cols], in_=staged[c][:, 0, :])
                 nc.sync.dma_start(out=out_view[:, 1, cols], in_=staged[c][:, 1, :])
 
+        seed = keep.tile([P, 1], F32, name="seed")
+        sink = keep.tile([P, 1], F32, name="sink")
+        nc.gpsimd.memset(seed[:], 0.0)
+        nc.scalar.copy(out=sink[:], in_=seed[:])
         nc.sync.dma_start(offsets[:], offs)
         load_scale_rows(table_scales, x_scales)
-        load_weight(0)
         nc.sync.dma_start(out=table_words[:].bitcast(I32), in_=x_words[0].rearrange("p c r -> p (c r)").bitcast(I32))
+        load_weight(0)
         load_weight(1)
         load_weight(2)
         nc.sync.dma_start(out=last_words[:].bitcast(I32), in_=w4_words[0].bitcast(I32))
         load_scale_rows(last_scales, w4_scales)
 
         nc.vector.tensor_copy(out=x_bytes[:], in_=table_scales[:].indirect(offsets[:]))
-        place_rounded(0, AT + KIB)
-        round_scalar(0, 0)
-        round_gpsimd(0, 1)
+        gather_words(0, 12, AT)
+        place_rounded(0, 0, 4, AT + 6 * KIB)
+        round_scalar(0, 0, 4)
+        place_codes(0, AT + 24 * KIB)
         quantize_weight(0, 0, 4)
-        gather_words(0, 2, AT + KIB // 2)
-        gather_words(2, 8, AT + 3 * KIB // 2)
-        gather_words(8, 10, AT + 9 * KIB // 2)
-        first_factor(0, AT + 10 * KIB)
-        place_rounded(1, AT + 6 * KIB)
-        round_scalar(1, 0)
-        round_gpsimd(1, 1)
-        quantize_weight(1, 2, 4)
-        quantize_weight(1, 0, 2)
-        gather_words(10, 12, AT + 6 * KIB)
-        first_factor(1, RAW_AT[1])
-        place_rounded(2, AT + 14 * KIB)
-        round_scalar(2, 0)
-        round_gpsimd(2, 1)
-        second_factor(0, AT + 18 * KIB)
+        for c in range(CHUNKS):
+            product(0, c)
+        place_rounded(1, 0, 4, AT + 5 * KIB + 5 * KIB)
+        round_scalar(1, 0, 2)
+        round_vector(1, 2, 4)
+        place_codes(1, AT + 18 * KIB)
+        quantize_weight(1, 0, 4)
+        for c in (0, 1, 3):
+            product(1, c)
+        place_rounded(2, 0, 4, AT + 14 * KIB)
+        round_scalar(2, 0, 2)
+        round_vector(2, 2, 4)
+        place_codes(2, AT + 20 * KIB)
         quantize_weight(2, 0, 4)
-        first_factor(2, RAW_AT[2])
-        first_factor(3, RAW_AT[2] + 2 * KIB)
-        second_factor(1, AT + 14 * KIB)
-        second_factor_gpsimd(3, AT + 24 * KIB)
-        second_factor(2, AT + 26 * KIB)
+        for c in (0, 1, 3):
+            first_factor(c, RAW_AT[2] + 2 * KIB * c)
+        second_factor(0)
+        second_factor(1)
+        second_factor_gpsimd(3, AT + 14 * KIB)
+        product(2, 0)
         third_factor(0)
-        for c in range(1, CHUNKS):
-            third_factor(c)
-            finish(c - 1)
-        finish(CHUNKS - 1)
+        product(2, 1)
+        third_factor(1)
+        first_factor(2, RAW_AT[2] + 4 * KIB)
+        product(1, 2)
+        second_factor(2)
+        quantize_z(0, 2, AT + 14 * KIB)
+        product(2, 2)
+        third_factor(2)
+        product(2, 3)
+        finish(0)
+        finish(1)
+        third_factor(3)
+        quantize_z(2, 3, AT + 22 * KIB)
+        finish(2)
+        quantize_z(3, 4, AT + 23 * KIB)
+        finish(3)

@@ -44,6 +44,7 @@ def tile_picked_trilin_none_p_kernel(
         w_codes = {}
         w_scales = [keep.tile([P, H], U8, name=f"w_scales{d}", align_bytes=64) for d in range(PIECES)]
         x_bytes = keep.tile([P, S], U8, name="x_bytes", align_bytes=64)
+        picked_bytes = keep.tile([P, S], U8, name="picked_bytes", align_bytes=64)
 
         RAW_AT = [0, 8 * KIB, 16 * KIB]
         AT = 24 * KIB
@@ -187,7 +188,10 @@ def tile_picked_trilin_none_p_kernel(
         nc.gpsimd.memset(seed[:], 0.0)
         nc.scalar.copy(out=sink[:], in_=seed[:])
         nc.sync.dma_start(offsets[:], offs)
-        load_scale_rows(table_scales, x_scales)
+        nc.sync.dma_start(
+            out=table_scales[:].bitcast(I32),
+            in_=x_scales[0].bitcast(I32).unsqueeze(1).to_broadcast([16, 8, T // 4]),
+        )
         nc.sync.dma_start(out=table_words[:].bitcast(I32), in_=x_words[0].rearrange("p c r -> p (c r)").bitcast(I32))
         load_weight(0)
         load_weight(1)
@@ -195,7 +199,13 @@ def tile_picked_trilin_none_p_kernel(
         nc.sync.dma_start(out=last_words[:].bitcast(I32), in_=w4_words[0].bitcast(I32))
         load_scale_rows(last_scales, w4_scales)
 
-        nc.vector.tensor_copy(out=x_bytes[:], in_=table_scales[:].indirect(offsets[:]))
+        nc.gpsimd.memset(x_bytes[:].bitcast(I32), 0)
+        nc.vector.tensor_copy(out=picked_bytes[:], in_=table_scales[:].indirect(offsets[:]))
+        for q in range(4):
+            nc.scalar.dma_start(
+                out=x_bytes[32 * q : 32 * q + 4, :].bitcast(I32),
+                in_=picked_bytes[32 * q : 32 * q + 32 : 8, :].bitcast(I32),
+            )
         gather_words(0, 12, AT)
         place_rounded(0, 0, 4, AT + 6 * KIB)
         round_scalar(0, 0, 4)

@@ -195,17 +195,17 @@ def tile_picked_trilin_none_p_kernel(
         nc.sync.dma_start(out=table_words[:].bitcast(I32), in_=x_words[0].rearrange("p c r -> p (c r)").bitcast(I32))
         load_weight(0)
         load_weight(1)
-        load_weight(2)
-        nc.sync.dma_start(out=last_words[:].bitcast(I32), in_=w4_words[0].bitcast(I32))
-        load_scale_rows(last_scales, w4_scales)
 
         nc.gpsimd.memset(x_bytes[:].bitcast(I32), 0)
         nc.vector.tensor_copy(out=picked_bytes[:], in_=table_scales[:].indirect(offsets[:]))
         for q in range(4):
-            nc.scalar.dma_start(
+            nc.sync.dma_start(
                 out=x_bytes[32 * q : 32 * q + 4, :].bitcast(I32),
                 in_=picked_bytes[32 * q : 32 * q + 32 : 8, :].bitcast(I32),
             )
+        load_weight(2)
+        nc.sync.dma_start(out=last_words[:].bitcast(I32), in_=w4_words[0].bitcast(I32))
+        load_scale_rows(last_scales, w4_scales)
         gather_words(0, 12, AT)
         place_rounded(0, 0, 4, AT + 6 * KIB)
         round_scalar(0, 0, 4)

@@ -63,6 +63,13 @@ def tile_picked_trilin_none_p_kernel(
                     in_=rows[0, 4 * q : 4 * q + 4, :].bitcast(I32).partition_broadcast(8),
                 )
 
+        def move_scale_rows(lo, hi):
+            for q in (0, 2, 1, 3):
+                nc.sync.dma_start(
+                    out=x_bytes[32 * q : 32 * q + 4, lo:hi].bitcast(I32),
+                    in_=picked_bytes[32 * q : 32 * q + 32 : 8, lo:hi].bitcast(I32),
+                )
+
         def load_weight(d):
             raw[d] = shared.tile([P, PACK, H], F32, name=f"raw{d}", align_bytes=64, offset=RAW_AT[d])
             nc.sync.dma_start(out=raw[d][:], in_=weights[d].rearrange("(p j) c -> p j c", j=PACK))
@@ -121,7 +128,6 @@ def tile_picked_trilin_none_p_kernel(
                 )
             banks[d, c] = bank[:].rearrange("p t v -> p v t")
 
-        staged = [keep.tile([P, HALVES, CHUNK], F32, name=f"staged{c}", align_bytes=64) for c in range(CHUNKS)]
         out_view = out.rearrange("(h m) v -> m h v", h=HALVES)
         z = keep.tile([P, V * PACK], BF16, name="z", align_bytes=64)
         z_scales = keep.tile([P, V], U8, name="z_scales", align_bytes=64)
@@ -145,50 +151,43 @@ def tile_picked_trilin_none_p_kernel(
             nc.vector.tensor_tensor(out=part, in0=banks[2, c], in1=pair[c][:], op=MULT)
 
         def quantize_z(c0, c1, at):
-            codes = shared.tile([P, (c1 - c0) * CHUNK], U32, name=f"z_codes{c0}", align_bytes=64, offset=at)
+            z_codes[c0] = shared.tile([P, (c1 - c0) * CHUNK], U32, name=f"z_codes{c0}", align_bytes=64, offset=at)
             nc.vector.quantize_mx(
-                out=codes[:].bitcast(FP8X4),
+                out=z_codes[c0][:].bitcast(FP8X4),
                 scales=z_scales[:, c0 * CHUNK : c1 * CHUNK],
                 in_=z[:, c0 * CHUNK * PACK : c1 * CHUNK * PACK],
             )
-            for c in range(c0, c1):
-                z_codes[c] = codes[:, (c - c0) * CHUNK : (c - c0 + 1) * CHUNK]
 
-        def finish(c):
-            cols = slice(c * CHUNK, (c + 1) * CHUNK)
+        def last_product(target, h, c0, c1):
+            nc.tensor.matmul_mx(
+                out=target,
+                lhsT=last_words[:, 2 * P * h : 2 * P * (h + 1)].bitcast(FP4X4),
+                lhsT_scale=last_scales[:, P * h : P * (h + 1)],
+                rhs=z_codes[c0][:].bitcast(FP8X4),
+                rhs_scale=z_scales[:, c0 * CHUNK : c1 * CHUNK],
+                start=True,
+                stop=True,
+            )
 
-            def last_product(target, h):
-                nc.tensor.matmul_mx(
-                    out=target,
-                    lhsT=last_words[:, 2 * P * h : 2 * P * (h + 1)].bitcast(FP4X4),
-                    lhsT_scale=last_scales[:, P * h : P * (h + 1)],
-                    rhs=z_codes[c].bitcast(FP8X4),
-                    rhs_scale=z_scales[:, cols],
-                    start=True,
-                    stop=True,
-                )
+        def finish(c0, c1, copy):
+            width = (c1 - c0) * CHUNK
+            res = psum.tile([P, HALVES, width], F32, name="res", tag="bank", bufs=8)
+            staged = keep.tile([P, HALVES, width], F32, name=f"staged{c0}", align_bytes=64)
+            for h in range(HALVES):
+                last_product(res[:, h, :], h, c0, c1)
+            copy(out=staged[:], in_=res[:])
+            nc.sync.dma_start(out=out_view[:, :, c0 * CHUNK : c1 * CHUNK], in_=staged[:])
 
-            res = psum.tile([P, HALVES, CHUNK], F32, name="res", tag="bank", bufs=8)
-            if c < CHUNKS - 1:
-                for h in range(HALVES):
-                    last_product(res[:, h, :], h)
-                nc.scalar.copy(out=staged[c][:], in_=res[:])
-                nc.sync.dma_start(out=out_view[:, :, cols], in_=staged[c][:])
-            else:
-                other = psum.tile([P, CHUNK], F32, name="other", tag="bank", bufs=8)
-                last_product(res[:, 0, :], 0)
-                last_product(other[:], 1)
-                nc.scalar.copy(out=staged[c][:, 0, :], in_=res[:, 0, :])
-                nc.vector.tensor_copy(out=staged[c][:, 1, :], in_=other[:])
-                nc.scalar.dma_start(out=out_view[:, 0, cols], in_=staged[c][:, 0, :])
-                nc.sync.dma_start(out=out_view[:, 1, cols], in_=staged[c][:, 1, :])
+        def finish_last(c):
+            for h, copy, queue in ((0, nc.scalar.copy, nc.scalar), (1, nc.vector.tensor_copy, nc.sync)):
+                res = psum.tile([P, CHUNK], F32, name="res", tag="bank", bufs=8)
+                staged = keep.tile([P, CHUNK], F32, name=f"staged_last{h}", align_bytes=64)
+                last_product(res[:], h, c, c + 1)
+                copy(out=staged[:], in_=res[:])
+                queue.dma_start(out=out_view[:, h, c * CHUNK : (c + 1) * CHUNK], in_=staged[:])
 
-        seed = keep.tile([P, 1], F32, name="seed")
-        sink = keep.tile([P, 1], F32, name="sink")
-        nc.gpsimd.memset(seed[:], 0.0)
-        nc.scalar.copy(out=sink[:], in_=seed[:])
         nc.sync.dma_start(offsets[:], offs)
-        nc.sync.dma_start(
+        nc.scalar.dma_start(
             out=table_scales[:].bitcast(I32),
             in_=x_scales[0].bitcast(I32).unsqueeze(1).to_broadcast([16, 8, T // 4]),
         )
@@ -198,12 +197,9 @@ def tile_picked_trilin_none_p_kernel(
 
         nc.gpsimd.memset(x_bytes[:].bitcast(I32), 0)
         nc.vector.tensor_copy(out=picked_bytes[:], in_=table_scales[:].indirect(offsets[:]))
-        for q in range(4):
-            nc.sync.dma_start(
-                out=x_bytes[32 * q : 32 * q + 4, :].bitcast(I32),
-                in_=picked_bytes[32 * q : 32 * q + 32 : 8, :].bitcast(I32),
-            )
+        move_scale_rows(0, 2 * V)
         load_weight(2)
+        move_scale_rows(2 * V, S)
         nc.sync.dma_start(out=last_words[:].bitcast(I32), in_=w4_words[0].bitcast(I32))
         load_scale_rows(last_scales, w4_scales)
         gather_words(0, 12, AT)
@@ -213,11 +209,13 @@ def tile_picked_trilin_none_p_kernel(
         quantize_weight(0, 0, 4)
         for c in range(CHUNKS):
             product(0, c)
-        place_rounded(1, 0, 4, AT + 5 * KIB + 5 * KIB)
+        place_rounded(1, 0, 2, AT + 10 * KIB)
+        place_rounded(1, 2, 4, AT + 6 * KIB)
         round_scalar(1, 0, 2)
         round_vector(1, 2, 4)
         place_codes(1, AT + 18 * KIB)
-        quantize_weight(1, 0, 4)
+        quantize_weight(1, 0, 2)
+        quantize_weight(1, 2, 4)
         for c in (0, 1, 3):
             product(1, c)
         place_rounded(2, 0, 4, AT + 14 * KIB)
@@ -241,10 +239,9 @@ def tile_picked_trilin_none_p_kernel(
         product(2, 2)
         third_factor(2)
         product(2, 3)
-        finish(0)
-        finish(1)
+        finish(0, 2, nc.scalar.copy)
         third_factor(3)
         quantize_z(2, 3, AT + 22 * KIB)
-        finish(2)
+        finish(2, 3, nc.scalar.copy)
         quantize_z(3, 4, AT + 23 * KIB)
-        finish(3)
+        finish_last(3)

@@ -67,7 +67,7 @@ def tile_picked_trilin_none_p_kernel(
             for q in (0, 2, 1, 3):
                 nc.sync.dma_start(
                     out=x_bytes[32 * q : 32 * q + 4, lo:hi].bitcast(I32),
-                    in_=picked_bytes[32 * q : 32 * q + 32 : 8, lo:hi].bitcast(I32),
+                    in_=picked_bytes[32 + 16 * q : 48 + 16 * q : 4, lo:hi].bitcast(I32),
                 )
 
         def load_weight(d):
@@ -83,17 +83,17 @@ def tile_picked_trilin_none_p_kernel(
             tile, base = rounded[d, t0]
             return tile[:, (t0 - base) * H : (t1 - base) * H]
 
-        def round_views(d, t0, t1):
-            src = raw[d][:].rearrange("p j (m t) -> p m j t", t=PACK)[:, :, :, t0:t1]
-            dst = rounded_part(d, t0, t1).rearrange("p (t m j) -> p m j t", m=P, j=PACK)
+        def round_views(d, t0, t1, m0, m1):
+            src = raw[d][:].rearrange("p j (m t) -> p m j t", t=PACK)[:, m0:m1, :, t0:t1]
+            dst = rounded_part(d, t0, t1).rearrange("p (t m j) -> p m j t", m=P, j=PACK)[:, m0:m1]
             return dst, src
 
-        def round_scalar(d, t0, t1):
-            dst, src = round_views(d, t0, t1)
+        def round_scalar(d, t0, t1, m0=0, m1=P):
+            dst, src = round_views(d, t0, t1, m0, m1)
             nc.scalar.copy(out=dst, in_=src)
 
-        def round_vector(d, t0, t1):
-            dst, src = round_views(d, t0, t1)
+        def round_vector(d, t0, t1, m0=0, m1=P):
+            dst, src = round_views(d, t0, t1, m0, m1)
             nc.vector.tensor_copy(out=dst, in_=src)
 
         def place_codes(d, at):
@@ -113,7 +113,10 @@ def tile_picked_trilin_none_p_kernel(
                 x_codes[divmod(c, CHUNKS)] = codes[:, (c - c0) * CHUNK : (c - c0 + 1) * CHUNK]
 
         def product(d, c):
-            bank = psum.tile([P, PACK, CHUNK], F32, name="bank", bufs=8)
+            if d == 0:
+                bank = psum.tile([P, PACK, CHUNK], F32, name="first_bank", bufs=2)
+            else:
+                bank = psum.tile([P, PACK, CHUNK], F32, name="bank", bufs=6)
             cols = slice(d * V + c * CHUNK, d * V + (c + 1) * CHUNK)
             for t in range(PACK):
                 chans = slice(t * P, (t + 1) * P)
@@ -142,8 +145,8 @@ def tile_picked_trilin_none_p_kernel(
             nc.scalar.copy(out=second[:], in_=banks[1, c])
             nc.gpsimd.tensor_tensor(out=pair[c][:], in0=second[:], in1=first[c][:], op=MULT)
 
-        def second_factor(c):
-            pair[c] = keep.tile([P, CHUNK, PACK], F32, name=f"pair{c}", align_bytes=64)
+        def second_factor(c, at):
+            pair[c] = shared.tile([P, CHUNK, PACK], F32, name=f"pair{c}", align_bytes=64, offset=at)
             nc.vector.tensor_tensor(out=pair[c][:], in0=banks[1, c], in1=first[c][:], op=MULT)
 
         def third_factor(c):
@@ -171,7 +174,7 @@ def tile_picked_trilin_none_p_kernel(
 
         def finish(c0, c1, copy):
             width = (c1 - c0) * CHUNK
-            res = psum.tile([P, HALVES, width], F32, name="res", tag="bank", bufs=8)
+            res = psum.tile([P, HALVES, width], F32, name="res", tag="bank", bufs=6)
             staged = keep.tile([P, HALVES, width], F32, name=f"staged{c0}", align_bytes=64)
             for h in range(HALVES):
                 last_product(res[:, h, :], h, c0, c1)
@@ -180,7 +183,7 @@ def tile_picked_trilin_none_p_kernel(
 
         def finish_last(c):
             for h, copy, queue in ((0, nc.scalar.copy, nc.scalar), (1, nc.vector.tensor_copy, nc.sync)):
-                res = psum.tile([P, CHUNK], F32, name="res", tag="bank", bufs=8)
+                res = psum.tile([P, CHUNK], F32, name="res", tag="bank", bufs=6)
                 staged = keep.tile([P, CHUNK], F32, name=f"staged_last{h}", align_bytes=64)
                 last_product(res[:], h, c, c + 1)
                 copy(out=staged[:], in_=res[:])
@@ -188,9 +191,11 @@ def tile_picked_trilin_none_p_kernel(
 
         nc.sync.dma_start(offsets[:], offs)
         nc.scalar.dma_start(
-            out=table_scales[:].bitcast(I32),
-            in_=x_scales[0].bitcast(I32).unsqueeze(1).to_broadcast([16, 8, T // 4]),
+            out=table_scales[32:96, :].bitcast(I32),
+            in_=x_scales[0].bitcast(I32).unsqueeze(1).to_broadcast([16, 4, T // 4]),
         )
+        nc.gpsimd.memset(table_scales[0:32, :].bitcast(I32), 0)
+        nc.gpsimd.memset(table_scales[96:P, :].bitcast(I32), 0)
         nc.sync.dma_start(out=table_words[:].bitcast(I32), in_=x_words[0].rearrange("p c r -> p (c r)").bitcast(I32))
         load_weight(0)
         load_weight(1)
@@ -207,8 +212,9 @@ def tile_picked_trilin_none_p_kernel(
         round_scalar(0, 0, 4)
         place_codes(0, AT + 24 * KIB)
         quantize_weight(0, 0, 4)
-        for c in range(CHUNKS):
-            product(0, c)
+        product(0, 0)
+        first_factor(0, AT + 26 * KIB)
+        product(0, 1)
         place_rounded(1, 0, 2, AT + 10 * KIB)
         place_rounded(1, 2, 4, AT + 6 * KIB)
         round_scalar(1, 0, 2)
@@ -216,25 +222,29 @@ def tile_picked_trilin_none_p_kernel(
         place_codes(1, AT + 18 * KIB)
         quantize_weight(1, 0, 2)
         quantize_weight(1, 2, 4)
-        for c in (0, 1, 3):
-            product(1, c)
+        product(1, 0)
         place_rounded(2, 0, 4, AT + 14 * KIB)
-        round_scalar(2, 0, 2)
+        round_vector(2, 0, 2, P // 2, P)
         round_vector(2, 2, 4)
+        round_scalar(2, 0, 2, 0, P // 2)
+        second_factor(0, RAW_AT[2])
         place_codes(2, AT + 20 * KIB)
-        quantize_weight(2, 0, 4)
-        for c in (0, 1, 3):
-            first_factor(c, RAW_AT[2] + 2 * KIB * c)
-        second_factor(0)
-        second_factor(1)
+        quantize_weight(2, 2, 4)
+        quantize_weight(2, 0, 2)
+        first_factor(1, RAW_AT[2] + 2 * KIB)
+        product(1, 1)
+        product(0, 3)
+        first_factor(3, RAW_AT[2] + 6 * KIB)
+        product(1, 3)
+        second_factor(1, AT + 28 * KIB)
         second_factor_gpsimd(3, AT + 14 * KIB)
-        product(2, 0)
-        third_factor(0)
-        product(2, 1)
-        third_factor(1)
+        product(0, 2)
         first_factor(2, RAW_AT[2] + 4 * KIB)
+        for c in range(2):
+            product(2, c)
+            third_factor(c)
         product(1, 2)
-        second_factor(2)
+        second_factor(2, AT + 30 * KIB)
         quantize_z(0, 2, AT + 14 * KIB)
         product(2, 2)
         third_factor(2)

@@ -207,11 +207,15 @@ def tile_picked_trilin_none_p_kernel(
         move_scale_rows(2 * V, S)
         nc.sync.dma_start(out=last_words[:].bitcast(I32), in_=w4_words[0].bitcast(I32))
         load_scale_rows(last_scales, w4_scales)
-        gather_words(0, 12, AT)
-        place_rounded(0, 0, 4, AT + 6 * KIB)
-        round_scalar(0, 0, 4)
+        gather_words(0, 10, AT)
+        place_rounded(0, 0, 2, AT + 8 * KIB)
+        place_rounded(0, 2, 4, AT + 6 * KIB)
+        round_scalar(0, 0, 2)
+        round_scalar(0, 2, 4)
         place_codes(0, AT + 24 * KIB)
-        quantize_weight(0, 0, 4)
+        quantize_weight(0, 0, 2)
+        gather_words(10, 12, AT + 8 * KIB)
+        quantize_weight(0, 2, 4)
         product(0, 0)
         first_factor(0, AT + 26 * KIB)
         product(0, 1)
@@ -224,9 +228,8 @@ def tile_picked_trilin_none_p_kernel(
         quantize_weight(1, 2, 4)
         product(1, 0)
         place_rounded(2, 0, 4, AT + 14 * KIB)
-        round_vector(2, 0, 2, P // 2, P)
         round_vector(2, 2, 4)
-        round_scalar(2, 0, 2, 0, P // 2)
+        round_scalar(2, 0, 2)
         second_factor(0, RAW_AT[2])
         place_codes(2, AT + 20 * KIB)
         quantize_weight(2, 2, 4)

@@ -181,13 +181,13 @@ def tile_picked_trilin_none_p_kernel(
             copy(out=staged[:], in_=res[:])
             nc.sync.dma_start(out=out_view[:, :, c0 * CHUNK : c1 * CHUNK], in_=staged[:])
 
-        def finish_last(c):
-            for h, copy, queue in ((0, nc.scalar.copy, nc.scalar), (1, nc.vector.tensor_copy, nc.sync)):
+        def finish_split(c):
+            staged = keep.tile([P, HALVES, CHUNK], F32, name=f"staged{c}", align_bytes=64)
+            for h, copy in enumerate((nc.scalar.copy, nc.vector.tensor_copy)):
                 res = psum.tile([P, CHUNK], F32, name="res", tag="bank", bufs=6)
-                staged = keep.tile([P, CHUNK], F32, name=f"staged_last{h}", align_bytes=64)
                 last_product(res[:], h, c, c + 1)
-                copy(out=staged[:], in_=res[:])
-                queue.dma_start(out=out_view[:, h, c * CHUNK : (c + 1) * CHUNK], in_=staged[:])
+                copy(out=staged[:, h, :], in_=res[:])
+            nc.sync.dma_start(out=out_view[:, :, c * CHUNK : (c + 1) * CHUNK], in_=staged[:])
 
         nc.sync.dma_start(offsets[:], offs)
         nc.scalar.dma_start(
@@ -228,8 +228,9 @@ def tile_picked_trilin_none_p_kernel(
         quantize_weight(1, 2, 4)
         product(1, 0)
         place_rounded(2, 0, 4, AT + 14 * KIB)
+        round_vector(2, 0, 2, 3 * P // 4, P)
         round_vector(2, 2, 4)
-        round_scalar(2, 0, 2)
+        round_scalar(2, 0, 2, 0, 3 * P // 4)
         second_factor(0, RAW_AT[2])
         place_codes(2, AT + 20 * KIB)
         quantize_weight(2, 2, 4)
@@ -255,6 +256,6 @@ def tile_picked_trilin_none_p_kernel(
         finish(0, 2, nc.scalar.copy)
         third_factor(3)
         quantize_z(2, 3, AT + 22 * KIB)
-        finish(2, 3, nc.scalar.copy)
         quantize_z(3, 4, AT + 23 * KIB)
-        finish_last(3)
+        finish_split(2)
+        finish_split(3)

@@ -181,13 +181,13 @@ def tile_picked_trilin_none_p_kernel(
             copy(out=staged[:], in_=res[:])
             nc.sync.dma_start(out=out_view[:, :, c0 * CHUNK : c1 * CHUNK], in_=staged[:])
 
-        def finish_split(c):
-            staged = keep.tile([P, HALVES, CHUNK], F32, name=f"staged{c}", align_bytes=64)
-            for h, copy in enumerate((nc.scalar.copy, nc.vector.tensor_copy)):
+        def finish_last(c):
+            for h, copy, queue in ((0, nc.scalar.copy, nc.scalar), (1, nc.vector.tensor_copy, nc.sync)):
                 res = psum.tile([P, CHUNK], F32, name="res", tag="bank", bufs=6)
+                staged = keep.tile([P, CHUNK], F32, name=f"staged_last{h}", align_bytes=64)
                 last_product(res[:], h, c, c + 1)
-                copy(out=staged[:, h, :], in_=res[:])
-            nc.sync.dma_start(out=out_view[:, :, c * CHUNK : (c + 1) * CHUNK], in_=staged[:])
+                copy(out=staged[:], in_=res[:])
+                queue.dma_start(out=out_view[:, h, c * CHUNK : (c + 1) * CHUNK], in_=staged[:])
 
         nc.sync.dma_start(offsets[:], offs)
         nc.scalar.dma_start(
@@ -256,6 +256,6 @@ def tile_picked_trilin_none_p_kernel(
         finish(0, 2, nc.scalar.copy)
         third_factor(3)
         quantize_z(2, 3, AT + 22 * KIB)
+        finish(2, 3, nc.scalar.copy)
         quantize_z(3, 4, AT + 23 * KIB)
-        finish_split(2)
-        finish_split(3)
+        finish_last(3)

@@ -112,13 +112,14 @@ def tile_picked_trilin_none_p_kernel(
             for c in range(c0, c1):
                 x_codes[divmod(c, CHUNKS)] = codes[:, (c - c0) * CHUNK : (c - c0 + 1) * CHUNK]
 
-        def product(d, c):
-            if d == 0:
-                bank = psum.tile([P, PACK, CHUNK], F32, name="first_bank", bufs=2)
+        def product(d, c, t_first=0):
+            if (d, c) in ((0, 1), (0, 2)):
+                bank = psum.tile([P, PACK, CHUNK], F32, name="side_bank", bufs=1)
             else:
-                bank = psum.tile([P, PACK, CHUNK], F32, name="bank", bufs=6)
+                bank = psum.tile([P, PACK, CHUNK], F32, name="bank", bufs=7)
             cols = slice(d * V + c * CHUNK, d * V + (c + 1) * CHUNK)
-            for t in range(PACK):
+            for step in range(PACK):
+                t = (t_first + step) % PACK
                 chans = slice(t * P, (t + 1) * P)
                 nc.tensor.matmul_mx(
                     out=bank[:, t, :],
@@ -174,7 +175,7 @@ def tile_picked_trilin_none_p_kernel(
 
         def finish(c0, c1, copy):
             width = (c1 - c0) * CHUNK
-            res = psum.tile([P, HALVES, width], F32, name="res", tag="bank", bufs=6)
+            res = psum.tile([P, HALVES, width], F32, name="res", tag="bank", bufs=7)
             staged = keep.tile([P, HALVES, width], F32, name=f"staged{c0}", align_bytes=64)
             for h in range(HALVES):
                 last_product(res[:, h, :], h, c0, c1)
@@ -183,7 +184,7 @@ def tile_picked_trilin_none_p_kernel(
 
         def finish_last(c):
             for h, copy, queue in ((0, nc.scalar.copy, nc.scalar), (1, nc.vector.tensor_copy, nc.sync)):
-                res = psum.tile([P, CHUNK], F32, name="res", tag="bank", bufs=6)
+                res = psum.tile([P, CHUNK], F32, name="res", tag="bank", bufs=7)
                 staged = keep.tile([P, CHUNK], F32, name=f"staged_last{h}", align_bytes=64)
                 last_product(res[:], h, c, c + 1)
                 copy(out=staged[:], in_=res[:])
@@ -219,6 +220,7 @@ def tile_picked_trilin_none_p_kernel(
         product(0, 0)
         first_factor(0, AT + 26 * KIB)
         product(0, 1)
+        product(0, 3)
         place_rounded(1, 0, 2, AT + 10 * KIB)
         place_rounded(1, 2, 4, AT + 6 * KIB)
         round_scalar(1, 0, 2)
@@ -236,18 +238,17 @@ def tile_picked_trilin_none_p_kernel(
         quantize_weight(2, 2, 4)
         quantize_weight(2, 0, 2)
         first_factor(1, RAW_AT[2] + 2 * KIB)
-        product(1, 1)
-        product(0, 3)
+        product(1, 1, 2)
         first_factor(3, RAW_AT[2] + 6 * KIB)
-        product(1, 3)
-        second_factor(1, AT + 28 * KIB)
+        product(1, 3, 2)
+        second_factor(1, AT + 16 * KIB)
         second_factor_gpsimd(3, AT + 14 * KIB)
         product(0, 2)
         first_factor(2, RAW_AT[2] + 4 * KIB)
         for c in range(2):
-            product(2, c)
+            product(2, c, 2 if c == 0 else 0)
             third_factor(c)
-        product(1, 2)
+        product(1, 2, 2)
         second_factor(2, AT + 30 * KIB)
         quantize_z(0, 2, AT + 14 * KIB)
         product(2, 2)

@@ -14,7 +14,6 @@ U8 = mybir.dt.uint8
 FP8X4 = mybir.dt.float8_e4m3fn_x4
 FP4X4 = mybir.dt.float4_e2m1fn_x4
 MULT = mybir.AluOpType.mult
-ADD = mybir.AluOpType.add
 
 P = 128
 PACK = 4
@@ -22,6 +21,7 @@ PIECES = 3
 CHUNK = 128
 CHUNKS = V // CHUNK
 HALVES = N // P
+CUTS = (64, 64, 64)
 KIB = 1024
 
 
@@ -41,20 +41,29 @@ def tile_picked_trilin_none_p_kernel(
         table_scales = keep.tile([P, T], U8, name="table_scales", align_bytes=64)
         last_words = keep.tile([P, 2 * N], U8, name="last_words", align_bytes=64)
         last_scales = keep.tile([P, N], U8, name="last_scales", align_bytes=64)
-        w_codes = {}
         w_scales = [keep.tile([P, H], U8, name=f"w_scales{d}", align_bytes=64) for d in range(PIECES)]
+        rounded = [
+            [keep.tile([P, 2 * H], BF16, name=f"rounded{d}_{u}", align_bytes=64) for u in range(2)] for d in range(PIECES)
+        ]
         x_bytes = keep.tile([P, S], U8, name="x_bytes", align_bytes=64)
         picked_bytes = keep.tile([P, S], U8, name="picked_bytes", align_bytes=64)
+        z = keep.tile([P, V * PACK], BF16, name="z", align_bytes=64)
+        z_scales = keep.tile([P, V], U8, name="z_scales", align_bytes=64)
+        out_view = out.rearrange("(h m) v -> m h v", h=HALVES)
 
-        RAW_AT = [0, 8 * KIB, 16 * KIB]
-        AT = 24 * KIB
         raw = {}
-        rounded = {}
+        w_codes = {}
         x_codes = {}
         first = {}
         pair = {}
         banks = {}
         z_codes = {}
+
+        def raw_at(d, side):
+            return (2 + (2 * d + side) * 8) * KIB
+
+        def span(d, side):
+            return (0, CUTS[d]) if side == 0 else (CUTS[d], P)
 
         def load_scale_rows(plane, rows):
             for q in range(4):
@@ -63,6 +72,9 @@ def tile_picked_trilin_none_p_kernel(
                     in_=rows[0, 4 * q : 4 * q + 4, :].bitcast(I32).partition_broadcast(8),
                 )
 
+        def gather_bytes(lo, hi):
+            nc.vector.tensor_copy(out=picked_bytes[:, lo:hi], in_=table_scales[:].indirect(offsets[:, lo // 16 : hi // 16]))
+
         def move_scale_rows(lo, hi):
             for q in (0, 2, 1, 3):
                 nc.sync.dma_start(
@@ -70,40 +82,23 @@ def tile_picked_trilin_none_p_kernel(
                     in_=picked_bytes[32 + 16 * q : 48 + 16 * q : 4, lo:hi].bitcast(I32),
                 )
 
-        def load_weight(d):
-            raw[d] = shared.tile([P, PACK, H], F32, name=f"raw{d}", align_bytes=64, offset=RAW_AT[d])
-            nc.sync.dma_start(out=raw[d][:], in_=weights[d].rearrange("(p j) c -> p j c", j=PACK))
-
-        def place_rounded(d, t0, t1, at):
-            tile = shared.tile([P, (t1 - t0) * H], BF16, name=f"rounded{d}_{t0}", align_bytes=64, offset=at)
-            for t in range(t0, t1):
-                rounded[d, t] = (tile, t0)
-
-        def rounded_part(d, t0, t1):
-            tile, base = rounded[d, t0]
-            return tile[:, (t0 - base) * H : (t1 - base) * H]
-
-        def round_views(d, t0, t1, m0, m1):
-            src = raw[d][:].rearrange("p j (m t) -> p m j t", t=PACK)[:, m0:m1, :, t0:t1]
-            dst = rounded_part(d, t0, t1).rearrange("p (t m j) -> p m j t", m=P, j=PACK)[:, m0:m1]
-            return dst, src
-
-        def round_scalar(d, t0, t1, m0=0, m1=P):
-            dst, src = round_views(d, t0, t1, m0, m1)
-            nc.scalar.copy(out=dst, in_=src)
-
-        def round_vector(d, t0, t1, m0=0, m1=P):
-            dst, src = round_views(d, t0, t1, m0, m1)
-            nc.vector.tensor_copy(out=dst, in_=src)
-
-        def place_codes(d, at):
-            w_codes[d] = shared.tile([P, H], U32, name=f"w_codes{d}", align_bytes=64, offset=at)
-
-        def quantize_weight(d, t0, t1):
-            cols = slice(P * t0, P * t1)
-            nc.vector.quantize_mx(
-                out=w_codes[d][:, cols].bitcast(FP8X4), scales=w_scales[d][:, cols], in_=rounded_part(d, t0, t1)
+        def load_weight(d, side):
+            m0, m1 = span(d, side)
+            raw[d, side] = shared.tile(
+                [P, PACK, PACK * (m1 - m0)], F32, name=f"raw{d}_{side}", align_bytes=64, offset=raw_at(d, side)
             )
+            rows = weights[d].rearrange("(p j) c -> p j c", j=PACK)
+            nc.sync.dma_start(out=raw[d, side][:], in_=rows[:, :, PACK * m0 : PACK * m1])
+
+        def round_weight(copy, d, side, u):
+            src = raw[d, side][:].rearrange("p j (m t) -> p m j t", t=PACK)[:, :, :, 2 * u : 2 * u + 2]
+            dst = rounded[d][u][:].rearrange("p (t m j) -> p m j t", m=P, j=PACK)[:, slice(*span(d, side))]
+            copy(out=dst, in_=src)
+
+        def quantize_weight(d, u, at):
+            cols = slice(2 * P * u, 2 * P * (u + 1))
+            w_codes[d, u] = shared.tile([P, 2 * P], U32, name=f"w_codes{d}_{u}", align_bytes=64, offset=at)
+            nc.vector.quantize_mx(out=w_codes[d, u][:].bitcast(FP8X4), scales=w_scales[d][:, cols], in_=rounded[d][u][:])
 
         def gather_words(c0, c1, at):
             codes = shared.tile([P, (c1 - c0) * CHUNK], U32, name=f"x_codes{c0}", align_bytes=64, offset=at)
@@ -112,18 +107,18 @@ def tile_picked_trilin_none_p_kernel(
             for c in range(c0, c1):
                 x_codes[divmod(c, CHUNKS)] = codes[:, (c - c0) * CHUNK : (c - c0 + 1) * CHUNK]
 
-        def product(d, c, t_first=0):
-            if (d, c) in ((0, 1), (0, 2)):
-                bank = psum.tile([P, PACK, CHUNK], F32, name="side_bank", bufs=1)
-            else:
-                bank = psum.tile([P, PACK, CHUNK], F32, name="bank", bufs=7)
+        def bank_tile(shape, b):
+            return psum.tile(shape, F32, name=f"bank{b}", tag=f"bank{b}", bufs=1)
+
+        def product(d, c, b):
+            bank = bank_tile([P, PACK, CHUNK], b)
             cols = slice(d * V + c * CHUNK, d * V + (c + 1) * CHUNK)
             for step in range(PACK):
-                t = (t_first + step) % PACK
+                t = step if c == 0 else (2 + step) % PACK
                 chans = slice(t * P, (t + 1) * P)
                 nc.tensor.matmul_mx(
                     out=bank[:, t, :],
-                    lhsT=w_codes[d][:, chans].bitcast(FP8X4),
+                    lhsT=w_codes[d, t // 2][:, t % 2 * P : (t % 2 + 1) * P].bitcast(FP8X4),
                     lhsT_scale=w_scales[d][:, chans],
                     rhs=x_codes[d, c].bitcast(FP8X4),
                     rhs_scale=x_bytes[:, cols],
@@ -132,16 +127,12 @@ def tile_picked_trilin_none_p_kernel(
                 )
             banks[d, c] = bank[:].rearrange("p t v -> p v t")
 
-        out_view = out.rearrange("(h m) v -> m h v", h=HALVES)
-        z = keep.tile([P, V * PACK], BF16, name="z", align_bytes=64)
-        z_scales = keep.tile([P, V], U8, name="z_scales", align_bytes=64)
-
         def first_factor(c, at):
             first[c] = shared.tile([P, CHUNK, PACK], F32, name=f"first{c}", align_bytes=64, offset=at)
             nc.scalar.copy(out=first[c][:], in_=banks[0, c])
 
-        def second_factor_gpsimd(c, at):
-            second = shared.tile([P, CHUNK, PACK], F32, name="second", align_bytes=64, offset=at)
+        def second_factor_gpsimd(c):
+            second = shared.tile([P, CHUNK, PACK], F32, name="second", align_bytes=64, offset=raw_at(2, 0) + 7 * KIB // 2)
             pair[c] = keep.tile([P, CHUNK, PACK], F32, name=f"pair{c}", align_bytes=64)
             nc.scalar.copy(out=second[:], in_=banks[1, c])
             nc.gpsimd.tensor_tensor(out=pair[c][:], in0=second[:], in1=first[c][:], op=MULT)
@@ -154,8 +145,8 @@ def tile_picked_trilin_none_p_kernel(
             part = z[:, c * CHUNK * PACK : (c + 1) * CHUNK * PACK].rearrange("p (v t) -> p v t", t=PACK)
             nc.vector.tensor_tensor(out=part, in0=banks[2, c], in1=pair[c][:], op=MULT)
 
-        def quantize_z(c0, c1, at):
-            z_codes[c0] = shared.tile([P, (c1 - c0) * CHUNK], U32, name=f"z_codes{c0}", align_bytes=64, offset=at)
+        def quantize_z(c0, c1):
+            z_codes[c0] = keep.tile([P, (c1 - c0) * CHUNK], U32, name=f"z_codes{c0}", align_bytes=64)
             nc.vector.quantize_mx(
                 out=z_codes[c0][:].bitcast(FP8X4),
                 scales=z_scales[:, c0 * CHUNK : c1 * CHUNK],
@@ -173,22 +164,24 @@ def tile_picked_trilin_none_p_kernel(
                 stop=True,
             )
 
-        def finish(c0, c1, copy):
+        def finish(c0, c1, b):
             width = (c1 - c0) * CHUNK
-            res = psum.tile([P, HALVES, width], F32, name="res", tag="bank", bufs=7)
+            res = bank_tile([P, HALVES, width], b)
             staged = keep.tile([P, HALVES, width], F32, name=f"staged{c0}", align_bytes=64)
             for h in range(HALVES):
                 last_product(res[:, h, :], h, c0, c1)
-            copy(out=staged[:], in_=res[:])
+            nc.scalar.copy(out=staged[:], in_=res[:])
             nc.sync.dma_start(out=out_view[:, :, c0 * CHUNK : c1 * CHUNK], in_=staged[:])
 
         def finish_last(c):
-            for h, copy, queue in ((0, nc.scalar.copy, nc.scalar), (1, nc.vector.tensor_copy, nc.sync)):
-                res = psum.tile([P, CHUNK], F32, name="res", tag="bank", bufs=7)
+            for h, copy, queue, b in ((0, nc.scalar.copy, nc.scalar, 2), (1, nc.vector.tensor_copy, nc.sync, 0)):
+                res = bank_tile([P, CHUNK], b)
                 staged = keep.tile([P, CHUNK], F32, name=f"staged_last{h}", align_bytes=64)
                 last_product(res[:], h, c, c + 1)
                 copy(out=staged[:], in_=res[:])
                 queue.dma_start(out=out_view[:, h, c * CHUNK : (c + 1) * CHUNK], in_=staged[:])
+
+        on_scalar, on_vector = nc.scalar.copy, nc.vector.tensor_copy
 
         nc.sync.dma_start(offsets[:], offs)
         nc.scalar.dma_start(
@@ -197,66 +190,68 @@ def tile_picked_trilin_none_p_kernel(
         )
         nc.gpsimd.memset(table_scales[0:32, :].bitcast(I32), 0)
         nc.gpsimd.memset(table_scales[96:P, :].bitcast(I32), 0)
-        nc.sync.dma_start(out=table_words[:].bitcast(I32), in_=x_words[0].rearrange("p c r -> p (c r)").bitcast(I32))
-        load_weight(0)
-        load_weight(1)
-
         nc.gpsimd.memset(x_bytes[:].bitcast(I32), 0)
-        nc.vector.tensor_copy(out=picked_bytes[:], in_=table_scales[:].indirect(offsets[:]))
+        load_weight(0, 0)
+        nc.sync.dma_start(out=table_words[:].bitcast(I32), in_=x_words[0].rearrange("p c r -> p (c r)").bitcast(I32))
+        load_weight(0, 1)
+        load_weight(1, 0)
+        load_weight(1, 1)
+        gather_bytes(0, S)
         move_scale_rows(0, 2 * V)
-        load_weight(2)
+        load_weight(2, 0)
+        load_weight(2, 1)
         move_scale_rows(2 * V, S)
         nc.sync.dma_start(out=last_words[:].bitcast(I32), in_=w4_words[0].bitcast(I32))
         load_scale_rows(last_scales, w4_scales)
-        gather_words(0, 10, AT)
-        place_rounded(0, 0, 2, AT + 8 * KIB)
-        place_rounded(0, 2, 4, AT + 6 * KIB)
-        round_scalar(0, 0, 2)
-        round_scalar(0, 2, 4)
-        place_codes(0, AT + 24 * KIB)
-        quantize_weight(0, 0, 2)
-        gather_words(10, 12, AT + 8 * KIB)
-        quantize_weight(0, 2, 4)
-        product(0, 0)
-        first_factor(0, AT + 26 * KIB)
-        product(0, 1)
-        product(0, 3)
-        place_rounded(1, 0, 2, AT + 10 * KIB)
-        place_rounded(1, 2, 4, AT + 6 * KIB)
-        round_scalar(1, 0, 2)
-        round_vector(1, 2, 4)
-        place_codes(1, AT + 18 * KIB)
-        quantize_weight(1, 0, 2)
-        quantize_weight(1, 2, 4)
-        product(1, 0)
-        place_rounded(2, 0, 4, AT + 14 * KIB)
-        round_vector(2, 0, 2, 3 * P // 4, P)
-        round_vector(2, 2, 4)
-        round_scalar(2, 0, 2, 0, 3 * P // 4)
-        second_factor(0, RAW_AT[2])
-        place_codes(2, AT + 20 * KIB)
-        quantize_weight(2, 2, 4)
-        quantize_weight(2, 0, 2)
-        first_factor(1, RAW_AT[2] + 2 * KIB)
-        product(1, 1, 2)
-        first_factor(3, RAW_AT[2] + 6 * KIB)
-        product(1, 3, 2)
-        second_factor(1, AT + 16 * KIB)
-        second_factor_gpsimd(3, AT + 14 * KIB)
-        product(0, 2)
-        first_factor(2, RAW_AT[2] + 4 * KIB)
-        for c in range(2):
-            product(2, c, 2 if c == 0 else 0)
-            third_factor(c)
-        product(1, 2, 2)
-        second_factor(2, AT + 30 * KIB)
-        quantize_z(0, 2, AT + 14 * KIB)
-        product(2, 2)
+
+        free = 52 * KIB
+        gather_words(0, 6, free)
+        for side in range(2):
+            for u in range(2):
+                round_weight(on_scalar, 0, side, u)
+        quantize_weight(0, 0, free + 3 * KIB)
+        quantize_weight(0, 1, free + 4 * KIB)
+        gather_words(6, 10, raw_at(0, 1))
+        round_weight(on_scalar, 1, 0, 0)
+        round_weight(on_scalar, 1, 0, 1)
+        round_weight(on_scalar, 1, 1, 0)
+        round_weight(on_vector, 1, 1, 1)
+        quantize_weight(1, 0, free + 5 * KIB)
+        quantize_weight(1, 1, raw_at(1, 1) + KIB)
+        gather_words(10, 12, raw_at(1, 1))
+        product(0, 0, 0)
+        first_factor(0, free + 8 * KIB)
+        product(0, 1, 1)
+        round_weight(on_scalar, 2, 0, 0)
+        round_weight(on_scalar, 2, 0, 1)
+        product(1, 0, 2)
+        second_factor(0, free + 12 * KIB)
+        product(1, 1, 3)
+        product(0, 3, 4)
+        product(1, 3, 5)
+        product(0, 2, 2)
+        round_weight(on_vector, 2, 1, 0)
+        round_weight(on_vector, 2, 1, 1)
+        quantize_weight(2, 0, raw_at(2, 0) + KIB // 2)
+        quantize_weight(2, 1, free + 6 * KIB)
+        first_factor(1, raw_at(2, 0) - 3 * KIB // 2)
+        second_factor(1, raw_at(2, 1))
+        first_factor(3, raw_at(2, 0) + 3 * KIB // 2)
+        second_factor_gpsimd(3)
+        first_factor(2, raw_at(2, 1) + 2 * KIB)
+        product(1, 2, 1)
+        product(2, 0, 0)
+        third_factor(0)
+        product(2, 1, 4)
+        third_factor(1)
+        second_factor(2, free + 12 * KIB)
+        product(2, 2, 6)
+        product(2, 3, 7)
+        quantize_z(0, 2)
+        finish(0, 2, 3)
         third_factor(2)
-        product(2, 3)
-        finish(0, 2, nc.scalar.copy)
         third_factor(3)
-        quantize_z(2, 3, AT + 22 * KIB)
-        finish(2, 3, nc.scalar.copy)
-        quantize_z(3, 4, AT + 23 * KIB)
+        quantize_z(2, 3)
+        finish(2, 3, 5)
+        quantize_z(3, 4)
         finish_last(3)

@@ -21,7 +21,6 @@ PIECES = 3
 CHUNK = 128
 CHUNKS = V // CHUNK
 HALVES = N // P
-CUTS = (64, 64, 64)
 KIB = 1024
 
 
@@ -42,9 +41,6 @@ def tile_picked_trilin_none_p_kernel(
         last_words = keep.tile([P, 2 * N], U8, name="last_words", align_bytes=64)
         last_scales = keep.tile([P, N], U8, name="last_scales", align_bytes=64)
         w_scales = [keep.tile([P, H], U8, name=f"w_scales{d}", align_bytes=64) for d in range(PIECES)]
-        rounded = [
-            [keep.tile([P, 2 * H], BF16, name=f"rounded{d}_{u}", align_bytes=64) for u in range(2)] for d in range(PIECES)
-        ]
         x_bytes = keep.tile([P, S], U8, name="x_bytes", align_bytes=64)
         picked_bytes = keep.tile([P, S], U8, name="picked_bytes", align_bytes=64)
         z = keep.tile([P, V * PACK], BF16, name="z", align_bytes=64)
@@ -52,6 +48,7 @@ def tile_picked_trilin_none_p_kernel(
         out_view = out.rearrange("(h m) v -> m h v", h=HALVES)
 
         raw = {}
+        rounded = {}
         w_codes = {}
         x_codes = {}
         first = {}
@@ -59,11 +56,8 @@ def tile_picked_trilin_none_p_kernel(
         banks = {}
         z_codes = {}
 
-        def raw_at(d, side):
-            return (2 + (2 * d + side) * 8) * KIB
-
-        def span(d, side):
-            return (0, CUTS[d]) if side == 0 else (CUTS[d], P)
+        def raw_at(d):
+            return 8 * d * KIB
 
         def load_scale_rows(plane, rows):
             for q in range(4):
@@ -82,23 +76,22 @@ def tile_picked_trilin_none_p_kernel(
                     in_=picked_bytes[32 + 16 * q : 48 + 16 * q : 4, lo:hi].bitcast(I32),
                 )
 
-        def load_weight(d, side):
-            m0, m1 = span(d, side)
-            raw[d, side] = shared.tile(
-                [P, PACK, PACK * (m1 - m0)], F32, name=f"raw{d}_{side}", align_bytes=64, offset=raw_at(d, side)
-            )
-            rows = weights[d].rearrange("(p j) c -> p j c", j=PACK)
-            nc.sync.dma_start(out=raw[d, side][:], in_=rows[:, :, PACK * m0 : PACK * m1])
+        def load_weight(d):
+            raw[d] = shared.tile([P, PACK, H], F32, name=f"raw{d}", align_bytes=64, offset=raw_at(d))
+            nc.sync.dma_start(out=raw[d][:], in_=weights[d].rearrange("(p j) c -> p j c", j=PACK))
 
-        def round_weight(copy, d, side, u):
-            src = raw[d, side][:].rearrange("p j (m t) -> p m j t", t=PACK)[:, :, :, 2 * u : 2 * u + 2]
-            dst = rounded[d][u][:].rearrange("p (t m j) -> p m j t", m=P, j=PACK)[:, slice(*span(d, side))]
-            copy(out=dst, in_=src)
+        def place_rounded(d, u, at):
+            rounded[d, u] = shared.tile([P, 2 * H], BF16, name=f"rounded{d}_{u}", align_bytes=64, offset=at)
+
+        def round_weight(copy, d, u, m0=0, m1=P, walk="p m j t"):
+            src = raw[d][:].rearrange("p j (m t) -> p m j t", t=PACK)[:, m0:m1, :, 2 * u : 2 * u + 2]
+            dst = rounded[d, u][:].rearrange("p (t m j) -> p m j t", m=P, j=PACK)[:, m0:m1]
+            copy(out=dst.rearrange(f"p m j t -> {walk}"), in_=src.rearrange(f"p m j t -> {walk}"))
 
         def quantize_weight(d, u, at):
             cols = slice(2 * P * u, 2 * P * (u + 1))
             w_codes[d, u] = shared.tile([P, 2 * P], U32, name=f"w_codes{d}_{u}", align_bytes=64, offset=at)
-            nc.vector.quantize_mx(out=w_codes[d, u][:].bitcast(FP8X4), scales=w_scales[d][:, cols], in_=rounded[d][u][:])
+            nc.vector.quantize_mx(out=w_codes[d, u][:].bitcast(FP8X4), scales=w_scales[d][:, cols], in_=rounded[d, u][:])
 
         def gather_words(c0, c1, at):
             codes = shared.tile([P, (c1 - c0) * CHUNK], U32, name=f"x_codes{c0}", align_bytes=64, offset=at)
@@ -110,11 +103,11 @@ def tile_picked_trilin_none_p_kernel(
         def bank_tile(shape, b):
             return psum.tile(shape, F32, name=f"bank{b}", tag=f"bank{b}", bufs=1)
 
-        def product(d, c, b):
+        def product(d, c, b, t_first=0):
             bank = bank_tile([P, PACK, CHUNK], b)
             cols = slice(d * V + c * CHUNK, d * V + (c + 1) * CHUNK)
             for step in range(PACK):
-                t = step if c == 0 else (2 + step) % PACK
+                t = (t_first + step) % PACK
                 chans = slice(t * P, (t + 1) * P)
                 nc.tensor.matmul_mx(
                     out=bank[:, t, :],
@@ -132,7 +125,7 @@ def tile_picked_trilin_none_p_kernel(
             nc.scalar.copy(out=first[c][:], in_=banks[0, c])
 
         def second_factor_gpsimd(c):
-            second = shared.tile([P, CHUNK, PACK], F32, name="second", align_bytes=64, offset=raw_at(2, 0) + 7 * KIB // 2)
+            second = shared.tile([P, CHUNK, PACK], F32, name="second", align_bytes=64, offset=raw_at(2) + 4 * KIB)
             pair[c] = keep.tile([P, CHUNK, PACK], F32, name=f"pair{c}", align_bytes=64)
             nc.scalar.copy(out=second[:], in_=banks[1, c])
             nc.gpsimd.tensor_tensor(out=pair[c][:], in0=second[:], in1=first[c][:], op=MULT)
@@ -174,7 +167,7 @@ def tile_picked_trilin_none_p_kernel(
             nc.sync.dma_start(out=out_view[:, :, c0 * CHUNK : c1 * CHUNK], in_=staged[:])
 
         def finish_last(c):
-            for h, copy, queue, b in ((0, nc.scalar.copy, nc.scalar, 2), (1, nc.vector.tensor_copy, nc.sync, 0)):
+            for h, copy, queue, b in ((0, nc.scalar.copy, nc.scalar, 2), (1, nc.vector.tensor_copy, nc.sync, 5)):
                 res = bank_tile([P, CHUNK], b)
                 staged = keep.tile([P, CHUNK], F32, name=f"staged_last{h}", align_bytes=64)
                 last_product(res[:], h, c, c + 1)
@@ -191,67 +184,65 @@ def tile_picked_trilin_none_p_kernel(
         nc.gpsimd.memset(table_scales[0:32, :].bitcast(I32), 0)
         nc.gpsimd.memset(table_scales[96:P, :].bitcast(I32), 0)
         nc.gpsimd.memset(x_bytes[:].bitcast(I32), 0)
-        load_weight(0, 0)
         nc.sync.dma_start(out=table_words[:].bitcast(I32), in_=x_words[0].rearrange("p c r -> p (c r)").bitcast(I32))
-        load_weight(0, 1)
-        load_weight(1, 0)
-        load_weight(1, 1)
+        load_weight(0)
+        load_weight(1)
         gather_bytes(0, S)
         move_scale_rows(0, 2 * V)
-        load_weight(2, 0)
-        load_weight(2, 1)
+        load_weight(2)
         move_scale_rows(2 * V, S)
         nc.sync.dma_start(out=last_words[:].bitcast(I32), in_=w4_words[0].bitcast(I32))
         load_scale_rows(last_scales, w4_scales)
 
-        free = 52 * KIB
-        gather_words(0, 6, free)
-        for side in range(2):
-            for u in range(2):
-                round_weight(on_scalar, 0, side, u)
-        quantize_weight(0, 0, free + 3 * KIB)
-        quantize_weight(0, 1, free + 4 * KIB)
-        gather_words(6, 10, raw_at(0, 1))
-        round_weight(on_scalar, 1, 0, 0)
-        round_weight(on_scalar, 1, 0, 1)
-        round_weight(on_scalar, 1, 1, 0)
-        round_weight(on_vector, 1, 1, 1)
-        quantize_weight(1, 0, free + 5 * KIB)
-        quantize_weight(1, 1, raw_at(1, 1) + KIB)
-        gather_words(10, 12, raw_at(1, 1))
+        free = 24 * KIB
+        gather_words(0, 10, free)
+        place_rounded(0, 0, free + 6 * KIB)
+        place_rounded(0, 1, free + 8 * KIB)
+        round_weight(nc.gpsimd.tensor_copy, 0, 1, P // 2, P, "p t m j")
+        round_weight(on_scalar, 0, 0)
+        round_weight(on_scalar, 0, 1, 0, P // 2)
+        quantize_weight(0, 0, free + 10 * KIB)
+        quantize_weight(0, 1, free + 11 * KIB)
+        place_rounded(1, 0, free + 12 * KIB)
+        place_rounded(1, 1, raw_at(0))
+        round_weight(on_scalar, 1, 0)
+        round_weight(on_vector, 1, 1)
+        quantize_weight(1, 1, free + 14 * KIB)
+        quantize_weight(1, 0, free + 15 * KIB)
+        gather_words(10, 12, raw_at(1))
         product(0, 0, 0)
-        first_factor(0, free + 8 * KIB)
+        first_factor(0, free + 16 * KIB)
         product(0, 1, 1)
-        round_weight(on_scalar, 2, 0, 0)
-        round_weight(on_scalar, 2, 0, 1)
-        product(1, 0, 2)
-        second_factor(0, free + 12 * KIB)
+        first_factor(1, free + 18 * KIB)
+        product(1, 0, 2, 2)
+        second_factor(0, free + 20 * KIB)
         product(1, 1, 3)
         product(0, 3, 4)
         product(1, 3, 5)
+        product(1, 2, 6)
         product(0, 2, 2)
-        round_weight(on_vector, 2, 1, 0)
-        round_weight(on_vector, 2, 1, 1)
-        quantize_weight(2, 0, raw_at(2, 0) + KIB // 2)
-        quantize_weight(2, 1, free + 6 * KIB)
-        first_factor(1, raw_at(2, 0) - 3 * KIB // 2)
-        second_factor(1, raw_at(2, 1))
-        first_factor(3, raw_at(2, 0) + 3 * KIB // 2)
+        place_rounded(2, 0, free + 22 * KIB)
+        place_rounded(2, 1, free + 24 * KIB)
+        round_weight(on_scalar, 2, 0)
+        round_weight(on_vector, 2, 1)
+        quantize_weight(2, 1, free + 26 * KIB)
+        quantize_weight(2, 0, free + 27 * KIB)
+        second_factor(1, raw_at(2))
+        first_factor(3, raw_at(2) + 2 * KIB)
         second_factor_gpsimd(3)
-        first_factor(2, raw_at(2, 1) + 2 * KIB)
-        product(1, 2, 1)
-        product(2, 0, 0)
+        first_factor(2, raw_at(2) + 6 * KIB)
+        product(2, 0, 0, 2)
         third_factor(0)
-        product(2, 1, 4)
+        product(2, 1, 1)
         third_factor(1)
-        second_factor(2, free + 12 * KIB)
-        product(2, 2, 6)
-        product(2, 3, 7)
+        second_factor(2, free + 20 * KIB)
+        product(2, 2, 0)
+        product(2, 3, 1)
         quantize_z(0, 2)
         finish(0, 2, 3)
         third_factor(2)
         third_factor(3)
         quantize_z(2, 3)
-        finish(2, 3, 5)
+        finish(2, 3, 4)
         quantize_z(3, 4)
         finish_last(3)

@@ -80,18 +80,27 @@ def tile_picked_trilin_none_p_kernel(
             raw[d] = shared.tile([P, PACK, H], F32, name=f"raw{d}", align_bytes=64, offset=raw_at(d))
             nc.sync.dma_start(out=raw[d][:], in_=weights[d].rearrange("(p j) c -> p j c", j=PACK))
 
-        def place_rounded(d, u, at):
-            rounded[d, u] = shared.tile([P, 2 * H], BF16, name=f"rounded{d}_{u}", align_bytes=64, offset=at)
+        def place_rounded(d, t0, t1, at):
+            tile = shared.tile([P, (t1 - t0) * H], BF16, name=f"rounded{d}_{t0}", align_bytes=64, offset=at)
+            for t in range(t0, t1):
+                rounded[d, t] = (tile, t0)
 
-        def round_weight(copy, d, u, m0=0, m1=P, walk="p m j t"):
-            src = raw[d][:].rearrange("p j (m t) -> p m j t", t=PACK)[:, m0:m1, :, 2 * u : 2 * u + 2]
-            dst = rounded[d, u][:].rearrange("p (t m j) -> p m j t", m=P, j=PACK)[:, m0:m1]
+        def rounded_part(d, t0, t1):
+            tile, base = rounded[d, t0]
+            return tile[:, (t0 - base) * H : (t1 - base) * H]
+
+        def round_weight(copy, d, t0, t1, m0=0, m1=P, walk="p m j t"):
+            src = raw[d][:].rearrange("p j (m t) -> p m j t", t=PACK)[:, m0:m1, :, t0:t1]
+            dst = rounded_part(d, t0, t1).rearrange("p (t m j) -> p m j t", m=P, j=PACK)[:, m0:m1]
             copy(out=dst.rearrange(f"p m j t -> {walk}"), in_=src.rearrange(f"p m j t -> {walk}"))
 
-        def quantize_weight(d, u, at):
-            cols = slice(2 * P * u, 2 * P * (u + 1))
-            w_codes[d, u] = shared.tile([P, 2 * P], U32, name=f"w_codes{d}_{u}", align_bytes=64, offset=at)
-            nc.vector.quantize_mx(out=w_codes[d, u][:].bitcast(FP8X4), scales=w_scales[d][:, cols], in_=rounded[d, u][:])
+        def quantize_weight(d, t0, t1, at):
+            codes = shared.tile([P, (t1 - t0) * P], U32, name=f"w_codes{d}_{t0}", align_bytes=64, offset=at)
+            nc.vector.quantize_mx(
+                out=codes[:].bitcast(FP8X4), scales=w_scales[d][:, t0 * P : t1 * P], in_=rounded_part(d, t0, t1)
+            )
+            for t in range(t0, t1):
+                w_codes[d, t] = codes[:, (t - t0) * P : (t - t0 + 1) * P]
 
         def gather_words(c0, c1, at):
             codes = shared.tile([P, (c1 - c0) * CHUNK], U32, name=f"x_codes{c0}", align_bytes=64, offset=at)
@@ -111,7 +120,7 @@ def tile_picked_trilin_none_p_kernel(
                 chans = slice(t * P, (t + 1) * P)
                 nc.tensor.matmul_mx(
                     out=bank[:, t, :],
-                    lhsT=w_codes[d, t // 2][:, t % 2 * P : (t % 2 + 1) * P].bitcast(FP8X4),
+                    lhsT=w_codes[d, t].bitcast(FP8X4),
                     lhsT_scale=w_scales[d][:, chans],
                     rhs=x_codes[d, c].bitcast(FP8X4),
                     rhs_scale=x_bytes[:, cols],
@@ -167,7 +176,7 @@ def tile_picked_trilin_none_p_kernel(
             nc.sync.dma_start(out=out_view[:, :, c0 * CHUNK : c1 * CHUNK], in_=staged[:])
 
         def finish_last(c):
-            for h, copy, queue, b in ((0, nc.scalar.copy, nc.scalar, 2), (1, nc.vector.tensor_copy, nc.sync, 5)):
+            for h, copy, queue, b in ((0, nc.scalar.copy, nc.scalar, 6), (1, nc.vector.tensor_copy, nc.sync, 0)):
                 res = bank_tile([P, CHUNK], b)
                 staged = keep.tile([P, CHUNK], F32, name=f"staged_last{h}", align_bytes=64)
                 last_product(res[:], h, c, c + 1)
@@ -195,54 +204,50 @@ def tile_picked_trilin_none_p_kernel(
         load_scale_rows(last_scales, w4_scales)
 
         free = 24 * KIB
-        gather_words(0, 10, free)
-        place_rounded(0, 0, free + 6 * KIB)
-        place_rounded(0, 1, free + 8 * KIB)
-        round_weight(nc.gpsimd.tensor_copy, 0, 1, P // 2, P, "p t m j")
-        round_weight(on_scalar, 0, 0)
-        round_weight(on_scalar, 0, 1, 0, P // 2)
-        quantize_weight(0, 0, free + 10 * KIB)
-        quantize_weight(0, 1, free + 11 * KIB)
-        place_rounded(1, 0, free + 12 * KIB)
-        place_rounded(1, 1, raw_at(0))
-        round_weight(on_scalar, 1, 0)
-        round_weight(on_vector, 1, 1)
-        quantize_weight(1, 1, free + 14 * KIB)
-        quantize_weight(1, 0, free + 15 * KIB)
-        gather_words(10, 12, raw_at(1))
+        gather_words(0, 9, free)
+        place_rounded(0, 0, 4, free + 6 * KIB)
+        round_weight(nc.gpsimd.tensor_copy, 0, 2, 4, P // 2, P, "p t m j")
+        round_weight(on_scalar, 0, 0, 2)
+        round_weight(on_scalar, 0, 2, 4, 0, P // 2)
+        quantize_weight(0, 0, 4, free + 10 * KIB)
+        place_rounded(1, 0, 4, raw_at(0) + 4 * KIB)
+        round_weight(on_scalar, 1, 0, 2)
+        round_weight(on_vector, 1, 2, 4)
+        gather_words(9, 12, raw_at(0))
+        quantize_weight(1, 0, 4, raw_at(1))
         product(0, 0, 0)
         first_factor(0, free + 16 * KIB)
         product(0, 1, 1)
-        first_factor(1, free + 18 * KIB)
         product(1, 0, 2, 2)
-        second_factor(0, free + 20 * KIB)
         product(1, 1, 3)
         product(0, 3, 4)
         product(1, 3, 5)
-        product(1, 2, 6)
-        product(0, 2, 2)
-        place_rounded(2, 0, free + 22 * KIB)
-        place_rounded(2, 1, free + 24 * KIB)
-        round_weight(on_scalar, 2, 0)
-        round_weight(on_vector, 2, 1)
-        quantize_weight(2, 1, free + 26 * KIB)
-        quantize_weight(2, 0, free + 27 * KIB)
-        second_factor(1, raw_at(2))
+        product(0, 2, 6)
+        product(1, 2, 7)
+        place_rounded(2, 0, 2, free + 22 * KIB)
+        place_rounded(2, 2, 4, free + 24 * KIB)
+        round_weight(on_vector, 2, 2, 4)
+        round_weight(on_scalar, 2, 0, 2)
+        quantize_weight(2, 2, 4, free + 26 * KIB)
+        second_factor(0, raw_at(2))
+        first_factor(1, raw_at(2) + 6 * KIB)
+        quantize_weight(2, 0, 2, free + 27 * KIB)
+        second_factor(1, free + 28 * KIB)
         first_factor(3, raw_at(2) + 2 * KIB)
         second_factor_gpsimd(3)
-        first_factor(2, raw_at(2) + 6 * KIB)
+        first_factor(2, free + 16 * KIB)
         product(2, 0, 0, 2)
         third_factor(0)
         product(2, 1, 1)
         third_factor(1)
-        second_factor(2, free + 20 * KIB)
-        product(2, 2, 0)
-        product(2, 3, 1)
+        second_factor(2, raw_at(2))
+        product(2, 2, 2)
+        product(2, 3, 3)
         quantize_z(0, 2)
-        finish(0, 2, 3)
+        finish(0, 2, 4)
         third_factor(2)
         third_factor(3)
         quantize_z(2, 3)
-        finish(2, 3, 4)
+        finish(2, 3, 5)
         quantize_z(3, 4)
         finish_last(3)

@@ -197,9 +197,9 @@ def tile_picked_trilin_none_p_kernel(
         load_weight(0)
         load_weight(1)
         gather_bytes(0, S)
-        move_scale_rows(0, 2 * V)
+        move_scale_rows(0, 2 * CHUNK)
         load_weight(2)
-        move_scale_rows(2 * V, S)
+        move_scale_rows(2 * CHUNK, S)
         nc.sync.dma_start(out=last_words[:].bitcast(I32), in_=w4_words[0].bitcast(I32))
         load_scale_rows(last_scales, w4_scales)
 
@@ -218,29 +218,29 @@ def tile_picked_trilin_none_p_kernel(
         product(0, 0, 0)
         first_factor(0, free + 16 * KIB)
         product(0, 1, 1)
-        product(1, 0, 2, 2)
-        product(1, 1, 3)
-        product(0, 3, 4)
-        product(1, 3, 5)
-        product(0, 2, 6)
-        product(1, 2, 7)
         place_rounded(2, 0, 2, free + 22 * KIB)
         place_rounded(2, 2, 4, free + 24 * KIB)
         round_weight(on_vector, 2, 2, 4)
         round_weight(on_scalar, 2, 0, 2)
         quantize_weight(2, 2, 4, free + 26 * KIB)
-        second_factor(0, raw_at(2))
-        first_factor(1, raw_at(2) + 6 * KIB)
         quantize_weight(2, 0, 2, free + 27 * KIB)
+        product(1, 0, 2)
+        second_factor(0, free + 18 * KIB)
+        first_factor(1, raw_at(2) + 6 * KIB)
+        product(0, 3, 4)
+        product(1, 1, 3)
         second_factor(1, free + 28 * KIB)
+        product(1, 3, 5)
         first_factor(3, raw_at(2) + 2 * KIB)
         second_factor_gpsimd(3)
-        first_factor(2, free + 16 * KIB)
         product(2, 0, 0, 2)
+        product(0, 2, 6)
+        first_factor(2, free + 12 * KIB)
         third_factor(0)
-        product(2, 1, 1)
+        product(2, 1, 7)
         third_factor(1)
-        second_factor(2, raw_at(2))
+        product(1, 2, 1)
+        second_factor(2, free + 18 * KIB)
         product(2, 2, 2)
         product(2, 3, 3)
         quantize_z(0, 2)

@@ -176,7 +176,7 @@ def tile_picked_trilin_none_p_kernel(
             nc.sync.dma_start(out=out_view[:, :, c0 * CHUNK : c1 * CHUNK], in_=staged[:])
 
         def finish_last(c):
-            for h, copy, queue, b in ((0, nc.scalar.copy, nc.scalar, 6), (1, nc.vector.tensor_copy, nc.sync, 0)):
+            for h, copy, queue, b in ((0, nc.scalar.copy, nc.scalar, 6), (1, nc.vector.tensor_copy, nc.sync, 2)):
                 res = bank_tile([P, CHUNK], b)
                 staged = keep.tile([P, CHUNK], F32, name=f"staged_last{h}", align_bytes=64)
                 last_product(res[:], h, c, c + 1)
@@ -197,9 +197,9 @@ def tile_picked_trilin_none_p_kernel(
         load_weight(0)
         load_weight(1)
         gather_bytes(0, S)
-        move_scale_rows(0, 2 * CHUNK)
+        move_scale_rows(0, V)
         load_weight(2)
-        move_scale_rows(2 * CHUNK, S)
+        move_scale_rows(V, S)
         nc.sync.dma_start(out=last_words[:].bitcast(I32), in_=w4_words[0].bitcast(I32))
         load_scale_rows(last_scales, w4_scales)
 
@@ -218,6 +218,8 @@ def tile_picked_trilin_none_p_kernel(
         product(0, 0, 0)
         first_factor(0, free + 16 * KIB)
         product(0, 1, 1)
+        product(0, 3, 4)
+        product(0, 2, 6)
         place_rounded(2, 0, 2, free + 22 * KIB)
         place_rounded(2, 2, 4, free + 24 * KIB)
         round_weight(on_vector, 2, 2, 4)
@@ -227,22 +229,20 @@ def tile_picked_trilin_none_p_kernel(
         product(1, 0, 2)
         second_factor(0, free + 18 * KIB)
         first_factor(1, raw_at(2) + 6 * KIB)
-        product(0, 3, 4)
         product(1, 1, 3)
         second_factor(1, free + 28 * KIB)
         product(1, 3, 5)
         first_factor(3, raw_at(2) + 2 * KIB)
         second_factor_gpsimd(3)
         product(2, 0, 0, 2)
-        product(0, 2, 6)
-        first_factor(2, free + 12 * KIB)
+        first_factor(2, free + 16 * KIB)
         third_factor(0)
         product(2, 1, 7)
         third_factor(1)
         product(1, 2, 1)
         second_factor(2, free + 18 * KIB)
-        product(2, 2, 2)
-        product(2, 3, 3)
+        product(2, 2, 0)
+        product(2, 3, 7)
         quantize_z(0, 2)
         finish(0, 2, 4)
         third_factor(2)

@@ -21,6 +21,7 @@ PIECES = 3
 CHUNK = 128
 CHUNKS = V // CHUNK
 HALVES = N // P
+SPLIT = 88
 KIB = 1024
 
 
@@ -143,9 +144,16 @@ def tile_picked_trilin_none_p_kernel(
             pair[c] = shared.tile([P, CHUNK, PACK], F32, name=f"pair{c}", align_bytes=64, offset=at)
             nc.vector.tensor_tensor(out=pair[c][:], in0=banks[1, c], in1=first[c][:], op=MULT)
 
-        def third_factor(c):
-            part = z[:, c * CHUNK * PACK : (c + 1) * CHUNK * PACK].rearrange("p (v t) -> p v t", t=PACK)
-            nc.vector.tensor_tensor(out=part, in0=banks[2, c], in1=pair[c][:], op=MULT)
+        def z_part(c, v0, v1):
+            return z[:, (c * CHUNK + v0) * PACK : (c * CHUNK + v1) * PACK].rearrange("p (v t) -> p v t", t=PACK)
+
+        def third_factor(c, v1=CHUNK):
+            nc.vector.tensor_tensor(out=z_part(c, 0, v1), in0=banks[2, c][:, :v1], in1=pair[c][:, :v1], op=MULT)
+
+        def third_factor_gpsimd(c, v0, at):
+            third = shared.tile([P, CHUNK - v0, PACK], F32, name="third", align_bytes=64, offset=at)
+            nc.scalar.copy(out=third[:], in_=banks[2, c][:, v0:])
+            nc.gpsimd.tensor_tensor(out=z_part(c, v0, CHUNK), in0=third[:], in1=pair[c][:, v0:], op=MULT)
 
         def quantize_z(c0, c1):
             z_codes[c0] = keep.tile([P, (c1 - c0) * CHUNK], U32, name=f"z_codes{c0}", align_bytes=64)
@@ -222,10 +230,11 @@ def tile_picked_trilin_none_p_kernel(
         product(0, 2, 6)
         place_rounded(2, 0, 2, free + 22 * KIB)
         place_rounded(2, 2, 4, free + 24 * KIB)
+        round_weight(on_vector, 2, 0, 2, 5 * P // 8, P)
         round_weight(on_vector, 2, 2, 4)
-        round_weight(on_scalar, 2, 0, 2)
-        quantize_weight(2, 2, 4, free + 26 * KIB)
+        round_weight(on_scalar, 2, 0, 2, 0, 5 * P // 8)
         quantize_weight(2, 0, 2, free + 27 * KIB)
+        quantize_weight(2, 2, 4, raw_at(2))
         product(1, 0, 2)
         second_factor(0, free + 18 * KIB)
         first_factor(1, raw_at(2) + 6 * KIB)
@@ -234,19 +243,20 @@ def tile_picked_trilin_none_p_kernel(
         product(1, 3, 5)
         first_factor(3, raw_at(2) + 2 * KIB)
         second_factor_gpsimd(3)
-        product(2, 0, 0, 2)
+        product(2, 0, 0)
         first_factor(2, free + 16 * KIB)
         third_factor(0)
-        product(2, 1, 7)
+        product(2, 1, 7, 2)
         third_factor(1)
         product(1, 2, 1)
         second_factor(2, free + 18 * KIB)
         product(2, 2, 0)
         product(2, 3, 7)
+        third_factor_gpsimd(3, SPLIT, free + 16 * KIB)
         quantize_z(0, 2)
         finish(0, 2, 4)
         third_factor(2)
-        third_factor(3)
+        third_factor(3, SPLIT)
         quantize_z(2, 3)
         finish(2, 3, 5)
         quantize_z(3, 4)

@@ -74,7 +74,7 @@ def tile_picked_trilin_none_p_kernel(
             for q in (0, 2, 1, 3):
                 nc.sync.dma_start(
                     out=x_bytes[32 * q : 32 * q + 4, lo:hi].bitcast(I32),
-                    in_=picked_bytes[32 + 16 * q : 48 + 16 * q : 4, lo:hi].bitcast(I32),
+                    in_=picked_bytes[64 + 8 * q : 72 + 8 * q : 2, lo:hi].bitcast(I32),
                 )
 
         def load_weight(d):
@@ -174,14 +174,15 @@ def tile_picked_trilin_none_p_kernel(
                 stop=True,
             )
 
-        def finish(c0, c1, b):
+        def finish(c0, c1, b, stores):
             width = (c1 - c0) * CHUNK
             res = bank_tile([P, HALVES, width], b)
             staged = keep.tile([P, HALVES, width], F32, name=f"staged{c0}", align_bytes=64)
             for h in range(HALVES):
                 last_product(res[:, h, :], h, c0, c1)
-            nc.scalar.copy(out=staged[:], in_=res[:])
-            nc.sync.dma_start(out=out_view[:, :, c0 * CHUNK : c1 * CHUNK], in_=staged[:])
+            for h0, h1 in stores:
+                nc.scalar.copy(out=staged[:, h0:h1], in_=res[:, h0:h1])
+                nc.sync.dma_start(out=out_view[:, h0:h1, c0 * CHUNK : c1 * CHUNK], in_=staged[:, h0:h1])
 
         def finish_last(c):
             for h, copy, queue, b in ((0, nc.scalar.copy, nc.scalar, 6), (1, nc.vector.tensor_copy, nc.sync, 2)):
@@ -195,10 +196,10 @@ def tile_picked_trilin_none_p_kernel(
 
         nc.sync.dma_start(offsets[:], offs)
         nc.scalar.dma_start(
-            out=table_scales[32:96, :].bitcast(I32),
-            in_=x_scales[0].bitcast(I32).unsqueeze(1).to_broadcast([16, 4, T // 4]),
+            out=table_scales[64:96, :].bitcast(I32),
+            in_=x_scales[0].bitcast(I32).unsqueeze(1).to_broadcast([16, 2, T // 4]),
         )
-        nc.gpsimd.memset(table_scales[0:32, :].bitcast(I32), 0)
+        nc.gpsimd.memset(table_scales[0:64, :].bitcast(I32), 0)
         nc.gpsimd.memset(table_scales[96:P, :].bitcast(I32), 0)
         nc.gpsimd.memset(x_bytes[:].bitcast(I32), 0)
         nc.sync.dma_start(out=table_words[:].bitcast(I32), in_=x_words[0].rearrange("p c r -> p (c r)").bitcast(I32))
@@ -254,10 +255,10 @@ def tile_picked_trilin_none_p_kernel(
         product(2, 3, 7)
         third_factor_gpsimd(3, SPLIT, free + 16 * KIB)
         quantize_z(0, 2)
-        finish(0, 2, 4)
+        finish(0, 2, 4, ((0, 1), (1, 2)))
         third_factor(2)
         third_factor(3, SPLIT)
         quantize_z(2, 3)
-        finish(2, 3, 5)
+        finish(2, 3, 5, ((0, 2),))
         quantize_z(3, 4)
         finish_last(3)

@@ -213,16 +213,16 @@ def tile_picked_trilin_none_p_kernel(
         load_scale_rows(last_scales, w4_scales)
 
         free = 24 * KIB
-        gather_words(0, 9, free)
+        gather_words(0, 10, free)
         place_rounded(0, 0, 4, free + 6 * KIB)
-        round_weight(nc.gpsimd.tensor_copy, 0, 2, 4, P // 2, P, "p t m j")
+        round_weight(nc.gpsimd.tensor_copy, 0, 2, 4, 5 * P // 16, P, "p t m j")
         round_weight(on_scalar, 0, 0, 2)
-        round_weight(on_scalar, 0, 2, 4, 0, P // 2)
+        round_weight(on_scalar, 0, 2, 4, 0, 5 * P // 16)
         quantize_weight(0, 0, 4, free + 10 * KIB)
         place_rounded(1, 0, 4, raw_at(0) + 4 * KIB)
         round_weight(on_scalar, 1, 0, 2)
         round_weight(on_vector, 1, 2, 4)
-        gather_words(9, 12, raw_at(0))
+        gather_words(10, 12, raw_at(0))
         quantize_weight(1, 0, 4, raw_at(1))
         product(0, 0, 0)
         first_factor(0, free + 16 * KIB)

@@ -218,12 +218,14 @@ def tile_picked_trilin_none_p_kernel(
         round_weight(nc.gpsimd.tensor_copy, 0, 2, 4, 5 * P // 16, P, "p t m j")
         round_weight(on_scalar, 0, 0, 2)
         round_weight(on_scalar, 0, 2, 4, 0, 5 * P // 16)
-        quantize_weight(0, 0, 4, free + 10 * KIB)
+        quantize_weight(0, 0, 2, free + 10 * KIB)
+        quantize_weight(0, 2, 4, free + 11 * KIB)
         place_rounded(1, 0, 4, raw_at(0) + 4 * KIB)
         round_weight(on_scalar, 1, 0, 2)
         round_weight(on_vector, 1, 2, 4)
         gather_words(10, 12, raw_at(0))
-        quantize_weight(1, 0, 4, raw_at(1))
+        quantize_weight(1, 2, 4, free + 12 * KIB)
+        quantize_weight(1, 0, 2, free + 13 * KIB)
         product(0, 0, 0)
         first_factor(0, free + 16 * KIB)
         product(0, 1, 1)
@@ -231,11 +233,11 @@ def tile_picked_trilin_none_p_kernel(
         product(0, 2, 6)
         place_rounded(2, 0, 2, free + 22 * KIB)
         place_rounded(2, 2, 4, free + 24 * KIB)
-        round_weight(on_vector, 2, 0, 2, 5 * P // 8, P)
         round_weight(on_vector, 2, 2, 4)
-        round_weight(on_scalar, 2, 0, 2, 0, 5 * P // 8)
+        round_weight(on_vector, 2, 0, 2, 11 * P // 16, P)
+        round_weight(on_scalar, 2, 0, 2, 0, 11 * P // 16)
+        quantize_weight(2, 2, 4, free + 26 * KIB)
         quantize_weight(2, 0, 2, free + 27 * KIB)
-        quantize_weight(2, 2, 4, raw_at(2))
         product(1, 0, 2)
         second_factor(0, free + 18 * KIB)
         first_factor(1, raw_at(2) + 6 * KIB)
@@ -244,10 +246,10 @@ def tile_picked_trilin_none_p_kernel(
         product(1, 3, 5)
         first_factor(3, raw_at(2) + 2 * KIB)
         second_factor_gpsimd(3)
-        product(2, 0, 0)
+        product(2, 0, 0, 2)
         first_factor(2, free + 16 * KIB)
         third_factor(0)
-        product(2, 1, 7, 2)
+        product(2, 1, 7)
         third_factor(1)
         product(1, 2, 1)
         second_factor(2, free + 18 * KIB)

@@ -21,7 +21,7 @@ PIECES = 3
 CHUNK = 128
 CHUNKS = V // CHUNK
 HALVES = N // P
-SPLIT = 88
+SPLIT = 48
 KIB = 1024
 
 
@@ -255,12 +255,12 @@ def tile_picked_trilin_none_p_kernel(
         second_factor(2, free + 18 * KIB)
         product(2, 2, 0)
         product(2, 3, 7)
-        third_factor_gpsimd(3, SPLIT, free + 16 * KIB)
+        third_factor_gpsimd(2, SPLIT, free + 30 * KIB)
         quantize_z(0, 2)
         finish(0, 2, 4, ((0, 1), (1, 2)))
-        third_factor(2)
-        third_factor(3, SPLIT)
-        quantize_z(2, 3)
-        finish(2, 3, 5, ((0, 2),))
+        third_factor(3)
+        third_factor(2, SPLIT)
         quantize_z(3, 4)
-        finish_last(3)
+        finish(3, 4, 5, ((0, 2),))
+        quantize_z(2, 3)
+        finish_last(2)

@@ -74,7 +74,7 @@ def tile_picked_trilin_none_p_kernel(
             for q in (0, 2, 1, 3):
                 nc.sync.dma_start(
                     out=x_bytes[32 * q : 32 * q + 4, lo:hi].bitcast(I32),
-                    in_=picked_bytes[64 + 8 * q : 72 + 8 * q : 2, lo:hi].bitcast(I32),
+                    in_=picked_bytes[112 + 4 * q : 116 + 4 * q, lo:hi].bitcast(I32),
                 )
 
         def load_weight(d):
@@ -196,11 +196,11 @@ def tile_picked_trilin_none_p_kernel(
 
         nc.sync.dma_start(offsets[:], offs)
         nc.scalar.dma_start(
-            out=table_scales[64:96, :].bitcast(I32),
-            in_=x_scales[0].bitcast(I32).unsqueeze(1).to_broadcast([16, 2, T // 4]),
+            out=table_scales[112:P, :].bitcast(I32),
+            in_=x_scales[0].bitcast(I32),
         )
-        nc.gpsimd.memset(table_scales[0:64, :].bitcast(I32), 0)
-        nc.gpsimd.memset(table_scales[96:P, :].bitcast(I32), 0)
+        nc.gpsimd.memset(table_scales[0:96, :].bitcast(I32), 0)
+        nc.gpsimd.memset(table_scales[96:112, :].bitcast(I32), 0)
         nc.gpsimd.memset(x_bytes[:].bitcast(I32), 0)
         nc.sync.dma_start(out=table_words[:].bitcast(I32), in_=x_words[0].rearrange("p c r -> p (c r)").bitcast(I32))
         load_weight(0)

@@ -23,6 +23,7 @@ CHUNKS = V // CHUNK
 HALVES = N // P
 SPLIT = 48
 KIB = 1024
+ROWS_AT = 112
 
 
 def tile_picked_trilin_none_p_kernel(
@@ -43,11 +44,11 @@ def tile_picked_trilin_none_p_kernel(
         last_scales = keep.tile([P, N], U8, name="last_scales", align_bytes=64)
         w_scales = [keep.tile([P, H], U8, name=f"w_scales{d}", align_bytes=64) for d in range(PIECES)]
         x_bytes = keep.tile([P, S], U8, name="x_bytes", align_bytes=64)
-        picked_bytes = keep.tile([P, S], U8, name="picked_bytes", align_bytes=64)
         z = keep.tile([P, V * PACK], BF16, name="z", align_bytes=64)
         z_scales = keep.tile([P, V], U8, name="z_scales", align_bytes=64)
         out_view = out.rearrange("(h m) v -> m h v", h=HALVES)
 
+        picked = {}
         raw = {}
         rounded = {}
         w_codes = {}
@@ -57,8 +58,18 @@ def tile_picked_trilin_none_p_kernel(
         banks = {}
         z_codes = {}
 
+        def place(shape, dtype, name, at):
+            if at is None:
+                return keep.tile(shape, dtype, name=name, align_bytes=64)
+            return shared.tile(shape, dtype, name=name, align_bytes=64, offset=at)
+
         def raw_at(d):
             return 8 * d * KIB
+
+        def rounded_at(d, half):
+            return (24 + 4 * d + 2 * half) * KIB
+
+        spare = 36 * KIB
 
         def load_scale_rows(plane, rows):
             for q in range(4):
@@ -67,46 +78,42 @@ def tile_picked_trilin_none_p_kernel(
                     in_=rows[0, 4 * q : 4 * q + 4, :].bitcast(I32).partition_broadcast(8),
                 )
 
-        def gather_bytes(lo, hi):
-            nc.vector.tensor_copy(out=picked_bytes[:, lo:hi], in_=table_scales[:].indirect(offsets[:, lo // 16 : hi // 16]))
+        def gather_bytes(d0, d1):
+            tile = place([P, (d1 - d0) * V], U8, f"picked{d0}", None)
+            nc.vector.tensor_copy(out=tile[:], in_=table_scales[:].indirect(offsets[:, d0 * V // 16 : d1 * V // 16]))
+            for d in range(d0, d1):
+                picked[d] = (tile, (d - d0) * V)
 
-        def move_scale_rows(lo, hi):
+        def move_scale_rows(d):
+            tile, lo = picked[d]
             for q in (0, 2, 1, 3):
                 nc.sync.dma_start(
-                    out=x_bytes[32 * q : 32 * q + 4, lo:hi].bitcast(I32),
-                    in_=picked_bytes[112 + 4 * q : 116 + 4 * q, lo:hi].bitcast(I32),
+                    out=x_bytes[32 * q : 32 * q + 4, d * V : (d + 1) * V].bitcast(I32),
+                    in_=tile[ROWS_AT + 4 * q : ROWS_AT + 4 * q + 4, lo : lo + V].bitcast(I32),
                 )
 
         def load_weight(d):
-            raw[d] = shared.tile([P, PACK, H], F32, name=f"raw{d}", align_bytes=64, offset=raw_at(d))
+            raw[d] = place([P, PACK, H], F32, f"raw{d}", raw_at(d))
             nc.sync.dma_start(out=raw[d][:], in_=weights[d].rearrange("(p j) c -> p j c", j=PACK))
 
-        def place_rounded(d, t0, t1, at):
-            tile = shared.tile([P, (t1 - t0) * H], BF16, name=f"rounded{d}_{t0}", align_bytes=64, offset=at)
-            for t in range(t0, t1):
-                rounded[d, t] = (tile, t0)
+        def round_part(copy, d, half, m0, m1):
+            if (d, half) not in rounded:
+                rounded[d, half] = place([P, 2 * H], BF16, f"rounded{d}_{half}", rounded_at(d, half))
+            src = raw[d][:].rearrange("p j (m t) -> p m j t", t=PACK)[:, m0:m1, :, 2 * half : 2 * half + 2]
+            dst = rounded[d, half][:].rearrange("p (t m j) -> p m j t", m=P, j=PACK)[:, m0:m1]
+            copy(out=dst, in_=src)
 
-        def rounded_part(d, t0, t1):
-            tile, base = rounded[d, t0]
-            return tile[:, (t0 - base) * H : (t1 - base) * H]
-
-        def round_weight(copy, d, t0, t1, m0=0, m1=P, walk="p m j t"):
-            src = raw[d][:].rearrange("p j (m t) -> p m j t", t=PACK)[:, m0:m1, :, t0:t1]
-            dst = rounded_part(d, t0, t1).rearrange("p (t m j) -> p m j t", m=P, j=PACK)[:, m0:m1]
-            copy(out=dst.rearrange(f"p m j t -> {walk}"), in_=src.rearrange(f"p m j t -> {walk}"))
-
-        def quantize_weight(d, t0, t1, at):
-            codes = shared.tile([P, (t1 - t0) * P], U32, name=f"w_codes{d}_{t0}", align_bytes=64, offset=at)
-            nc.vector.quantize_mx(
-                out=codes[:].bitcast(FP8X4), scales=w_scales[d][:, t0 * P : t1 * P], in_=rounded_part(d, t0, t1)
-            )
-            for t in range(t0, t1):
-                w_codes[d, t] = codes[:, (t - t0) * P : (t - t0 + 1) * P]
+        def quantize_weight(d, half):
+            codes = place([P, 2 * P], U32, f"w_codes{d}_{half}", None)
+            cols = slice(2 * half * P, 2 * (half + 1) * P)
+            nc.vector.quantize_mx(out=codes[:].bitcast(FP8X4), scales=w_scales[d][:, cols], in_=rounded[d, half][:])
+            for t in range(2):
+                w_codes[d, 2 * half + t] = codes[:, t * P : (t + 1) * P]
 
         def gather_words(c0, c1, at):
-            codes = shared.tile([P, (c1 - c0) * CHUNK], U32, name=f"x_codes{c0}", align_bytes=64, offset=at)
-            picked = offsets[:, c0 * CHUNK // 16 : c1 * CHUNK // 16]
-            nc.vector.tensor_copy(out=codes[:], in_=table_words[:].indirect(picked))
+            codes = place([P, (c1 - c0) * CHUNK], U32, f"x_codes{c0}", at)
+            entries = offsets[:, c0 * CHUNK // 16 : c1 * CHUNK // 16]
+            nc.vector.tensor_copy(out=codes[:], in_=table_words[:].indirect(entries))
             for c in range(c0, c1):
                 x_codes[divmod(c, CHUNKS)] = codes[:, (c - c0) * CHUNK : (c - c0 + 1) * CHUNK]
 
@@ -131,17 +138,17 @@ def tile_picked_trilin_none_p_kernel(
             banks[d, c] = bank[:].rearrange("p t v -> p v t")
 
         def first_factor(c, at):
-            first[c] = shared.tile([P, CHUNK, PACK], F32, name=f"first{c}", align_bytes=64, offset=at)
+            first[c] = place([P, CHUNK, PACK], F32, f"first{c}", at)
             nc.scalar.copy(out=first[c][:], in_=banks[0, c])
 
-        def second_factor_gpsimd(c):
-            second = shared.tile([P, CHUNK, PACK], F32, name="second", align_bytes=64, offset=raw_at(2) + 4 * KIB)
-            pair[c] = keep.tile([P, CHUNK, PACK], F32, name=f"pair{c}", align_bytes=64)
+        def second_factor_gpsimd(c, at, pair_at):
+            second = place([P, CHUNK, PACK], F32, "second", at)
+            pair[c] = place([P, CHUNK, PACK], F32, f"pair{c}", pair_at)
             nc.scalar.copy(out=second[:], in_=banks[1, c])
             nc.gpsimd.tensor_tensor(out=pair[c][:], in0=second[:], in1=first[c][:], op=MULT)
 
         def second_factor(c, at):
-            pair[c] = shared.tile([P, CHUNK, PACK], F32, name=f"pair{c}", align_bytes=64, offset=at)
+            pair[c] = place([P, CHUNK, PACK], F32, f"pair{c}", at)
             nc.vector.tensor_tensor(out=pair[c][:], in0=banks[1, c], in1=first[c][:], op=MULT)
 
         def z_part(c, v0, v1):
@@ -150,13 +157,13 @@ def tile_picked_trilin_none_p_kernel(
         def third_factor(c, v1=CHUNK):
             nc.vector.tensor_tensor(out=z_part(c, 0, v1), in0=banks[2, c][:, :v1], in1=pair[c][:, :v1], op=MULT)
 
-        def third_factor_gpsimd(c, v0, at):
-            third = shared.tile([P, CHUNK - v0, PACK], F32, name="third", align_bytes=64, offset=at)
+        def third_factor_gpsimd(c, v0):
+            third = place([P, CHUNK - v0, PACK], F32, "third", None)
             nc.scalar.copy(out=third[:], in_=banks[2, c][:, v0:])
             nc.gpsimd.tensor_tensor(out=z_part(c, v0, CHUNK), in0=third[:], in1=pair[c][:, v0:], op=MULT)
 
         def quantize_z(c0, c1):
-            z_codes[c0] = keep.tile([P, (c1 - c0) * CHUNK], U32, name=f"z_codes{c0}", align_bytes=64)
+            z_codes[c0] = place([P, (c1 - c0) * CHUNK], U32, f"z_codes{c0}", None)
             nc.vector.quantize_mx(
                 out=z_codes[c0][:].bitcast(FP8X4),
                 scales=z_scales[:, c0 * CHUNK : c1 * CHUNK],
@@ -177,17 +184,17 @@ def tile_picked_trilin_none_p_kernel(
         def finish(c0, c1, b, stores):
             width = (c1 - c0) * CHUNK
             res = bank_tile([P, HALVES, width], b)
-            staged = keep.tile([P, HALVES, width], F32, name=f"staged{c0}", align_bytes=64)
+            staged = place([P, HALVES, width], F32, f"staged{c0}", None)
             for h in range(HALVES):
                 last_product(res[:, h, :], h, c0, c1)
             for h0, h1 in stores:
                 nc.scalar.copy(out=staged[:, h0:h1], in_=res[:, h0:h1])
                 nc.sync.dma_start(out=out_view[:, h0:h1, c0 * CHUNK : c1 * CHUNK], in_=staged[:, h0:h1])
 
-        def finish_last(c):
-            for h, copy, queue, b in ((0, nc.scalar.copy, nc.scalar, 6), (1, nc.vector.tensor_copy, nc.sync, 2)):
+        def finish_last(c, b0, b1):
+            for h, copy, queue, b in ((0, nc.scalar.copy, nc.scalar, b0), (1, nc.vector.tensor_copy, nc.sync, b1)):
                 res = bank_tile([P, CHUNK], b)
-                staged = keep.tile([P, CHUNK], F32, name=f"staged_last{h}", align_bytes=64)
+                staged = place([P, CHUNK], F32, f"staged_last{h}", None)
                 last_product(res[:], h, c, c + 1)
                 copy(out=staged[:], in_=res[:])
                 queue.dma_start(out=out_view[:, h, c * CHUNK : (c + 1) * CHUNK], in_=staged[:])
@@ -195,67 +202,63 @@ def tile_picked_trilin_none_p_kernel(
         on_scalar, on_vector = nc.scalar.copy, nc.vector.tensor_copy
 
         nc.sync.dma_start(offsets[:], offs)
-        nc.scalar.dma_start(
-            out=table_scales[112:P, :].bitcast(I32),
-            in_=x_scales[0].bitcast(I32),
-        )
+        nc.scalar.dma_start(out=table_scales[ROWS_AT:P, :].bitcast(I32), in_=x_scales[0].bitcast(I32))
         nc.gpsimd.memset(table_scales[0:96, :].bitcast(I32), 0)
-        nc.gpsimd.memset(table_scales[96:112, :].bitcast(I32), 0)
+        nc.gpsimd.memset(table_scales[96:ROWS_AT, :].bitcast(I32), 0)
         nc.gpsimd.memset(x_bytes[:].bitcast(I32), 0)
         nc.sync.dma_start(out=table_words[:].bitcast(I32), in_=x_words[0].rearrange("p c r -> p (c r)").bitcast(I32))
         load_weight(0)
+        gather_bytes(0, 1)
+        gather_bytes(1, 3)
+        move_scale_rows(0)
         load_weight(1)
-        gather_bytes(0, S)
-        move_scale_rows(0, V)
+        move_scale_rows(1)
         load_weight(2)
-        move_scale_rows(V, S)
+        move_scale_rows(2)
         nc.sync.dma_start(out=last_words[:].bitcast(I32), in_=w4_words[0].bitcast(I32))
         load_scale_rows(last_scales, w4_scales)
 
-        free = 24 * KIB
-        gather_words(0, 10, free)
-        place_rounded(0, 0, 4, free + 6 * KIB)
-        round_weight(nc.gpsimd.tensor_copy, 0, 2, 4, 5 * P // 16, P, "p t m j")
-        round_weight(on_scalar, 0, 0, 2)
-        round_weight(on_scalar, 0, 2, 4, 0, 5 * P // 16)
-        quantize_weight(0, 0, 2, free + 10 * KIB)
-        quantize_weight(0, 2, 4, free + 11 * KIB)
-        place_rounded(1, 0, 4, raw_at(0) + 4 * KIB)
-        round_weight(on_scalar, 1, 0, 2)
-        round_weight(on_vector, 1, 2, 4)
-        gather_words(10, 12, raw_at(0))
-        quantize_weight(1, 2, 4, free + 12 * KIB)
-        quantize_weight(1, 0, 2, free + 13 * KIB)
+        gather_words(0, 10, None)
+        round_part(on_scalar, 0, 0, 0, P)
+        round_part(on_vector, 0, 1, 40, P)
+        round_part(on_scalar, 0, 1, 0, 40)
+        quantize_weight(0, 0)
+        quantize_weight(0, 1)
+        gather_words(10, 11, rounded_at(0, 0))
         product(0, 0, 0)
-        first_factor(0, free + 16 * KIB)
         product(0, 1, 1)
-        product(0, 3, 4)
-        product(0, 2, 6)
-        place_rounded(2, 0, 2, free + 22 * KIB)
-        place_rounded(2, 2, 4, free + 24 * KIB)
-        round_weight(on_vector, 2, 2, 4)
-        round_weight(on_vector, 2, 0, 2, 11 * P // 16, P)
-        round_weight(on_scalar, 2, 0, 2, 0, 11 * P // 16)
-        quantize_weight(2, 2, 4, free + 26 * KIB)
-        quantize_weight(2, 0, 2, free + 27 * KIB)
-        product(1, 0, 2)
-        second_factor(0, free + 18 * KIB)
-        first_factor(1, raw_at(2) + 6 * KIB)
-        product(1, 1, 3)
-        second_factor(1, free + 28 * KIB)
+        product(0, 3, 2)
+        round_part(on_vector, 1, 1, 0, P)
+        round_part(on_vector, 1, 0, 88, P)
+        round_part(on_scalar, 1, 0, 0, 88)
+        quantize_weight(1, 1)
+        quantize_weight(1, 0)
+        gather_words(11, 12, rounded_at(1, 1))
+        first_factor(0, raw_at(1))
+        first_factor(1, raw_at(1) + 2 * KIB)
+        first_factor(3, raw_at(1) + 4 * KIB)
+        product(1, 0, 3, 2)
+        second_factor(0, spare)
+        product(1, 1, 4)
         product(1, 3, 5)
-        first_factor(3, raw_at(2) + 2 * KIB)
-        second_factor_gpsimd(3)
+        product(1, 2, 6)
+        product(0, 2, 3)
+        round_part(on_vector, 2, 1, 0, P)
+        round_part(on_vector, 2, 0, 88, P)
+        round_part(on_scalar, 2, 0, 0, 88)
+        quantize_weight(2, 1)
+        quantize_weight(2, 0)
+        second_factor(1, rounded_at(2, 1))
+        second_factor_gpsimd(3, raw_at(2), rounded_at(2, 0))
+        first_factor(2, raw_at(2) + 2 * KIB)
         product(2, 0, 0, 2)
-        first_factor(2, free + 16 * KIB)
         third_factor(0)
         product(2, 1, 7)
         third_factor(1)
-        product(1, 2, 1)
-        second_factor(2, free + 18 * KIB)
+        second_factor(2, spare)
         product(2, 2, 0)
         product(2, 3, 7)
-        third_factor_gpsimd(2, SPLIT, free + 30 * KIB)
+        third_factor_gpsimd(2, SPLIT)
         quantize_z(0, 2)
         finish(0, 2, 4, ((0, 1), (1, 2)))
         third_factor(3)
@@ -263,4 +266,4 @@ def tile_picked_trilin_none_p_kernel(
         quantize_z(3, 4)
         finish(3, 4, 5, ((0, 2),))
         quantize_z(2, 3)
-        finish_last(2)
+        finish_last(2, 1, 2)

@@ -21,7 +21,7 @@ PIECES = 3
 CHUNK = 128
 CHUNKS = V // CHUNK
 HALVES = N // P
-SPLIT = 48
+SPLIT = 92
 KIB = 1024
 ROWS_AT = 112
 
@@ -44,7 +44,6 @@ def tile_picked_trilin_none_p_kernel(
         last_scales = keep.tile([P, N], U8, name="last_scales", align_bytes=64)
         w_scales = [keep.tile([P, H], U8, name=f"w_scales{d}", align_bytes=64) for d in range(PIECES)]
         x_bytes = keep.tile([P, S], U8, name="x_bytes", align_bytes=64)
-        z = keep.tile([P, V * PACK], BF16, name="z", align_bytes=64)
         z_scales = keep.tile([P, V], U8, name="z_scales", align_bytes=64)
         out_view = out.rearrange("(h m) v -> m h v", h=HALVES)
 
@@ -53,6 +52,7 @@ def tile_picked_trilin_none_p_kernel(
         rounded = {}
         w_codes = {}
         x_codes = {}
+        x_tiles = {}
         first = {}
         pair = {}
         banks = {}
@@ -70,6 +70,7 @@ def tile_picked_trilin_none_p_kernel(
             return (24 + 4 * d + 2 * half) * KIB
 
         spare = 36 * KIB
+        z = {}
 
         def load_scale_rows(plane, rows):
             for q in range(4):
@@ -78,33 +79,30 @@ def tile_picked_trilin_none_p_kernel(
                     in_=rows[0, 4 * q : 4 * q + 4, :].bitcast(I32).partition_broadcast(8),
                 )
 
-        def gather_bytes(d0, d1):
-            tile = place([P, (d1 - d0) * V], U8, f"picked{d0}", None)
-            nc.vector.tensor_copy(out=tile[:], in_=table_scales[:].indirect(offsets[:, d0 * V // 16 : d1 * V // 16]))
-            for d in range(d0, d1):
-                picked[d] = (tile, (d - d0) * V)
+        def gather_bytes(lo, hi):
+            picked[lo] = place([P, hi - lo], U8, f"picked{lo}", None)
+            nc.vector.tensor_copy(out=picked[lo][:], in_=table_scales[:].indirect(offsets[:, lo // 16 : hi // 16]))
 
-        def move_scale_rows(d):
-            tile, lo = picked[d]
+        def move_scale_rows(base, lo, hi):
             for q in (0, 2, 1, 3):
                 nc.sync.dma_start(
-                    out=x_bytes[32 * q : 32 * q + 4, d * V : (d + 1) * V].bitcast(I32),
-                    in_=tile[ROWS_AT + 4 * q : ROWS_AT + 4 * q + 4, lo : lo + V].bitcast(I32),
+                    out=x_bytes[32 * q : 32 * q + 4, lo:hi].bitcast(I32),
+                    in_=picked[base][ROWS_AT + 4 * q : ROWS_AT + 4 * q + 4, lo - base : hi - base].bitcast(I32),
                 )
 
         def load_weight(d):
             raw[d] = place([P, PACK, H], F32, f"raw{d}", raw_at(d))
             nc.sync.dma_start(out=raw[d][:], in_=weights[d].rearrange("(p j) c -> p j c", j=PACK))
 
-        def round_part(copy, d, half, m0, m1):
+        def round_part(copy, d, half, m0, m1, walk="p m j t"):
             if (d, half) not in rounded:
                 rounded[d, half] = place([P, 2 * H], BF16, f"rounded{d}_{half}", rounded_at(d, half))
             src = raw[d][:].rearrange("p j (m t) -> p m j t", t=PACK)[:, m0:m1, :, 2 * half : 2 * half + 2]
             dst = rounded[d, half][:].rearrange("p (t m j) -> p m j t", m=P, j=PACK)[:, m0:m1]
-            copy(out=dst, in_=src)
+            copy(out=dst.rearrange(f"p m j t -> {walk}"), in_=src.rearrange(f"p m j t -> {walk}"))
 
-        def quantize_weight(d, half):
-            codes = place([P, 2 * P], U32, f"w_codes{d}_{half}", None)
+        def quantize_weight(d, half, at=None):
+            codes = place([P, 2 * P], U32, f"w_codes{d}_{half}", at)
             cols = slice(2 * half * P, 2 * (half + 1) * P)
             nc.vector.quantize_mx(out=codes[:].bitcast(FP8X4), scales=w_scales[d][:, cols], in_=rounded[d, half][:])
             for t in range(2):
@@ -115,6 +113,7 @@ def tile_picked_trilin_none_p_kernel(
             entries = offsets[:, c0 * CHUNK // 16 : c1 * CHUNK // 16]
             nc.vector.tensor_copy(out=codes[:], in_=table_words[:].indirect(entries))
             for c in range(c0, c1):
+                x_tiles[divmod(c, CHUNKS)] = (codes, (c - c0) * CHUNK)
                 x_codes[divmod(c, CHUNKS)] = codes[:, (c - c0) * CHUNK : (c - c0 + 1) * CHUNK]
 
         def bank_tile(shape, b):
@@ -137,9 +136,48 @@ def tile_picked_trilin_none_p_kernel(
                 )
             banks[d, c] = bank[:].rearrange("p t v -> p v t")
 
-        def first_factor(c, at):
+        def pass_into(target, d, t, c0, c1):
+            cols = slice(d * V + c0 * CHUNK, d * V + c1 * CHUNK)
+            tile, base = x_tiles[d, c0]
+            nc.tensor.matmul_mx(
+                out=target,
+                lhsT=w_codes[d, t].bitcast(FP8X4),
+                lhsT_scale=w_scales[d][:, t * P : (t + 1) * P],
+                rhs=tile[:, base : base + (c1 - c0) * CHUNK].bitcast(FP8X4),
+                rhs_scale=x_bytes[:, cols],
+                start=True,
+                stop=True,
+            )
+
+        first_low = [keep.tile([P, 2 * CHUNK, 2], F32, name=f"first_low{h}", align_bytes=64) for h in range(2)]
+        pair_low = place([P, 2, 2 * CHUNK, 2], F32, "pair_low", spare + 6 * KIB)
+
+        def first_factor_low(h, c, b):
+            bank = bank_tile([P, 2, CHUNK], b)
+            for u in range(2):
+                pass_into(bank[:, u, :], 0, 2 * h + u, c, c + 1)
+            banks[0, h, c] = bank[:].rearrange("p u v -> p v u")
+
+        def empty_low(h, c, copy):
+            copy(out=first_low[h][:, c * CHUNK : (c + 1) * CHUNK, :], in_=banks[0, h, c])
+
+        def second_factor_low(h, b):
+            bank = bank_tile([P, 2, 2 * CHUNK], b)
+            for u in range(2):
+                pass_into(bank[:, u, :], 1, 2 * h + u, 0, 2)
+            nc.vector.tensor_tensor(out=pair_low[:, h], in0=bank[:].rearrange("p u v -> p v u"), in1=first_low[h][:], op=MULT)
+
+        def third_factor_low(c):
+            nc.vector.tensor_tensor(
+                out=z_part(c, 0, CHUNK).rearrange("p v (h u) -> p v h u", u=2),
+                in0=banks[2, c].rearrange("p v (h u) -> p v h u", u=2),
+                in1=pair_low[:, :, c * CHUNK : (c + 1) * CHUNK, :].rearrange("p h v u -> p v h u"),
+                op=MULT,
+            )
+
+        def first_factor(c, at, copy=nc.scalar.copy):
             first[c] = place([P, CHUNK, PACK], F32, f"first{c}", at)
-            nc.scalar.copy(out=first[c][:], in_=banks[0, c])
+            copy(out=first[c][:], in_=banks[0, c])
 
         def second_factor_gpsimd(c, at, pair_at):
             second = place([P, CHUNK, PACK], F32, "second", at)
@@ -152,22 +190,24 @@ def tile_picked_trilin_none_p_kernel(
             nc.vector.tensor_tensor(out=pair[c][:], in0=banks[1, c], in1=first[c][:], op=MULT)
 
         def z_part(c, v0, v1):
-            return z[:, (c * CHUNK + v0) * PACK : (c * CHUNK + v1) * PACK].rearrange("p (v t) -> p v t", t=PACK)
+            if c not in z:
+                z[c] = place([P, CHUNK * PACK], BF16, f"z{c}", spare + (0, 1, 2, 1)[c] * KIB)
+            return z[c][:, v0 * PACK : v1 * PACK].rearrange("p (v t) -> p v t", t=PACK)
 
-        def third_factor(c, v1=CHUNK):
-            nc.vector.tensor_tensor(out=z_part(c, 0, v1), in0=banks[2, c][:, :v1], in1=pair[c][:, :v1], op=MULT)
+        def third_factor(c, v1=CHUNK, v0=0):
+            nc.vector.tensor_tensor(out=z_part(c, v0, v1), in0=banks[2, c][:, v0:v1], in1=pair[c][:, v0:v1], op=MULT)
 
-        def third_factor_gpsimd(c, v0):
-            third = place([P, CHUNK - v0, PACK], F32, "third", None)
+        def third_factor_gpsimd(c, v0, at=None):
+            third = place([P, CHUNK - v0, PACK], F32, f"third{c}", at)
             nc.scalar.copy(out=third[:], in_=banks[2, c][:, v0:])
             nc.gpsimd.tensor_tensor(out=z_part(c, v0, CHUNK), in0=third[:], in1=pair[c][:, v0:], op=MULT)
 
-        def quantize_z(c0, c1):
-            z_codes[c0] = place([P, (c1 - c0) * CHUNK], U32, f"z_codes{c0}", None)
+        def quantize_z(c0, c1, at=None):
+            z_codes[c0] = place([P, (c1 - c0) * CHUNK], U32, f"z_codes{c0}", at)
             nc.vector.quantize_mx(
                 out=z_codes[c0][:].bitcast(FP8X4),
                 scales=z_scales[:, c0 * CHUNK : c1 * CHUNK],
-                in_=z[:, c0 * CHUNK * PACK : c1 * CHUNK * PACK],
+                in_=z[c0][:],
             )
 
         def last_product(target, h, c0, c1):
@@ -181,89 +221,96 @@ def tile_picked_trilin_none_p_kernel(
                 stop=True,
             )
 
-        def finish(c0, c1, b, stores):
+        def finish(c0, c1, b, stores, copy=nc.scalar.copy, at=None):
             width = (c1 - c0) * CHUNK
             res = bank_tile([P, HALVES, width], b)
-            staged = place([P, HALVES, width], F32, f"staged{c0}", None)
+            staged = place([P, HALVES, width], F32, f"staged{c0}", at)
             for h in range(HALVES):
                 last_product(res[:, h, :], h, c0, c1)
             for h0, h1 in stores:
-                nc.scalar.copy(out=staged[:, h0:h1], in_=res[:, h0:h1])
+                copy(out=staged[:, h0:h1], in_=res[:, h0:h1])
                 nc.sync.dma_start(out=out_view[:, h0:h1, c0 * CHUNK : c1 * CHUNK], in_=staged[:, h0:h1])
 
-        def finish_last(c, b0, b1):
+        def finish_last(c, b0, b1, at=None):
             for h, copy, queue, b in ((0, nc.scalar.copy, nc.scalar, b0), (1, nc.vector.tensor_copy, nc.sync, b1)):
                 res = bank_tile([P, CHUNK], b)
-                staged = place([P, CHUNK], F32, f"staged_last{h}", None)
+                staged = place([P, CHUNK], F32, f"staged{c}_{h}", at if h else None)
                 last_product(res[:], h, c, c + 1)
                 copy(out=staged[:], in_=res[:])
                 queue.dma_start(out=out_view[:, h, c * CHUNK : (c + 1) * CHUNK], in_=staged[:])
 
-        on_scalar, on_vector = nc.scalar.copy, nc.vector.tensor_copy
+        on_scalar, on_vector, on_gpsimd = nc.scalar.copy, nc.vector.tensor_copy, nc.gpsimd.tensor_copy
+
+        def round_weight(d, share):
+            if share < P:
+                round_part(on_scalar, d, 0, 0, P - share, "p m j t")
+            round_part(on_gpsimd, d, 0, P - share, P, "p m j t")
+            round_part(on_scalar, d, 1, 0, P)
 
         nc.sync.dma_start(offsets[:], offs)
         nc.scalar.dma_start(out=table_scales[ROWS_AT:P, :].bitcast(I32), in_=x_scales[0].bitcast(I32))
         nc.gpsimd.memset(table_scales[0:96, :].bitcast(I32), 0)
         nc.gpsimd.memset(table_scales[96:ROWS_AT, :].bitcast(I32), 0)
         nc.gpsimd.memset(x_bytes[:].bitcast(I32), 0)
-        nc.sync.dma_start(out=table_words[:].bitcast(I32), in_=x_words[0].rearrange("p c r -> p (c r)").bitcast(I32))
         load_weight(0)
-        gather_bytes(0, 1)
-        gather_bytes(1, 3)
-        move_scale_rows(0)
+        nc.sync.dma_start(out=table_words[:].bitcast(I32), in_=x_words[0].rearrange("p c r -> p (c r)").bitcast(I32))
+        gather_bytes(0, 2 * CHUNK)
+        gather_bytes(2 * CHUNK, S)
+        move_scale_rows(0, 0, 2 * CHUNK)
         load_weight(1)
-        move_scale_rows(1)
+        move_scale_rows(2 * CHUNK, 2 * CHUNK, 2 * V - CHUNK)
         load_weight(2)
-        move_scale_rows(2)
+        move_scale_rows(2 * CHUNK, 2 * V - CHUNK, S)
         nc.sync.dma_start(out=last_words[:].bitcast(I32), in_=w4_words[0].bitcast(I32))
         load_scale_rows(last_scales, w4_scales)
 
-        gather_words(0, 10, None)
-        round_part(on_scalar, 0, 0, 0, P)
-        round_part(on_vector, 0, 1, 40, P)
-        round_part(on_scalar, 0, 1, 0, 40)
+        round_weight(0, 128)
         quantize_weight(0, 0)
         quantize_weight(0, 1)
-        gather_words(10, 11, rounded_at(0, 0))
-        product(0, 0, 0)
-        product(0, 1, 1)
+        gather_words(0, 1, raw_at(0))
+        gather_words(1, 2, raw_at(0) + KIB)
+        gather_words(2, 4, raw_at(0) + 2 * KIB)
+        gather_words(4, 11, raw_at(0) + 3 * KIB)
+        first_factor_low(0, 0, 0)
+        empty_low(0, 0, on_scalar)
+        first_factor_low(1, 0, 1)
+        empty_low(1, 0, on_scalar)
+        first_factor_low(0, 1, 6)
+        empty_low(0, 1, on_scalar)
+        first_factor_low(1, 1, 7)
+        empty_low(1, 1, on_vector)
+        round_weight(1, 128)
         product(0, 3, 2)
-        round_part(on_vector, 1, 1, 0, P)
-        round_part(on_vector, 1, 0, 88, P)
-        round_part(on_scalar, 1, 0, 0, 88)
-        quantize_weight(1, 1)
-        quantize_weight(1, 0)
-        gather_words(11, 12, rounded_at(1, 1))
-        first_factor(0, raw_at(1))
-        first_factor(1, raw_at(1) + 2 * KIB)
-        first_factor(3, raw_at(1) + 4 * KIB)
-        product(1, 0, 3, 2)
-        second_factor(0, spare)
-        product(1, 1, 4)
-        product(1, 3, 5)
-        product(1, 2, 6)
         product(0, 2, 3)
-        round_part(on_vector, 2, 1, 0, P)
-        round_part(on_vector, 2, 0, 88, P)
-        round_part(on_scalar, 2, 0, 0, 88)
-        quantize_weight(2, 1)
+        quantize_weight(1, 0)
+        quantize_weight(1, 1, raw_at(1))
+        gather_words(11, 12, rounded_at(1, 0))
+        first_factor(3, spare + 4 * KIB)
+        first_factor(2, None)
+        second_factor_low(0, 4)
+        second_factor_low(1, 5)
+        product(1, 2, 7)
+        round_weight(2, 112)
+        product(1, 3, 6)
         quantize_weight(2, 0)
-        second_factor(1, rounded_at(2, 1))
-        second_factor_gpsimd(3, raw_at(2), rounded_at(2, 0))
-        first_factor(2, raw_at(2) + 2 * KIB)
-        product(2, 0, 0, 2)
-        third_factor(0)
-        product(2, 1, 7)
-        third_factor(1)
-        second_factor(2, spare)
-        product(2, 2, 0)
-        product(2, 3, 7)
-        third_factor_gpsimd(2, SPLIT)
-        quantize_z(0, 2)
-        finish(0, 2, 4, ((0, 1), (1, 2)))
-        third_factor(3)
-        third_factor(2, SPLIT)
+        quantize_weight(2, 1, raw_at(2))
+        second_factor(2, rounded_at(2, 0))
+        second_factor_gpsimd(3, None, rounded_at(2, 1))
+        product(2, 0, 0)
+        third_factor_low(0)
+        product(2, 1, 1)
+        third_factor_low(1)
+        product(2, 2, 3)
+        product(2, 3, 2)
+        third_factor(2, CHUNK // 2)
+        quantize_z(0, 1)
+        quantize_z(1, 2)
+        finish(0, 1, 4, ((0, 2),))
+        finish(1, 2, 5, ((0, 2),))
+        third_factor_gpsimd(3, SPLIT)
+        third_factor(2, CHUNK, CHUNK // 2)
+        third_factor(3, SPLIT)
+        quantize_z(2, 3, spare + 4 * KIB)
         quantize_z(3, 4)
-        finish(3, 4, 5, ((0, 2),))
-        quantize_z(2, 3)
-        finish_last(2, 1, 2)
+        finish_last(2, 6, 1, spare + KIB)
+        finish_last(3, 0, 7)

@@ -21,9 +21,12 @@ PIECES = 3
 CHUNK = 128
 CHUNKS = V // CHUNK
 HALVES = N // P
-SPLIT = 92
 KIB = 1024
 ROWS_AT = 112
+WALK = "p m j t"
+W3_SCALAR = 16
+COVER = 64
+SPLIT = 92
 
 
 def tile_picked_trilin_none_p_kernel(
@@ -31,143 +34,115 @@ def tile_picked_trilin_none_p_kernel(
 ):
     nc = tc.nc
     weights = (w1, w2, w3)
+    on_scalar, on_vector, on_gpsimd = nc.scalar.copy, nc.vector.tensor_copy, nc.gpsimd.tensor_copy
 
     with ExitStack() as ctx:
         keep = ctx.enter_context(tc.tile_pool(name="keep", bufs=1))
         shared = ctx.enter_context(tc.tile_pool(name="shared", bufs=1))
         psum = ctx.enter_context(tc.psum_pool(name="psum", bufs=1))
 
+        def place(shape, dtype, name, kib=None):
+            if kib is None:
+                return keep.tile(shape, dtype, name=name, align_bytes=64)
+            return shared.tile(shape, dtype, name=name, align_bytes=64, offset=kib * KIB)
+
+        def bank_tile(shape, b):
+            return psum.tile(shape, F32, name=f"bank{b}", tag=f"bank{b}", bufs=1)
+
+        raw_at = (0, 8, 16)
+        rounded_at = {(0, 0): 24, (0, 1): 26, (1, 0): 28, (1, 1): 30, (2, 1): 32, (2, 0): 35}
+        z_at = (38, 39, 40, 39)
+        first3_at = 42
+        pair_low_at = 44
+
         offsets = keep.tile([P, S // 16], U16, name="offsets")
-        table_words = keep.tile([P, T], U32, name="table_words", align_bytes=64)
-        table_scales = keep.tile([P, T], U8, name="table_scales", align_bytes=64)
-        last_words = keep.tile([P, 2 * N], U8, name="last_words", align_bytes=64)
-        last_scales = keep.tile([P, N], U8, name="last_scales", align_bytes=64)
-        w_scales = [keep.tile([P, H], U8, name=f"w_scales{d}", align_bytes=64) for d in range(PIECES)]
-        x_bytes = keep.tile([P, S], U8, name="x_bytes", align_bytes=64)
-        z_scales = keep.tile([P, V], U8, name="z_scales", align_bytes=64)
+        table_words = place([P, T], U32, "table_words")
+        table_scales = place([P, T], U8, "table_scales")
+        last_words = place([P, 2 * N], U8, "last_words")
+        last_scales = place([P, N], U8, "last_scales")
+        w_scales = [place([P, H], U8, f"w_scales{d}") for d in range(PIECES)]
+        x_bytes = place([P, S], U8, "x_bytes")
+        z_scales = place([P, V], U8, "z_scales")
         out_view = out.rearrange("(h m) v -> m h v", h=HALVES)
 
-        picked = {}
-        raw = {}
-        rounded = {}
-        w_codes = {}
-        x_codes = {}
-        x_tiles = {}
-        first = {}
-        pair = {}
-        banks = {}
-        z_codes = {}
-
-        def place(shape, dtype, name, at):
-            if at is None:
-                return keep.tile(shape, dtype, name=name, align_bytes=64)
-            return shared.tile(shape, dtype, name=name, align_bytes=64, offset=at)
-
-        def raw_at(d):
-            return 8 * d * KIB
-
-        def rounded_at(d, half):
-            return (24 + 4 * d + 2 * half) * KIB
-
-        spare = 36 * KIB
-        z = {}
-
-        def load_scale_rows(plane, rows):
-            for q in range(4):
-                nc.sync.dma_start(
-                    out=plane[32 * q : 32 * q + 32, :].bitcast(I32),
-                    in_=rows[0, 4 * q : 4 * q + 4, :].bitcast(I32).partition_broadcast(8),
-                )
+        picked, raw, rounded, w_codes, x_tiles, first, pair, banks, z, z_codes = ({} for i in range(10))
 
         def gather_bytes(lo, hi):
-            picked[lo] = place([P, hi - lo], U8, f"picked{lo}", None)
-            nc.vector.tensor_copy(out=picked[lo][:], in_=table_scales[:].indirect(offsets[:, lo // 16 : hi // 16]))
+            picked[lo] = place([P, hi - lo], U8, f"picked{lo}")
+            on_vector(out=picked[lo][:], in_=table_scales[:].indirect(offsets[:, lo // 16 : hi // 16]))
 
         def move_scale_rows(base, lo, hi):
-            for q in (0, 2, 1, 3):
+            for r in range(4):
                 nc.sync.dma_start(
-                    out=x_bytes[32 * q : 32 * q + 4, lo:hi].bitcast(I32),
-                    in_=picked[base][ROWS_AT + 4 * q : ROWS_AT + 4 * q + 4, lo - base : hi - base].bitcast(I32),
+                    out=x_bytes[r:P:32, lo:hi].bitcast(I32),
+                    in_=picked[base][ROWS_AT + r : P : 4, lo - base : hi - base].bitcast(I32),
                 )
 
         def load_weight(d):
-            raw[d] = place([P, PACK, H], F32, f"raw{d}", raw_at(d))
+            raw[d] = place([P, PACK, H], F32, f"raw{d}", raw_at[d])
             nc.sync.dma_start(out=raw[d][:], in_=weights[d].rearrange("(p j) c -> p j c", j=PACK))
 
         def round_part(copy, d, half, m0, m1, walk="p m j t"):
             if (d, half) not in rounded:
-                rounded[d, half] = place([P, 2 * H], BF16, f"rounded{d}_{half}", rounded_at(d, half))
+                rounded[d, half] = place([P, 2 * H], BF16, f"rounded{d}_{half}", rounded_at[d, half])
             src = raw[d][:].rearrange("p j (m t) -> p m j t", t=PACK)[:, m0:m1, :, 2 * half : 2 * half + 2]
             dst = rounded[d, half][:].rearrange("p (t m j) -> p m j t", m=P, j=PACK)[:, m0:m1]
             copy(out=dst.rearrange(f"p m j t -> {walk}"), in_=src.rearrange(f"p m j t -> {walk}"))
 
-        def quantize_weight(d, half, at=None):
-            codes = place([P, 2 * P], U32, f"w_codes{d}_{half}", at)
+        def quantize_weight(d, half, kib=None):
+            codes = place([P, 2 * P], U32, f"w_codes{d}_{half}", kib)
             cols = slice(2 * half * P, 2 * (half + 1) * P)
             nc.vector.quantize_mx(out=codes[:].bitcast(FP8X4), scales=w_scales[d][:, cols], in_=rounded[d, half][:])
             for t in range(2):
                 w_codes[d, 2 * half + t] = codes[:, t * P : (t + 1) * P]
 
-        def gather_words(c0, c1, at):
-            codes = place([P, (c1 - c0) * CHUNK], U32, f"x_codes{c0}", at)
-            entries = offsets[:, c0 * CHUNK // 16 : c1 * CHUNK // 16]
-            nc.vector.tensor_copy(out=codes[:], in_=table_words[:].indirect(entries))
+        def gather_words(c0, c1, kib):
+            codes = place([P, (c1 - c0) * CHUNK], U32, f"x_codes{c0}", kib)
+            on_vector(out=codes[:], in_=table_words[:].indirect(offsets[:, c0 * CHUNK // 16 : c1 * CHUNK // 16]))
             for c in range(c0, c1):
                 x_tiles[divmod(c, CHUNKS)] = (codes, (c - c0) * CHUNK)
-                x_codes[divmod(c, CHUNKS)] = codes[:, (c - c0) * CHUNK : (c - c0 + 1) * CHUNK]
 
-        def bank_tile(shape, b):
-            return psum.tile(shape, F32, name=f"bank{b}", tag=f"bank{b}", bufs=1)
-
-        def product(d, c, b, t_first=0):
-            bank = bank_tile([P, PACK, CHUNK], b)
-            cols = slice(d * V + c * CHUNK, d * V + (c + 1) * CHUNK)
-            for step in range(PACK):
-                t = (t_first + step) % PACK
-                chans = slice(t * P, (t + 1) * P)
-                nc.tensor.matmul_mx(
-                    out=bank[:, t, :],
-                    lhsT=w_codes[d, t].bitcast(FP8X4),
-                    lhsT_scale=w_scales[d][:, chans],
-                    rhs=x_codes[d, c].bitcast(FP8X4),
-                    rhs_scale=x_bytes[:, cols],
-                    start=True,
-                    stop=True,
-                )
-            banks[d, c] = bank[:].rearrange("p t v -> p v t")
-
-        def pass_into(target, d, t, c0, c1):
-            cols = slice(d * V + c0 * CHUNK, d * V + c1 * CHUNK)
-            tile, base = x_tiles[d, c0]
+        def one_pass(target, d, t, c0, c1):
+            codes, base = x_tiles[d, c0]
             nc.tensor.matmul_mx(
                 out=target,
                 lhsT=w_codes[d, t].bitcast(FP8X4),
                 lhsT_scale=w_scales[d][:, t * P : (t + 1) * P],
-                rhs=tile[:, base : base + (c1 - c0) * CHUNK].bitcast(FP8X4),
-                rhs_scale=x_bytes[:, cols],
+                rhs=codes[:, base : base + (c1 - c0) * CHUNK].bitcast(FP8X4),
+                rhs_scale=x_bytes[:, d * V + c0 * CHUNK : d * V + c1 * CHUNK],
                 start=True,
                 stop=True,
             )
 
-        first_low = [keep.tile([P, 2 * CHUNK, 2], F32, name=f"first_low{h}", align_bytes=64) for h in range(2)]
-        pair_low = place([P, 2, 2 * CHUNK, 2], F32, "pair_low", spare + 6 * KIB)
+        def factor(d, c, b):
+            bank = bank_tile([P, PACK, CHUNK], b)
+            for t in range(PACK):
+                one_pass(bank[:, t, :], d, t, c, c + 1)
+            banks[d, c] = bank[:].rearrange("p t v -> p v t")
 
-        def first_factor_low(h, c, b):
+        first_low = [place([P, 2 * CHUNK, 2], F32, f"first_low{h}") for h in range(2)]
+        pair_low = place([P, 2, 2 * CHUNK, 2], F32, "pair_low", pair_low_at)
+
+        def first_factor_low(h, c, b, copy):
             bank = bank_tile([P, 2, CHUNK], b)
             for u in range(2):
-                pass_into(bank[:, u, :], 0, 2 * h + u, c, c + 1)
-            banks[0, h, c] = bank[:].rearrange("p u v -> p v u")
+                one_pass(bank[:, u, :], 0, 2 * h + u, c, c + 1)
+            copy(out=first_low[h][:, c * CHUNK : (c + 1) * CHUNK, :], in_=bank[:].rearrange("p u v -> p v u"))
 
-        def empty_low(h, c, copy):
-            copy(out=first_low[h][:, c * CHUNK : (c + 1) * CHUNK, :], in_=banks[0, h, c])
-
-        def second_factor_low(h, b):
+        def first_product_low(h, b):
             bank = bank_tile([P, 2, 2 * CHUNK], b)
             for u in range(2):
-                pass_into(bank[:, u, :], 1, 2 * h + u, 0, 2)
-            nc.vector.tensor_tensor(out=pair_low[:, h], in0=bank[:].rearrange("p u v -> p v u"), in1=first_low[h][:], op=MULT)
+                one_pass(bank[:, u, :], 1, 2 * h + u, 0, 2)
+            nc.vector.tensor_tensor(
+                out=pair_low[:, h], in0=bank[:].rearrange("p u v -> p v u"), in1=first_low[h][:], op=MULT
+            )
 
-        def third_factor_low(c):
+        def z_part(c, v0, v1):
+            if c not in z:
+                z[c] = place([P, CHUNK * PACK], BF16, f"z{c}", z_at[c])
+            return z[c][:, v0 * PACK : v1 * PACK].rearrange("p (v t) -> p v t", t=PACK)
+
+        def last_product_low(c):
             nc.vector.tensor_tensor(
                 out=z_part(c, 0, CHUNK).rearrange("p v (h u) -> p v h u", u=2),
                 in0=banks[2, c].rearrange("p v (h u) -> p v h u", u=2),
@@ -175,77 +150,51 @@ def tile_picked_trilin_none_p_kernel(
                 op=MULT,
             )
 
-        def first_factor(c, at, copy=nc.scalar.copy):
-            first[c] = place([P, CHUNK, PACK], F32, f"first{c}", at)
-            copy(out=first[c][:], in_=banks[0, c])
+        def empty_first(c, kib=None):
+            first[c] = place([P, CHUNK, PACK], F32, f"first{c}", kib)
+            on_scalar(out=first[c][:], in_=banks[0, c])
 
-        def second_factor_gpsimd(c, at, pair_at):
-            second = place([P, CHUNK, PACK], F32, "second", at)
-            pair[c] = place([P, CHUNK, PACK], F32, f"pair{c}", pair_at)
-            nc.scalar.copy(out=second[:], in_=banks[1, c])
-            nc.gpsimd.tensor_tensor(out=pair[c][:], in0=second[:], in1=first[c][:], op=MULT)
-
-        def second_factor(c, at):
-            pair[c] = place([P, CHUNK, PACK], F32, f"pair{c}", at)
+        def first_product(c, kib):
+            pair[c] = place([P, CHUNK, PACK], F32, f"pair{c}", kib)
             nc.vector.tensor_tensor(out=pair[c][:], in0=banks[1, c], in1=first[c][:], op=MULT)
 
-        def z_part(c, v0, v1):
-            if c not in z:
-                z[c] = place([P, CHUNK * PACK], BF16, f"z{c}", spare + (0, 1, 2, 1)[c] * KIB)
-            return z[c][:, v0 * PACK : v1 * PACK].rearrange("p (v t) -> p v t", t=PACK)
+        def first_product_gpsimd(c, kib):
+            second = place([P, CHUNK, PACK], F32, "second")
+            pair[c] = place([P, CHUNK, PACK], F32, f"pair{c}", kib)
+            on_scalar(out=second[:], in_=banks[1, c])
+            nc.gpsimd.tensor_tensor(out=pair[c][:], in0=second[:], in1=first[c][:], op=MULT)
 
-        def third_factor(c, v1=CHUNK, v0=0):
+        def last_product(c, v0, v1):
             nc.vector.tensor_tensor(out=z_part(c, v0, v1), in0=banks[2, c][:, v0:v1], in1=pair[c][:, v0:v1], op=MULT)
 
-        def third_factor_gpsimd(c, v0, at=None):
-            third = place([P, CHUNK - v0, PACK], F32, f"third{c}", at)
-            nc.scalar.copy(out=third[:], in_=banks[2, c][:, v0:])
+        def last_product_gpsimd(c, v0):
+            third = place([P, CHUNK - v0, PACK], F32, "third")
+            on_scalar(out=third[:], in_=banks[2, c][:, v0:])
             nc.gpsimd.tensor_tensor(out=z_part(c, v0, CHUNK), in0=third[:], in1=pair[c][:, v0:], op=MULT)
 
-        def quantize_z(c0, c1, at=None):
-            z_codes[c0] = place([P, (c1 - c0) * CHUNK], U32, f"z_codes{c0}", at)
+        def quantize_z(c, kib=None):
+            z_codes[c] = place([P, CHUNK], U32, f"z_codes{c}", kib)
             nc.vector.quantize_mx(
-                out=z_codes[c0][:].bitcast(FP8X4),
-                scales=z_scales[:, c0 * CHUNK : c1 * CHUNK],
-                in_=z[c0][:],
+                out=z_codes[c][:].bitcast(FP8X4), scales=z_scales[:, c * CHUNK : (c + 1) * CHUNK], in_=z[c][:]
             )
 
-        def last_product(target, h, c0, c1):
+        def output_pass(target, h, c):
             nc.tensor.matmul_mx(
                 out=target,
                 lhsT=last_words[:, 2 * P * h : 2 * P * (h + 1)].bitcast(FP4X4),
                 lhsT_scale=last_scales[:, P * h : P * (h + 1)],
-                rhs=z_codes[c0][:].bitcast(FP8X4),
-                rhs_scale=z_scales[:, c0 * CHUNK : c1 * CHUNK],
+                rhs=z_codes[c][:].bitcast(FP8X4),
+                rhs_scale=z_scales[:, c * CHUNK : (c + 1) * CHUNK],
                 start=True,
                 stop=True,
             )
 
-        def finish(c0, c1, b, stores, copy=nc.scalar.copy, at=None):
-            width = (c1 - c0) * CHUNK
-            res = bank_tile([P, HALVES, width], b)
-            staged = place([P, HALVES, width], F32, f"staged{c0}", at)
-            for h in range(HALVES):
-                last_product(res[:, h, :], h, c0, c1)
-            for h0, h1 in stores:
-                copy(out=staged[:, h0:h1], in_=res[:, h0:h1])
-                nc.sync.dma_start(out=out_view[:, h0:h1, c0 * CHUNK : c1 * CHUNK], in_=staged[:, h0:h1])
-
-        def finish_last(c, b0, b1, at=None):
-            for h, copy, queue, b in ((0, nc.scalar.copy, nc.scalar, b0), (1, nc.vector.tensor_copy, nc.sync, b1)):
-                res = bank_tile([P, CHUNK], b)
-                staged = place([P, CHUNK], F32, f"staged{c}_{h}", at if h else None)
-                last_product(res[:], h, c, c + 1)
-                copy(out=staged[:], in_=res[:])
-                queue.dma_start(out=out_view[:, h, c * CHUNK : (c + 1) * CHUNK], in_=staged[:])
-
-        on_scalar, on_vector, on_gpsimd = nc.scalar.copy, nc.vector.tensor_copy, nc.gpsimd.tensor_copy
-
-        def round_weight(d, share):
-            if share < P:
-                round_part(on_scalar, d, 0, 0, P - share, "p m j t")
-            round_part(on_gpsimd, d, 0, P - share, P, "p m j t")
-            round_part(on_scalar, d, 1, 0, P)
+        def finish(c, h, b, copy, queue, kib=None):
+            res = bank_tile([P, CHUNK], b)
+            staged = place([P, CHUNK], F32, f"staged{c}_{h}", kib)
+            output_pass(res[:], h, c)
+            copy(out=staged[:], in_=res[:])
+            queue.dma_start(out=out_view[:, h, c * CHUNK : (c + 1) * CHUNK], in_=staged[:])
 
         nc.sync.dma_start(offsets[:], offs)
         nc.scalar.dma_start(out=table_scales[ROWS_AT:P, :].bitcast(I32), in_=x_scales[0].bitcast(I32))
@@ -258,59 +207,71 @@ def tile_picked_trilin_none_p_kernel(
         gather_bytes(2 * CHUNK, S)
         move_scale_rows(0, 0, 2 * CHUNK)
         load_weight(1)
-        move_scale_rows(2 * CHUNK, 2 * CHUNK, 2 * V - CHUNK)
+        move_scale_rows(2 * CHUNK, 2 * CHUNK, 6 * CHUNK)
         load_weight(2)
-        move_scale_rows(2 * CHUNK, 2 * V - CHUNK, S)
+        move_scale_rows(2 * CHUNK, 6 * CHUNK, S)
         nc.sync.dma_start(out=last_words[:].bitcast(I32), in_=w4_words[0].bitcast(I32))
-        load_scale_rows(last_scales, w4_scales)
+        for q in range(4):
+            nc.sync.dma_start(
+                out=last_scales[32 * q : 32 * q + 32, :].bitcast(I32),
+                in_=w4_scales[0, 4 * q : 4 * q + 4, :].bitcast(I32).partition_broadcast(8),
+            )
 
-        round_weight(0, 128)
+        round_part(on_gpsimd, 0, 0, 0, P, WALK)
+        round_part(on_scalar, 0, 1, 0, P)
         quantize_weight(0, 0)
         quantize_weight(0, 1)
-        gather_words(0, 1, raw_at(0))
-        gather_words(1, 2, raw_at(0) + KIB)
-        gather_words(2, 4, raw_at(0) + 2 * KIB)
-        gather_words(4, 11, raw_at(0) + 3 * KIB)
-        first_factor_low(0, 0, 0)
-        empty_low(0, 0, on_scalar)
-        first_factor_low(1, 0, 1)
-        empty_low(1, 0, on_scalar)
-        first_factor_low(0, 1, 6)
-        empty_low(0, 1, on_scalar)
-        first_factor_low(1, 1, 7)
-        empty_low(1, 1, on_vector)
-        round_weight(1, 128)
-        product(0, 3, 2)
-        product(0, 2, 3)
+        gather_words(0, 1, raw_at[0])
+        gather_words(1, 2, raw_at[0] + 1)
+        gather_words(2, 4, raw_at[0] + 2)
+        gather_words(4, 11, raw_at[0] + 3)
+        first_factor_low(0, 0, 0, on_scalar)
+        first_factor_low(1, 0, 1, on_scalar)
+        first_factor_low(0, 1, 6, on_scalar)
+        first_factor_low(1, 1, 7, on_vector)
+
+        round_part(on_gpsimd, 1, 0, 0, P, WALK)
+        round_part(on_scalar, 1, 1, 0, P)
+        factor(0, 3, 2)
+        factor(0, 2, 3)
         quantize_weight(1, 0)
-        quantize_weight(1, 1, raw_at(1))
-        gather_words(11, 12, rounded_at(1, 0))
-        first_factor(3, spare + 4 * KIB)
-        first_factor(2, None)
-        second_factor_low(0, 4)
-        second_factor_low(1, 5)
-        product(1, 2, 7)
-        round_weight(2, 112)
-        product(1, 3, 6)
+        quantize_weight(1, 1, raw_at[1])
+        gather_words(11, 12, rounded_at[1, 0])
+        empty_first(3, first3_at)
+        empty_first(2)
+        first_product_low(0, 4)
+        first_product_low(1, 5)
+
+        round_part(on_scalar, 2, 0, 0, W3_SCALAR, WALK)
+        round_part(on_gpsimd, 2, 0, W3_SCALAR, P, WALK)
+        round_part(on_scalar, 2, 1, 0, P)
+        factor(1, 3, 6)
+        factor(1, 2, 7)
         quantize_weight(2, 0)
-        quantize_weight(2, 1, raw_at(2))
-        second_factor(2, rounded_at(2, 0))
-        second_factor_gpsimd(3, None, rounded_at(2, 1))
-        product(2, 0, 0)
-        third_factor_low(0)
-        product(2, 1, 1)
-        third_factor_low(1)
-        product(2, 2, 3)
-        product(2, 3, 2)
-        third_factor(2, CHUNK // 2)
-        quantize_z(0, 1)
-        quantize_z(1, 2)
-        finish(0, 1, 4, ((0, 2),))
-        finish(1, 2, 5, ((0, 2),))
-        third_factor_gpsimd(3, SPLIT)
-        third_factor(2, CHUNK, CHUNK // 2)
-        third_factor(3, SPLIT)
-        quantize_z(2, 3, spare + 4 * KIB)
-        quantize_z(3, 4)
-        finish_last(2, 6, 1, spare + KIB)
-        finish_last(3, 0, 7)
+        quantize_weight(2, 1, raw_at[2])
+        first_product(2, rounded_at[2, 0] - 1)
+        first_product_gpsimd(3, rounded_at[2, 0] + 1)
+
+        factor(2, 0, 0)
+        last_product_low(0)
+        factor(2, 1, 1)
+        last_product_low(1)
+        factor(2, 2, 3)
+        factor(2, 3, 2)
+        one_pass(bank_tile([P, V], 1)[:], 1, 0, 0, CHUNKS)
+        last_product(2, 0, COVER)
+        quantize_z(0)
+        quantize_z(1)
+        finish(0, 0, 4, on_scalar, nc.sync)
+        finish(0, 1, 6, on_scalar, nc.sync)
+        finish(1, 0, 5, on_scalar, nc.sync)
+        finish(1, 1, 7, on_scalar, nc.sync)
+        last_product_gpsimd(3, SPLIT)
+        last_product(2, COVER, CHUNK)
+        last_product(3, 0, SPLIT)
+        quantize_z(2, first3_at)
+        quantize_z(3)
+        finish(2, 0, 0, on_scalar, nc.scalar)
+        finish(2, 1, 1, on_vector, nc.sync, z_at[3])
+        finish(3, 0, 4, on_scalar, nc.scalar)
+        finish(3, 1, 6, on_vector, nc.sync)

@@ -258,7 +258,6 @@ def tile_picked_trilin_none_p_kernel(
         last_product_low(1)
         factor(2, 2, 3)
         factor(2, 3, 2)
-        one_pass(bank_tile([P, V], 1)[:], 1, 0, 0, CHUNKS)
         last_product(2, 0, COVER)
         quantize_z(0)
         quantize_z(1)

from contextlib import ExitStack

import concourse.mybir as mybir

K, T, S, V, H, N = 512, 2048, 1536, 512, 512, 256
FLOPS = 2 * K * H * S + 2 * H * N * V

F32 = mybir.dt.float32
BF16 = mybir.dt.bfloat16
I32 = mybir.dt.int32
U32 = mybir.dt.uint32
U16 = mybir.dt.uint16
U8 = mybir.dt.uint8
FP8X4 = mybir.dt.float8_e4m3fn_x4
FP4X4 = mybir.dt.float4_e2m1fn_x4
MULT = mybir.AluOpType.mult

P = 128
PACK = 4
PIECES = 3
CHUNK = 128
CHUNKS = V // CHUNK
HALVES = N // P
KIB = 1024
ROWS_AT = 112
WALK = "p m j t"
W3_SCALAR = 16
COVER = 64
SPLIT = 92


def tile_picked_trilin_none_p_kernel(
    tc, x_words, x_scales, w1, w2, w3, w4_words, w4_scales, offs, out
):
    nc = tc.nc
    weights = (w1, w2, w3)
    on_scalar, on_vector, on_gpsimd = nc.scalar.copy, nc.vector.tensor_copy, nc.gpsimd.tensor_copy

    with ExitStack() as ctx:
        keep = ctx.enter_context(tc.tile_pool(name="keep", bufs=1))
        shared = ctx.enter_context(tc.tile_pool(name="shared", bufs=1))
        psum = ctx.enter_context(tc.psum_pool(name="psum", bufs=1))

        def place(shape, dtype, name, kib=None):
            if kib is None:
                return keep.tile(shape, dtype, name=name, align_bytes=64)
            return shared.tile(shape, dtype, name=name, align_bytes=64, offset=kib * KIB)

        def bank_tile(shape, b):
            return psum.tile(shape, F32, name=f"bank{b}", tag=f"bank{b}", bufs=1)

        raw_at = (0, 8, 16)
        rounded_at = {(0, 0): 24, (0, 1): 26, (1, 0): 28, (1, 1): 30, (2, 1): 32, (2, 0): 35}
        z_at = (38, 39, 40, 39)
        first3_at = 42
        pair_low_at = 44

        offsets = keep.tile([P, S // 16], U16, name="offsets")
        table_words = place([P, T], U32, "table_words")
        table_scales = place([P, T], U8, "table_scales")
        last_words = place([P, 2 * N], U8, "last_words")
        last_scales = place([P, N], U8, "last_scales")
        w_scales = [place([P, H], U8, f"w_scales{d}") for d in range(PIECES)]
        x_bytes = place([P, S], U8, "x_bytes")
        z_scales = place([P, V], U8, "z_scales")
        out_view = out.rearrange("(h m) v -> m h v", h=HALVES)

        picked, raw, rounded, w_codes, x_tiles, first, pair, banks, z, z_codes = ({} for i in range(10))

        def gather_bytes(lo, hi):
            picked[lo] = place([P, hi - lo], U8, f"picked{lo}")
            on_vector(out=picked[lo][:], in_=table_scales[:].indirect(offsets[:, lo // 16 : hi // 16]))

        def move_scale_rows(base, lo, hi):
            for r in range(4):
                nc.sync.dma_start(
                    out=x_bytes[r:P:32, lo:hi].bitcast(I32),
                    in_=picked[base][ROWS_AT + r : P : 4, lo - base : hi - base].bitcast(I32),
                )

        def load_weight(d):
            raw[d] = place([P, PACK, H], F32, f"raw{d}", raw_at[d])
            nc.sync.dma_start(out=raw[d][:], in_=weights[d].rearrange("(p j) c -> p j c", j=PACK))

        def round_part(copy, d, half, m0, m1, walk="p m j t"):
            if (d, half) not in rounded:
                rounded[d, half] = place([P, 2 * H], BF16, f"rounded{d}_{half}", rounded_at[d, half])
            src = raw[d][:].rearrange("p j (m t) -> p m j t", t=PACK)[:, m0:m1, :, 2 * half : 2 * half + 2]
            dst = rounded[d, half][:].rearrange("p (t m j) -> p m j t", m=P, j=PACK)[:, m0:m1]
            copy(out=dst.rearrange(f"p m j t -> {walk}"), in_=src.rearrange(f"p m j t -> {walk}"))

        def quantize_weight(d, half, kib=None):
            codes = place([P, 2 * P], U32, f"w_codes{d}_{half}", kib)
            cols = slice(2 * half * P, 2 * (half + 1) * P)
            nc.vector.quantize_mx(out=codes[:].bitcast(FP8X4), scales=w_scales[d][:, cols], in_=rounded[d, half][:])
            for t in range(2):
                w_codes[d, 2 * half + t] = codes[:, t * P : (t + 1) * P]

        def gather_words(c0, c1, kib):
            codes = place([P, (c1 - c0) * CHUNK], U32, f"x_codes{c0}", kib)
            on_vector(out=codes[:], in_=table_words[:].indirect(offsets[:, c0 * CHUNK // 16 : c1 * CHUNK // 16]))
            for c in range(c0, c1):
                x_tiles[divmod(c, CHUNKS)] = (codes, (c - c0) * CHUNK)

        def one_pass(target, d, t, c0, c1):
            codes, base = x_tiles[d, c0]
            nc.tensor.matmul_mx(
                out=target,
                lhsT=w_codes[d, t].bitcast(FP8X4),
                lhsT_scale=w_scales[d][:, t * P : (t + 1) * P],
                rhs=codes[:, base : base + (c1 - c0) * CHUNK].bitcast(FP8X4),
                rhs_scale=x_bytes[:, d * V + c0 * CHUNK : d * V + c1 * CHUNK],
                start=True,
                stop=True,
            )

        def factor(d, c, b):
            bank = bank_tile([P, PACK, CHUNK], b)
            for t in range(PACK):
                one_pass(bank[:, t, :], d, t, c, c + 1)
            banks[d, c] = bank[:].rearrange("p t v -> p v t")

        first_low = [place([P, 2 * CHUNK, 2], F32, f"first_low{h}") for h in range(2)]
        pair_low = place([P, 2, 2 * CHUNK, 2], F32, "pair_low", pair_low_at)

        def first_factor_low(h, c, b, copy):
            bank = bank_tile([P, 2, CHUNK], b)
            for u in range(2):
                one_pass(bank[:, u, :], 0, 2 * h + u, c, c + 1)
            copy(out=first_low[h][:, c * CHUNK : (c + 1) * CHUNK, :], in_=bank[:].rearrange("p u v -> p v u"))

        def first_product_low(h, b):
            bank = bank_tile([P, 2, 2 * CHUNK], b)
            for u in range(2):
                one_pass(bank[:, u, :], 1, 2 * h + u, 0, 2)
            nc.vector.tensor_tensor(
                out=pair_low[:, h], in0=bank[:].rearrange("p u v -> p v u"), in1=first_low[h][:], op=MULT
            )

        def z_part(c, v0, v1):
            if c not in z:
                z[c] = place([P, CHUNK * PACK], BF16, f"z{c}", z_at[c])
            return z[c][:, v0 * PACK : v1 * PACK].rearrange("p (v t) -> p v t", t=PACK)

        def last_product_low(c):
            nc.vector.tensor_tensor(
                out=z_part(c, 0, CHUNK).rearrange("p v (h u) -> p v h u", u=2),
                in0=banks[2, c].rearrange("p v (h u) -> p v h u", u=2),
                in1=pair_low[:, :, c * CHUNK : (c + 1) * CHUNK, :].rearrange("p h v u -> p v h u"),
                op=MULT,
            )

        def empty_first(c, kib=None):
            first[c] = place([P, CHUNK, PACK], F32, f"first{c}", kib)
            on_scalar(out=first[c][:], in_=banks[0, c])

        def first_product(c, kib):
            pair[c] = place([P, CHUNK, PACK], F32, f"pair{c}", kib)
            nc.vector.tensor_tensor(out=pair[c][:], in0=banks[1, c], in1=first[c][:], op=MULT)

        def first_product_gpsimd(c, kib):
            second = place([P, CHUNK, PACK], F32, "second")
            pair[c] = place([P, CHUNK, PACK], F32, f"pair{c}", kib)
            on_scalar(out=second[:], in_=banks[1, c])
            nc.gpsimd.tensor_tensor(out=pair[c][:], in0=second[:], in1=first[c][:], op=MULT)

        def last_product(c, v0, v1):
            nc.vector.tensor_tensor(out=z_part(c, v0, v1), in0=banks[2, c][:, v0:v1], in1=pair[c][:, v0:v1], op=MULT)

        def last_product_gpsimd(c, v0):
            third = place([P, CHUNK - v0, PACK], F32, "third")
            on_scalar(out=third[:], in_=banks[2, c][:, v0:])
            nc.gpsimd.tensor_tensor(out=z_part(c, v0, CHUNK), in0=third[:], in1=pair[c][:, v0:], op=MULT)

        def quantize_z(c, kib=None):
            z_codes[c] = place([P, CHUNK], U32, f"z_codes{c}", kib)
            nc.vector.quantize_mx(
                out=z_codes[c][:].bitcast(FP8X4), scales=z_scales[:, c * CHUNK : (c + 1) * CHUNK], in_=z[c][:]
            )

        def output_pass(target, h, c):
            nc.tensor.matmul_mx(
                out=target,
                lhsT=last_words[:, 2 * P * h : 2 * P * (h + 1)].bitcast(FP4X4),
                lhsT_scale=last_scales[:, P * h : P * (h + 1)],
                rhs=z_codes[c][:].bitcast(FP8X4),
                rhs_scale=z_scales[:, c * CHUNK : (c + 1) * CHUNK],
                start=True,
                stop=True,
            )

        def finish(c, h, b, copy, queue, kib=None):
            res = bank_tile([P, CHUNK], b)
            staged = place([P, CHUNK], F32, f"staged{c}_{h}", kib)
            output_pass(res[:], h, c)
            copy(out=staged[:], in_=res[:])
            queue.dma_start(out=out_view[:, h, c * CHUNK : (c + 1) * CHUNK], in_=staged[:])

        nc.sync.dma_start(offsets[:], offs)
        nc.scalar.dma_start(out=table_scales[ROWS_AT:P, :].bitcast(I32), in_=x_scales[0].bitcast(I32))
        nc.gpsimd.memset(table_scales[0:96, :].bitcast(I32), 0)
        nc.gpsimd.memset(table_scales[96:ROWS_AT, :].bitcast(I32), 0)
        nc.gpsimd.memset(x_bytes[:].bitcast(I32), 0)
        load_weight(0)
        nc.sync.dma_start(out=table_words[:].bitcast(I32), in_=x_words[0].rearrange("p c r -> p (c r)").bitcast(I32))
        gather_bytes(0, 2 * CHUNK)
        gather_bytes(2 * CHUNK, S)
        move_scale_rows(0, 0, 2 * CHUNK)
        load_weight(1)
        move_scale_rows(2 * CHUNK, 2 * CHUNK, 6 * CHUNK)
        load_weight(2)
        move_scale_rows(2 * CHUNK, 6 * CHUNK, S)
        nc.sync.dma_start(out=last_words[:].bitcast(I32), in_=w4_words[0].bitcast(I32))
        for q in range(4):
            nc.sync.dma_start(
                out=last_scales[32 * q : 32 * q + 32, :].bitcast(I32),
                in_=w4_scales[0, 4 * q : 4 * q + 4, :].bitcast(I32).partition_broadcast(8),
            )

        round_part(on_gpsimd, 0, 0, 0, P, WALK)
        round_part(on_scalar, 0, 1, 0, P)
        quantize_weight(0, 0)
        quantize_weight(0, 1)
        gather_words(0, 1, raw_at[0])
        gather_words(1, 2, raw_at[0] + 1)
        gather_words(2, 4, raw_at[0] + 2)
        gather_words(4, 11, raw_at[0] + 3)
        first_factor_low(0, 0, 0, on_scalar)
        first_factor_low(1, 0, 1, on_scalar)
        first_factor_low(0, 1, 6, on_scalar)
        first_factor_low(1, 1, 7, on_vector)

        round_part(on_gpsimd, 1, 0, 0, P, WALK)
        round_part(on_scalar, 1, 1, 0, P)
        factor(0, 3, 2)
        factor(0, 2, 3)
        quantize_weight(1, 0)
        quantize_weight(1, 1, raw_at[1])
        gather_words(11, 12, rounded_at[1, 0])
        empty_first(3, first3_at)
        empty_first(2)
        first_product_low(0, 4)
        first_product_low(1, 5)

        round_part(on_scalar, 2, 0, 0, W3_SCALAR, WALK)
        round_part(on_gpsimd, 2, 0, W3_SCALAR, P, WALK)
        round_part(on_scalar, 2, 1, 0, P)
        factor(1, 3, 6)
        factor(1, 2, 7)
        quantize_weight(2, 0)
        quantize_weight(2, 1, raw_at[2])
        first_product(2, rounded_at[2, 0] - 1)
        first_product_gpsimd(3, rounded_at[2, 0] + 1)

        factor(2, 0, 0)
        last_product_low(0)
        factor(2, 1, 1)
        last_product_low(1)
        factor(2, 2, 3)
        factor(2, 3, 2)
        last_product(2, 0, COVER)
        quantize_z(0)
        quantize_z(1)
        finish(0, 0, 4, on_scalar, nc.sync)
        finish(0, 1, 6, on_scalar, nc.sync)
        finish(1, 0, 5, on_scalar, nc.sync)
        finish(1, 1, 7, on_scalar, nc.sync)
        last_product_gpsimd(3, SPLIT)
        last_product(2, COVER, CHUNK)
        last_product(3, 0, SPLIT)
        quantize_z(2, first3_at)
        quantize_z(3)
        finish(2, 0, 0, on_scalar, nc.scalar)
        finish(2, 1, 1, on_vector, nc.sync, z_at[3])
        finish(3, 0, 4, on_scalar, nc.scalar)
        finish(3, 1, 6, on_vector, nc.sync)
